import numpy as np, ml_dtypes
CORES = [9,25,41,57]
N = 4
BF = ml_dtypes.bfloat16
def gentries(a):
    return np.ascontiguousarray(a.reshape(8, 16, -1).transpose(0, 2, 1)).reshape(8, -1)
def gtable(e):
    e = np.asarray(e); return np.ascontiguousarray(e.reshape(8, -1, 16).transpose(0, 2, 1)).reshape(128, -1).astype(np.int32)
M, K, D, CAP, A, RO = 960, 1792, 16, 128, 2, 4
W, S, L = N * M, K // D, K // N
PS, ST = 0.0078125, 0.03125
LIM = np.float32(4.0)
HOT = np.array([4.0, 2.0, 1.3359375, 1.0, 0.80078125, 0.66796875, 0.57421875])
COLD = np.array([3.984375, 1.9921875, 1.328125, 0.99609375, 0.796875, 0.6640625, 0.5703125])
def pay(rng, a):
    v = 1.0 + 0.2 * rng.standard_normal((N, 128, W), dtype=np.float32) + 0.1 * rng.integers(-1, 2, (N, 128, 1)) + a * (2.0 * rng.random((N, 1, W)) - 1.0)
    return np.clip(v, 0.5, 1.5).astype(BF)
def parts(rng):
    e = pay(rng, 0.0); w = np.exp2(4.0 * rng.random((N, 8, W)) - 2.0)
    share = rng.choice(np.array([0.05, 0.2, 0.5, 0.9]), (N, 8, N, 1))
    l = np.where(rng.random((N, 8, N, M)) < share, rng.integers(1, 8, (N, 8, N, M)), 0).reshape(N, 8, W)
    b = np.ascontiguousarray(np.argsort(rng.random((N, 8, RO, W)), axis=-1)[..., :2 * K]).reshape(N, 8, RO, 2, K)
    t = np.clip(0.625 * rng.standard_normal((N, 16, RO * S)), -1.0, 1.0).astype(BF)
    return e, w, l, b, t
def pack(e, w, l, b, t):
    return {"e0": e, "wt": np.asarray(w).astype(BF), "lag": np.asarray(l).astype(np.int32), "bt": np.stack([gtable(a.reshape(8, -1)) for a in b]), "tg": t}
def close(rng, n):
    v = (np.exp2(np.arange(-9.0, -5.0))[:, None] * np.arange(128, 256)).reshape(-1)
    x = (v[:, None] * (A * (RO - 1) + np.arange(8))).reshape(-1); o = np.argsort(x, kind="stable"); k = x[o]
    i = rng.choice(np.flatnonzero((k[1:] > k[:-1]) & (k[1:].astype(np.float16) == k[:-1].astype(np.float16))), n)
    lo = o[i]; hi = o[i + 1]
    return v[lo // 8], lo % 8, v[hi // 8], hi % 8
def herd(rng, w, l, b, g, q, lo):
    x = np.stack([np.concatenate([np.array([M - 1, 0]), 1 + rng.permutation(M - 2)]) + h * M for h in range(N)])
    m = x[:, :L]; a = x[:, L:2 * L]; o = x[:, 2 * L:]
    w[:, g] = 0.25; w[:, g][:, m] = 4.0
    l[:, g] = 0; l[:, g][:, m] = 7
    near = np.zeros(L // 2, bool); kind = np.arange(16) % 6
    if q >= 0:
        X = min(CAP, L - CAP); l[q, g][m[:, 2:X]] = rng.choice(np.array([lo, 7]), (N, X - 2))
        if lo > 0:
            w[q, g][m[:, 2:10]] = 0.75; l[q, g][m[:, 2:10]] = 7
            w[q, g][o[:, :8]] = (6.5 + (N - 1 + A) * (RO - 1)) * 0.75 * 0.142857142857; l[q, g][o[:, :8]] = 7
    else:
        y = CAP // 2 + rng.permutation(L // 2 - CAP // 2)[:(L - CAP) // 4]; near[y] = True
        wl, al, wh, ah = close(rng, len(y))
        w[:, g][:, m[:, 2 * y]] = wl; l[:, g][:, m[:, 2 * y]] = al; w[:, g][:, m[:, 2 * y + 1]] = wh; l[:, g][:, m[:, 2 * y + 1]] = ah
        w[:, g][:, o[:, :16]] = np.array([4.0, 4.0, 2.0, 2.0, 4.0, 4.0])[kind]
        l[:, g][:, o[:, :16]] = np.array([A, A, 2 * A - 1, 2 * A + 1, A + 1, A - 1])[kind]
    k = int(rng.integers(0, N)); k2 = (k + 1) % N
    j = np.arange(K); h = j % N; i = j // N
    for r in range(N):
        b[r, g, :, 0] = m[h, L - 1 - i if r == q else i]; b[r, g, :, 1] = a[h, i]
        if q == -2:
            f = m.copy(); s = a.copy(); f[k] = a[k2]; s[k2] = m[k]
            b[r, g, RO - 2, 0] = f[h, i]; b[r, g, RO - 2, 1] = s[h, i]
        sp = np.arange(0); first = np.zeros(0, bool)
        if q < 0:
            z = 1 + rng.permutation(CAP // 2 - 1)[:8]; sp = rng.permutation(np.concatenate([2 * z, 2 * z + 1])); first = kind % 2 == 1
        elif r == q and lo > 0:
            sp = np.arange(2, 10); first = rng.random(8) < 0.5
        n = len(sp); c = n // 2; p = m[:, sp]; v = o[:, :n]
        z = np.concatenate([rng.permutation(np.setdiff1d(np.arange(1, L // 2), sp // 2)), np.array([0])])
        f = np.concatenate([np.where(first, v, p), a[:, c:L // 2], m[:, 2 * z]], axis=1)
        s = np.concatenate([np.where(first, p, v), a[:, L // 2 + c:], m[:, 2 * z + 1]], axis=1)
        t = rng.random((N, L)) < 0.5; t[:, :n] = True; t[:, L // 2 + c:] |= near[z]
        if q == -1:
            f[k2] = m[k2]; s[k2] = m[k]; f[k] = a[k2]; s[k] = a[k]; t[k2] = True
        b[r, g, RO - 1, 0] = np.where(t, f, s)[h, i]; b[r, g, RO - 1, 1] = np.where(t, s, f)[h, i]
def leave(rng, w, l, b, g, q, v):
    x = np.stack([np.concatenate([np.array([M - 1, 0]), 1 + rng.permutation(M - 2)]) + h * M for h in range(N)])
    m = x[:, :L]; a = x[:, L:2 * L]; j = np.arange(K); h = j % N; i = j // N
    w[:, g] = 0.25; w[:, g][:, m] = 4.0
    l[:, g] = 0; l[:, g][:, m] = 7
    w[q, g][m[:, CAP:CAP + 16]] = v
    b[:, g, :RO - 1, 0] = m[h, i]; b[:, g, :RO - 1, 1] = a[h, i]
    b[q, g, RO - 2, 0] = m[h, L - 1 - i]
    z = rng.permutation(np.setdiff1d(np.arange(M), np.concatenate([np.arange(16), CAP + np.arange(16)])))[:2 * L - 32]
    f = np.concatenate([m[:, :16], x[:, z[:L - 16]]], axis=1); s = np.concatenate([m[:, CAP:CAP + 16], x[:, z[L - 16:]]], axis=1)
    t = rng.random((N, L)) < 0.5
    b[q, g, RO - 1, 0] = np.where(t, f, s)[h, i]; b[q, g, RO - 1, 1] = np.where(t, s, f)[h, i]
def full(rng, w, l, b, r, g, h):
    Q = K // 8; T = K - M - Q; k = (h + 1) % N; x = np.arange(W).reshape(N, M)
    y = rng.permutation(x[k]); z = rng.permutation(x[[v for v in range(N) if v != h and v != k]].reshape(-1))
    n = np.concatenate([rng.permutation(np.concatenate([x[h], z[:T]])), y[:Q]]); o = rng.permutation(np.concatenate([z[T:], y[Q:]]))[:K]
    v = rng.integers(1, 8, K); w[r, g][n] = HOT[v - 1]; l[r, g][n] = v
    v = rng.integers(0, 8, K); w[r, g][o] = np.where(v == 0, 4.0, COLD[v - 1]); l[r, g][o] = v
    t = rng.random(K) < 0.5
    b[r, g, 0, 0] = np.where(t, n, o); b[r, g, 0, 1] = np.where(t, o, n)
def setup_inputs(rng):
    return pack(*parts(rng))
def setup_inputs_spread(rng):
    e, w, l, b, t = parts(rng)
    e = np.where(rng.random((N, 1, W)) > 0.0625, pay(rng, 0.5).astype(np.float32), np.float32(0.5)).astype(BF)
    return pack(e, w, l, b, t)
def setup_inputs_ends(rng):
    e, w, l, b, t = parts(rng)
    w = rng.choice(np.array([0.25, 4.0]), (N, 8, W)); l = rng.choice(np.array([0, 7]), (N, 8, W))
    o = 1 + np.argsort(rng.random((N, 8, RO, W - 2)), axis=-1)[..., :2 * K - 2]
    b[..., 0, :K - 1] = o[..., :K - 1]; b[..., 1, :K - 1] = o[..., K - 1:]
    b[..., 0, K - 1] = W - 1; b[..., 1, K - 1] = 0
    l[..., 0] = 7; l[..., W - 1] = 7; w[..., 0] = 4.0; w[..., W - 1] = 4.0
    for g in (1, 3, 5, 7): herd(rng, w, l, b, g, N - 1 if g == 7 else int(rng.integers(0, N)), 0)
    t = rng.choice(np.array([-1.0, 1.0]), t.shape).astype(BF)
    q = int(rng.integers(0, N)); v = rng.choice(np.array([0.5, 1.5]), (N, 8, W)); v[q] = 1.5
    k = (q + int(rng.integers(1, N))) % N; y = rng.choice(np.array([0.5, 1.5]), (N, 8, W)); y[k] = 0.5
    t[k, 14, S - 1] = 1.0; t[k, 14, 0] = 1.0
    z = w * l; na = b[:, :, 0, 0]; nb = b[:, :, 0, 1]
    n = np.where(np.take_along_axis(z, nb, 2) > np.take_along_axis(z, na, 2), nb, na)
    for g in range(8):
        v[n[q, g] // M, g, n[q, g]] = 1.5
        y[n[k, g] // M, g, n[k, g]] = 0.5
    e = e.reshape(N, 8, 16, W).copy(); e[:, :, 15] = v.astype(BF); e[:, :, 14] = y.astype(BF); e = e.reshape(N, 128, W)
    return pack(e, w, l, b, t)
def setup_inputs_corners(rng):
    e, w, l, b, t = parts(rng)
    for r in range(N):
        for g in range(8):
            if r > 0 and (r + g) % 3 == 0:
                full(rng, w, l, b, r, g, (r + g) % N); continue
            sl = rng.permutation(K).reshape(N, L)
            for h in range(N):
                n = int(rng.choice(np.array([0, 1, CAP - 1, CAP, CAP + 1, L])))
                if r == 0 and h == 1: n = (CAP, 0, 1, CAP - 1, CAP + 1, L, CAP, CAP + 1)[g]
                nm = (h * M + rng.permutation(M))[:2 * L].reshape(2, L)
                z = rng.integers(1, 8, (2, L)); hot = np.zeros((2, L), bool); k = rng.permutation(L)[:n]; y = rng.integers(0, 3, n)
                z[1] = np.where(rng.random(L) < 0.3, z[0], z[1])
                hot[0, k] = y != 1; hot[1, k] = y != 0
                none = (rng.random((2, L)) < 0.4) & ~hot
                w[r, g][nm] = np.where(none, rng.choice(np.array([0.25, 4.0]), (2, L)), np.where(hot, HOT[z - 1], COLD[z - 1]))
                l[r, g][nm] = np.where(none, 0, z)
                b[r, g, 0][:, sl[h]] = nm
    return pack(e, w, l, b, t)
def setup_inputs_crowd(rng):
    e, w, l, b, t = parts(rng)
    for g, q in ((0, -1), (2, int(rng.integers(0, N))), (4, -2), (6, int(rng.integers(0, N))), (7, N - 1)): herd(rng, w, l, b, g, q, 6)
    leave(rng, w, l, b, 1, int(rng.integers(0, N)), 4.0 * (N - 1 + 2 * A + np.where(np.arange(16) % 4 == 3, 0.5, -0.5)) / (7 + A * (RO - 1)))
    return pack(e, w, l, b, t)
def setup_inputs_calm(rng):
    e, w, l, b, t = parts(rng)
    w = rng.choice(np.concatenate([HOT, COLD, np.array([0.5, 0.498046875])]), (N, 8, W))
    act = (rng.permutation(N)[:, None] < (np.arange(8) % 4)[None, :])[:, :, None]
    w = np.where(act | (rng.random((N, 8, W)) < 0.25), w, 0.25)
    l = rng.integers(0, 4, (N, 8, W)) * (np.arange(8) % 2)[None, :, None]
    return pack(e, w, l, b, t)
def cand(bt):
    return np.stack([gentries(np.asarray(a)) for a in bt]).astype(np.int64).reshape(N, 8, RO, 2, K)
def check_ranges(d):
    bad = []
    for k, lo, hi in (("e0", 0.5, 1.5), ("wt", 0.25, 4), ("lag", 0, 7), ("bt", 0, W - 1), ("tg", -1, 1)):
        v = np.asarray(d[k]).astype(np.float64)
        if not (np.min(v) >= lo and np.max(v) <= hi): bad.append("range of " + k)
    b = np.sort(cand(d["bt"]).reshape(N, 8, RO, 2 * K), axis=-1)
    if np.any(b[..., 1:] == b[..., :-1]): bad.append("candidates of a round differ")
    return bad
def reference(e0, wt, lag, bt, tg):
    R = e0.astype(np.float64).reshape(N, 8, 16, W).copy(); P = np.zeros((N, 8, 16, W)); u = np.zeros((N, 8, W), np.int64)
    H = np.concatenate([R[h, :, :, h * M:(h + 1) * M] for h in range(N)], axis=2)
    c = np.zeros((8, W), np.int64); seen = -lag.astype(np.int64); b = cand(bt); w32 = wt.astype(np.float32); tgt = tg.astype(np.float64)
    for t in range(RO):
        sc = w32 * (c[None] - seen + A * u).astype(np.float32)
        took = []; asked = []
        for r in range(N):
            na = b[r, :, t, 0]; nb = b[r, :, t, 1]; sa = np.take_along_axis(sc[r], na, 1); sb = np.take_along_axis(sc[r], nb, 1)
            n = np.where(sb > sa, nb, na); due = np.where(sb > sa, sb, sa) >= LIM; home = n // M; ok = np.zeros((8, K), bool)
            for h in range(N):
                m = due & (home == h); ok = ok | (m & (np.add.accumulate(m.astype(np.int64), axis=1) <= CAP))
            took.append(n); asked.append([n[g][ok[g]] for g in range(8)])
        for r in range(N):
            for g in range(8):
                ix = asked[r][g]; H[g][:, ix] += P[r, g][:, ix]; c[g][ix] += 1
        for r in range(N):
            for g in range(8):
                ix = asked[r][g]; R[r, g][:, ix] = H[g][:, ix]; P[r, g][:, ix] = 0.0; u[r, g][ix] = 0; seen[r, g][ix] = c[g][ix]
        for r in range(N):
            n = took[r]; ix = np.broadcast_to(n[:, None, :], (8, 16, K)); x = np.take_along_axis(R[r], ix, 2); y = x.reshape(8, 16, D, S)
            p = np.add.reduce(y[:, :, :D // 2] * y[:, :, D // 2:], axis=(0, 2))
            e = np.tanh(tgt[r][:, t * S:(t + 1) * S] - PS * p)
            step = (ST * e[None, :, None, :] * np.concatenate([y[:, :, D // 2:], y[:, :, :D // 2]], axis=2)).reshape(8, 16, K)
            np.put_along_axis(R[r], ix, x + step, 2)
            if t < RO - 1:
                np.put_along_axis(P[r], ix, np.take_along_axis(P[r], ix, 2) + step, 2)
                np.put_along_axis(u[r], n, np.take_along_axis(u[r], n, 1) + 1, 1)
    return {"yr": R.reshape(N, 128, W).astype(np.float32), "yh": np.stack([H[:, :, h * M:(h + 1) * M].reshape(128, M) for h in range(N)]).astype(np.float32)}

def check_inputs(d):
    bad = list(check_ranges(d))
    if not bad:
        for name, y in reference(**d).items():
            for q in range(N):
                v = np.abs(np.asarray(y[q], np.float64)); s = np.sqrt(np.mean(v * v))
                if v.max() > 2 * s or s < 2.0 ** -2: bad.append('%s of rank %d is uneven or too small' % (name, q))
    return bad

@@ -1,0 +1,611 @@
+from concourse.bass import DstId, RemoteDMATransfer
+from concourse.mybir import AluOpType as A, ActivationFunctionType as AF
+
+N, W, M, K, S, RO = 4, 3840, 960, 1792, 112, 4
+SEG = 2304
+NLOG = W + RO * SEG
+F32, BF, I32, U16 = "float32", "bfloat16", "int32", "uint16"
+
+
+def _sb(shape, dtype):
+    return ("sbuf", [128] + list(shape), dtype)
+
+
+SCRATCH = {
+    "bt32": _sb([896], I32), "bto": _sb([896], U16), "lag32": _sb([240], I32), "ac": _sb([240], F32),
+    "a0": _sb([240], BF), "cap": _sb([240], F32), "cc": _sb([240], F32), "gl": _sb([4 * 240], F32),
+    "dG": ("dram", [3, 128, 240], F32), "dL": ("dram", [9, 128, 240], F32), "dW": ("dram", [8, W], F32),
+    "TB0": _sb([W], BF), "dig32": _sb([512], F32), "IF": _sb([128], F32), "big": _sb([128], BF), "VB": _sb([2, 64], BF), "cl32": _sb([480], F32),
+    "cf": _sb([16], F32), "GM": _sb([16], BF), "SA": _sb([48], BF), "DYN": _sb([512], BF),
+    "TB": _sb([W + 512], F32), "DEF": _sb([512], F32), "rep": _sb([2 * K], BF),
+    "ion": _sb([256], F32), "dig": _sb([512], BF),
+    "iop": _sb([128], I32), "iop2": _sb([256], I32), "iob": _sb([128], I32), "iob2": _sb([128], I32),
+    "BO": _sb([128], F32), "BC": _sb([8], F32), "bci": _sb([8], F32), "bct": _sb([8], F32),
+    "rowf": _sb([1], F32), "hoff": _sb([32], F32), "hcap0": _sb([32], F32), "hcap": _sb([32], F32),
+    "one": _sb([128], BF), "neg": _sb([128], BF), "IB": _sb([128], BF), "I64": _sb([128], BF), "NU": _sb([128], BF),
+    "RR": _sb([5 * 224], BF), "SB": _sb([128], BF), "SX": _sb([128], BF), "MM": _sb([1024], BF), "sgm": _sb([512], BF),
+    "PAYC": _sb([128, 16], BF), "PAY": _sb([K], F32),
+    "zz": _sb([256], F32), "am": _sb([256], I32), "sc": _sb([8, 2, 16], F32), "sel": _sb([128], F32), "best": _sb([128], F32),
+    "nd": _sb([128], F32), "n1d": _sb([128], F32), "nhd": _sb([128], F32), "tq": _sb([512], F32), "key": _sb([128], I32),
+    "mk": _sb([512], BF), "scn": _sb([512], BF), "t1": _sb([512], BF),
+    "nB": _sb([S], F32), "lB": _sb([S], F32), "z": _sb([S], F32), "y": _sb([S], F32), "mo": _sb([S], F32), "xo": _sb([128], F32), "xv": _sb([128], F32), "MF": _sb([512], F32),
+    "moff": _sb([S], U16), "xoff": _sb([RO * S], U16),
+    "GS": _sb([512], F32), "VT": _sb([32, 16], F32), "hv1": _sb([32], F32),
+    "nl16": _sb([RO * 32], U16), "ll16": _sb([RO * 32], U16), "HL": _sb([RO * 32], U16),
+    "LOG": _sb([NLOG], F32), "B": _sb([W + 512], F32), "H": _sb([M + 128], F32), "Bg": _sb([512], F32),
+    "PO": _sb([16, 136], F32), "PL": _sb([12, 136], F32), "AO": _sb([12 * 128], F32), "ht": _sb([512], F32),
+    "x": _sb([K], F32), "PR": _sb([K // 2], F32), "e": _sb([S], F32), "tgb": _sb([448], BF), "tgf": _sb([448], F32),
+    "cl": _sb([512], BF), "VF": _sb([512], BF), "fo": _sb([240], U16), "YO": _sb([W], F32),
+}
+for _b in range(8):
+    SCRATCH["b%d" % _b] = ("psum", [128, 512], F32)
+NDMA = 56
+SEMAPHORES = (["cV", "cS", "cP", "cG", "ls"] + ["d%d" % i for i in range(NDMA)] + ["rG%d" % t for t in range(3)]
+              + ["rA%d" % t for t in range(4)] + ["rP%d_%d" % (t, j) for t in range(4) for j in range(3)])
+
+CY, CG, CS, FIX, WAKE, PECY = 1.04, 1.55, 3.9, 60.0, 110.0, 0.6
+DMA_T, REM_T = 2200.0, 2600.0
+HOME_S, NSP = True, 4
+CAND, XG, DEFE, TRIES = "SVSV", "SS", "V", 3000
+OFF, UNIT, SAT = 32, 2.0 ** -13, 20.0
+BOTH = 65 * OFF
+PLAN = {}
+SEED = 12345
+LEAD, HEAT = 100.0, 300.0
+
+
+def build(g, T, topo, rank):
+    ops = []; now = ["s", 0]
+    V, SC, PE = g.vector, g.scalar, g.tensor
+    me = T.cores[rank]
+
+    def op(eng, fn, r, w, cost, banks=(), lat=0.0, kind="c", **kw):
+        d = {"eng": eng, "fn": fn, "r": list(r), "w": list(w), "cost": cost, "banks": list(banks), "lat": lat, "kind": kind}
+        d.update(kw)
+        d["stage"] = now[1]
+        d["tag"] = now[0] + str(eng) + "".join(ch for ch in (list(w) or list(r))[-1] if not ch.isdigit())
+        ops.append(d)
+        return len(ops) - 1
+
+    def vtt(out, a, b, o, r, w, cyc, banks=()):
+        op("V", lambda: V.tensor_tensor(out, a, b, o), r, w, FIX + CY * max(cyc, 64), banks)
+
+    def vts(out, a, s1, s2, o0, o1, r, w, cyc, banks=()):
+        if o1 is None:
+            op("V", lambda: V.tensor_scalar(out, a, s1, None, o0), r, w, FIX + CY * max(cyc, 64), banks)
+        else:
+            op("V", lambda: V.tensor_scalar(out, a, s1, s2, o0, o1), r, w, FIX + CY * max(cyc, 64), banks)
+
+    def vcp(out, a, r, w, cyc, banks=()):
+        op("V", lambda: V.tensor_copy(out, a), r, w, FIX + CY * max(cyc, 64), banks)
+
+    def vms(ap, c, w, cyc):
+        op("V", lambda: V.memset(ap, c), [], w, FIX + CY * max(cyc, 64))
+
+    def act(out, a, r, w, cyc, banks=(), f=AF.Identity, bias=0.0, scale=1.0, extra=0.0):
+        kw = {}
+        if not (isinstance(bias, float) and bias == 0.0):
+            kw["bias"] = bias
+        if not (isinstance(scale, float) and scale == 1.0):
+            kw["scale"] = scale
+        op("S", lambda: SC.activation(out, a, f, **kw), r, w, FIX + extra + CY * max(cyc, 64), banks)
+
+    def cp(eng, out, a, r, w, cyc):
+        if eng == "V":
+            vcp(out, a, r, w, cyc)
+        else:
+            act(out, a, r, w, cyc)
+
+    def mm(lst, r, w, cyc, banks):
+        def fn():
+            ins = None
+            for (o, l, rh, st, sp) in lst:
+                ins = PE.matmul(o, l, rh, st, sp)
+            return ins
+        op("P", fn, r, w, 40.0 + PECY * cyc, banks)
+
+    def grp(o, prs):
+        return [(o, l, rh, i == 0, i == len(prs) - 1) for i, (l, rh) in enumerate(prs)]
+
+    def dma(q, out, a, r, w, extra=0.0):
+        e = {"Y": g.sync, "S": g.scalar, "G": g}[q]
+        op(q, lambda: e.dma_start(out, a), r, w, 1000.0 if q == "G" else 100.0, lat=DMA_T + extra, kind="dma")
+
+    def iota(out, pat, base, cm, w, n, flag=False):
+        if flag:
+            op("G", lambda: g.iota(out, pat, base, cm, allow_small_or_imprecise_dtypes=True), [], w, 130 + 2 * CY * n)
+        else:
+            op("G", lambda: g.iota(out, pat, base, cm), [], w, 130 + 2 * CY * n)
+
+    def asel(out, a, pat, cmp, base, cm, r, w, n):
+        op("G", lambda: g.affine_select(out, a, pat, cmp, 0.0, base, cm), r, w, 170 + 2 * CY * n)
+
+    peers = [(rank + j) % N for j in range(1, N)]
+
+    def slot(src, dst):
+        return (src - dst) % N - 1
+
+    def dst_id(r):
+        a = topo.addr(T.cores[r])
+        return DstId(rid=a[0], pnc=a[1])
+
+    def mask_of(es):
+        return sum(1 << e for e in es)
+
+    def send1(r, out, a, sem, rd):
+        ad = topo.addr(T.cores[r]); mk = topo.mask(me, T.cores[r]); n = len(topo.engines(me, T.cores[r]))
+        return op("G", lambda: g.remote_dma(out, a, T.sem[sem], T.sem.ls, ad[1], ad[0], mk), rd, [], 500.0, kind="rem", ls=n), n
+
+    def recv(sem, cnt, after, w, lat):
+        op(None, None, [], w, 0.0, kind="recv", sem=sem, cnt=cnt, after=after, lat=lat)
+
+    TB, LOG, PAYC, x = T.TB, T.LOG, T.PAYC, T.x
+    b0, b1, b2, b3, b4, b5, b6, b7 = [T["b%d" % i] for i in range(8)]
+    TBN = ["TBw", "TBa", "TB2", "TB3", "TB4", "TB5", "TBo", "TBc", "TBg", "TBf0", "TBf1", "TBf2"]
+    RG = (9, 13, 14)
+
+    def prow(r):
+        return PAYC[0:S, r::16, :]
+
+    dma("Y", T.lag32[:], T.lag[:], [], ["lag32"])
+    dma("Y", T.bt32[:], T.bt[:], [], ["bt32"], 600.0)
+    dma("Y", T.tgb[0:16, :], T.tg[:], [], ["tgb"])
+    T0 = T.TB0; T0N = ["T0w", "T0a", "T04", "T05", "T0o"]
+    vms(T0[:], 0.0, T0N, W // 2)
+    iota(T.iop2[:, 2:3], [[0, 1]], 0, 1, ["iop2b"], 1)
+    iota(T.dig[:, 256:512], [[0, 4], [1, 64]], OFF, 0, ["digl"], 256, True)
+    iota(T.ion[:], [[1, 4], [0, 64]], OFF, 4, ["ion"], 256, True)
+    iota(T.iob[:], [[1, 128]], 128, -1, ["iob"], 128)
+    vms(T.one[:], 1.0, ["one"], 64)
+    vms(T.neg[:], -1.0, ["neg"], 64)
+    asel(T.SB[:], T.one[:], [[-1, 16], [-16, 8]], A.is_equal, 0, 1, ["one"], ["SB"], 128)
+    vts(T.iob2[:], T.iob[:], 15, None, A.bitwise_and, None, ["iob"], ["iob2"], 128)
+    vts(T.BO[:], T.iob2[:], 0.0, None, A.is_equal, None, ["iob2"], ["BO"], 128)
+    vts(T.iop2[:, 4:5], T.iop2[:, 2:3], 15, None, A.bitwise_and, None, ["iop2b"], ["iop2c"], 1)
+    vcp(T.rowf[:], T.iop2[:, 4:5], ["iop2c"], ["rowf"], 1)
+    vts(T.iop2[:, 0:1], T.iop2[:, 2:3], 1.0 / 15.0, -7.0 / 15.0, A.mult, A.add, ["iop2b"], ["iop2a"], 1)
+    vts(T.bct[:, 0:1], T.iop2[:, 0:1], -60.0, None, A.mult, None, ["iop2a"], ["bct0"], 1)
+    vts(T.dig[:, 0:256], T.ion[:], T.bct[:, 0:1], None, A.add, None, ["ion", "bct0"], ["digh"], 256)
+    vcp(T.a0[:], T.lag32[:], ["lag32"], ["a0"], 240)
+    act(T.ac[:], T.a0[:], ["a0"], ["ac"], 240)
+    dma("Y", T0[0::16, :], T.wt[:], [], ["T0w"], 300.0)
+    dma("S", T0[1::16, :], T.a0[:], ["a0"], ["T0a"], 300.0)
+    dma("Y", T0[4::16, :], T.dig[0:120, 0:256], ["digh"], ["T04"], 600.0)
+    dma("S", T0[5::16, :], T.dig[0:120, 256:512], ["digl"], ["T05"], 600.0)
+    act(T.dig32[:], T.dig[:], ["digh", "digl"], ["dig32"], 512, scale=UNIT)
+    for c in range(4):
+        act(TB[:, M * c:M * c + M], T0[:, M * c:M * c + M], T0N, TBN, M, scale=UNIT)
+    dma("Y", TB[2::16, 0:W], T.dig32[0:120, 0:256], ["dig32"], ["TB2"], 300.0)
+    dma("Y", TB[3::16, 0:W], T.dig32[0:120, 256:512], ["dig32"], ["TB3"], 600.0)
+    vcp(T.bto[:, 0:224], T.bt32[:, 0:224], ["bt32"], ["bto0"], 224)
+    vcp(T.bto[:, 224:896], T.bt32[:, 224:896], ["bt32"], ["bto1", "bto2", "bto3"], 672)
+    asel(T.IB[:], T.one[:], [[-1, 128]], A.is_equal, 0, 1, ["one"], ["IB"], 128)
+    asel(T.NU[:], T.neg[:], [[-1, 128]], A.is_gt, 0, 1, ["neg"], ["NU"], 128)
+    asel(T.IF[:], T.BO[:], [[-1, 128]], A.is_equal, 0, 1, ["BO"], ["IF"], 128)
+    act(T.SX[:, 0:32], T.SB[:, 16:48], ["SB"], ["SXa"], 32, scale=-1.0 / UNIT)
+    act(T.SX[:, 96:128], T.SB[:, 16:48], ["SB"], ["SXd"], 32, scale=1.0 / UNIT)
+    for j in range(2):
+        act(T.SX[:, 32 + 16 * j:48 + 16 * j], T.SB[:, 32:48], ["SB"], ["SXb%d" % j], 16)
+        act(T.SX[:, 64 + 16 * j:80 + 16 * j], T.SB[:, 32:48], ["SB"], ["SXc%d" % j], 16, scale=-1.0)
+    act(T.I64[:], T.IB[:], ["IB"], ["I64"], 128, scale=64.0)
+    for h in range(5):
+        act(T.RR[:, 224 * h:224 * h + S], T.IB[:, 0:S], ["IB"], ["RR%da" % h], S, scale=-200.0 if h < 4 else 1.0)
+        act(T.RR[:, 224 * h + S:224 * h + 224], T.IB[:, 0:S], ["IB"], ["RR%db" % h], S, scale=128.0 * h if h < 4 else 1.0)
+    RRS = ["RR%d%s" % (h, s) for h in range(5) for s in "ab"]
+    vms(T.sgm[:], 1.0, ["sgm"], 256)
+    vms(T.sgm[:, 0::16], 0.0, ["sgm"], 32)
+    vms(PAYC[:], 0.0, ["pc2", "pc3", "pc4", "pc5", "pc10", "pc11"], 1024)
+    iota(T.iop[:], [[0, 8], [S, 16]], W + 512, 1, ["iop"], 128)
+    vts(T.iop2[:, 128:256], T.iop[:], 6, None, A.arith_shift_right, None, ["iop"], ["iopd"], 128)
+    vts(prow(2), T.iop2[0:S, 128:256], float(OFF), None, A.add, None, ["iopd"], ["pc2"], 128)
+    vts(T.iop2[:, 128:256], T.iop[:], 63, None, A.bitwise_and, None, ["iop"], ["iopd"], 128)
+    vts(prow(3), T.iop2[0:S, 128:256], float(OFF), None, A.add, None, ["iopd"], ["pc3"], 128)
+    iota(T.bci[:, 0:4], [[SEG // 64, 4]], 0, 0, ["bci"], 4, True)
+    vts(T.bct[:, 4:8], T.bci[:, 0:4], T.BO[:, 2:3], UNIT, A.mult, A.mult, ["bci", "BO"], ["bct1"], 4)
+    act(T.bci[:, 4:8], T.BO[:, 6:10], ["BO"], ["bci2"], 4, scale=SAT)
+    vtt(T.BC[:, 0:4], T.bci[:, 4:8], T.bct[:, 4:8], A.add, ["bci2", "bct1"], ["BC"], 8)
+    vcp(T.cf[:, 0:1], T.BO[:, 9:10], ["BO"], ["cf0"], 1)
+    vcp(T.cf[:, 1:3], T.BO[:, 13:15], ["BO"], ["cf1"], 2)
+    vtt(T.bct[:, 1:4], T.BO[:, 6:9], T.cf[:, 0:3], A.add, ["BO", "cf0", "cf1"], ["bct2"], 8)
+    act(T.BC[:, 5:8], T.bct[:, 1:4], ["bct2"], ["BC5"], 4, scale=SAT)
+    vtt(T.cf[:, 4:6], T.BO[:, 10:12], T.BO[:, 1:13:11], A.add, ["BO"], ["cf4"], 8)
+    vtt(T.cf[:, 6:7], T.cf[:, 4:5], T.cf[:, 5:6], A.add, ["cf4"], ["cf6"], 8)
+    vts(T.cf[:, 8:11], T.BO[:, 6:9], 2.0, T.cf[:, 6:7], A.mult, A.add, ["BO", "cf6"], ["cf8"], 8)
+    vts(T.cf[:, 12:15], T.cf[:, 0:3], -100.0, None, A.mult, None, ["cf0", "cf1"], ["cf12"], 8)
+    vtt(T.cf[:, 8:11], T.cf[:, 8:11], T.cf[:, 12:15], A.add, ["cf8", "cf12"], ["cf8"], 8)
+    asel(T.GM[:, 8:16], T.one[:, 0:8], [[-16, 8]], A.is_ge, 0, 1, ["one"], ["GM0"], 8)
+    asel(T.GM[:, 0:8], T.GM[:, 8:16], [[16, 8]], A.is_ge, 15, -1, ["GM0"], ["GM"], 8)
+    for t in range(3):
+        act(T.SA[:, 16 * t:16 * t + 8], T.SB[:, 0:8], ["SB"], ["SA%da" % t], 8)
+        act(T.SA[:, 16 * t + 8:16 * t + 16], T.GM[:, 0:8], ["GM", "cf8"], ["SA%db" % t], 8, scale=T.cf[:, 8 + t:9 + t])
+    vtt(T.cf[:, 3:4], T.BO[:, 10:11], T.BO[:, 11:12], A.add, ["BO"], ["cf3"], 2)
+    act(T.cf[:, 7:8], T.BO[:, 4:5], ["BO"], ["cf7"], 1, scale=UNIT * (W // 64))
+    vts(T.BC[:, 4:5], T.cf[:, 3:4], UNIT * OFF, T.cf[:, 7:8], A.mult, A.add, ["cf3", "cf7"], ["BC4"], 1)
+    act(T.DEF[:], T0[:, 0:512], T0N + ["BC4"], ["DEF"], 512, bias=T.BC[:, 4:5], scale=UNIT)
+    vms(T.big[:], 1.0 / UNIT, ["big"], 64)
+    iota(T.hoff[:], [[M, 4], [0, 8]], BOTH, 0, ["hoff"], 32, True)
+    iota(T.hcap0[:], [[0, 4], [16, 8]], M, 0, ["hcap0"], 32, True)
+    vts(T.hcap[:], T.hcap0[:], T.rowf[:], None, A.add, None, ["hcap0", "rowf"], ["hcap"], 32)
+    for xh in range(2):
+        for e in range(2):
+            c = 128 * (2 * xh + e)
+            asel(T.MM[:, c:c + 128], T.big[:], [[-32, 4], [1000 - 16, 2], [-1, 16]], A.is_equal, 16 * (e - xh) - 1000 * e, 1,
+                 ["big"], ["MM%d" % (2 * xh + e)], 128)
+    act(T.MM[:, 512:1024], T.MM[:, 0:512], ["MM0", "MM1", "MM2", "MM3"], ["MM4"], 512, scale=64.0)
+    act(T.MF[:], T.MM[:, 0:512], ["MM0", "MM1", "MM2", "MM3"], ["MF"], 512, scale=UNIT)
+    vms(T.xo[:, S:128], 0.0, ["xop"], 16)
+    MMS = ["MM0", "MM1", "MM2", "MM3", "MM4"]
+    vts(T.tgf[0:16, :], T.tgb[0:16, :], -128.0, None, A.mult, None, ["tgb"], ["tgf"], 448)
+    vms(T.H[:, M:M + 128], 0.0, ["Hd"], 128)
+    vms(T.B[:, W:W + 512], 0.0, ["Bd"], 512)
+    vms(T.cl[:, 240:256], 0.0, ["clp0"], 16)
+    vms(T.cl[:, 496:512], 0.0, ["clp1"], 16)
+    dma("G", T.H[:, 0:M], T.e0[:, rank * M:(rank + 1) * M], ["gate"], ["H"], 2000.0)
+    dma("G", LOG[:, 0:W], T.e0[:], ["gate"], ["L0"], 9000.0)
+    dma("G", T.dW[:], T.wt[:], ["gate"], ["dW"], 500.0)
+    vcp(T.B[:, 0:W // 2], LOG[:, 0:W // 2], ["L0"], ["Ba"], W // 2)
+    vcp(T.B[:, W // 2:W], LOG[:, W // 2:W], ["L0"], ["Bb"], W // 2)
+    keep = ops[-5:]
+    for o in keep:
+        ops.remove(o)
+
+    def logres(t, ans):
+        r = ["L0"]
+        for u in range(t):
+            r += ["A%d_%s" % (u, h) for h in ("o", "r")] + ["X%d_%d" % (u, c) for c in range(4)]
+        if ans:
+            r += ["A%d_o" % t, "A%d_r" % t]
+        return r
+
+    def control(t):
+        for s in range(2):
+            for hf in range(2):
+                c = 224 * t + S * s + 56 * hf; o = K * s + 896 * hf
+                cp(CAND[2 * s + hf], T.rep[:, o:o + 896], (TB if t else T0)[:, 0:W].indirect(T.bto[:, c:c + 56]),
+                   (TBN if t else T0N) + ["bto%d" % t], ["rep%d%d" % (s, hf)] + (["gate"] if (t, s, hf) == (0, 0, 0) else []), CG * 896)
+        if t == 0:
+            ops.extend(keep)
+
+        def ch(s, k):
+            return T.rep[:, K * s + S * k:K * s + S * k + S]
+        for s in range(2):
+            for hf in range(2):
+                sa = T.SB[:, 0:16] if t == 0 else T.SA[:, 16 * t - 16:16 * t]
+                mm([(b0[0:S, 16 * s + k::32], ch(s, k), sa, True, True) for k in range(8 * hf, 8 * hf + 8)],
+                   ["rep%d%d" % (s, hf), "SB"] + ([] if t == 0 else ["SA%da" % (t - 1), "SA%db" % (t - 1)]), ["F0_%d%d" % (s, hf)], 512, [0])
+        F0 = ["F0_00", "F0_01", "F0_10", "F0_11"]
+        sp, sn = (T.SX[:, 32:64], T.SX[:, 64:96]) if t == 0 else (T.SX[:, 96:128], T.SX[:, 0:32])
+        SXS = ["SXd", "SXa", "SXb0", "SXb1", "SXc0", "SXc1"]
+        REP = ["rep00", "rep01", "rep10", "rep11"]
+        lst = []
+        for k in range(16):
+            lst += grp(b2[0:S, k::16], [(ch(1, k), sp), (ch(0, k), sn)])
+        mm(lst, REP + SXS, ["F2"], 2048, [2])
+        mm([(b1[0:S, k::16], ch(0, k), sp, True, True) for k in range(16)], REP + SXS, ["F1"], 1024, [1])
+        if t == 0:
+            vcp(T.am[0:S, :], b0[0:S, 256:512], F0, ["am"], 256, [0])
+        else:
+            vts(T.zz[0:S, :], b0[0:S, 256:512], -1.0, 2.0, A.mult, A.min, F0, ["zz"], 256, [0])
+            vtt(T.am[0:S, :], b0[0:S, 256:512], T.zz[0:S, :], A.max, F0 + ["zz"], ["am"], 256, [0])
+        vtt(T.sc[0:S], b0[0:S, 0:256], T.am[0:S, :], A.mult, F0 + ["am"], ["sc"], 256, [0])
+        vtt(T.sel[0:S, :], T.sc[0:S, :, 1, :], T.sc[0:S, :, 0, :], A.is_gt, ["sc"], ["sel"], 256)
+        vtt(T.best[0:S, :], T.sc[0:S, :, 1, :], T.sc[0:S, :, 0, :], A.max, ["sc"], ["best"], 256)
+        vts(T.nd[0:S, :], T.best[0:S, :], 4.0, -1000.0, A.is_lt, A.mult, ["best"], ["nd"], 128)
+        for q in (2, 3, 0, 1):
+            vtt(T.tq[0:S, 128 * q:128 * q + 128], b2[0:S, 128 * q:128 * q + 128], T.sel[0:S, :], A.mult, ["F2", "sel"], ["tq%d" % q], 128, [2])
+        vtt(T.n1d[0:S, :], b1[0:S, 256:384], T.nd[0:S, :], A.add, ["F1", "nd"], ["n1d"], 128, [1])
+        vtt(T.nhd[0:S, :], T.tq[0:S, 256:384], T.n1d[0:S, :], A.add, ["tq2", "n1d"], ["nhd"], 256)
+        vts(T.key[0:S, :], T.nhd[0:S, :], 1.0 / 15.0, -(7.0 + OFF) / 15.0, A.mult, A.add, ["nhd"], ["key"], 128)
+        for h in range(4):
+            vts(T.mk[0:S, 128 * h:128 * h + 128], T.key[0:S, :], float(h), None, A.is_equal, None, ["key"], ["mk%d" % h], 128)
+        MK = ["mk0", "mk1", "mk2", "mk3"]
+        op("V", lambda: V.tensor_tensor_scan(T.scn[0:S, :], T.sgm[0:S, :], T.mk[0:S, :], 0.0, A.mult, A.add), MK + ["sgm"], ["scn"], FIX + CY * 256)
+        for q, r in ((2, 4), (3, 5), (0, 10), (1, 11)):
+            vtt(prow(r), b1[0:S, 128 * q:128 * q + 128], T.tq[0:S, 128 * q:128 * q + 128], A.add, ["F1", "tq%d" % q], ["pc%d" % r], 128, [1])
+            act(T.DYN[0:S, 128 * q:128 * q + 128], prow(r), ["pc%d" % r], ["DYN%d" % q], 128)
+        mm(grp(b2[0:S, :], [(T.NU[0:S, 0:S], T.mk[0:S, :]), (T.one[0:S, 0:S], T.scn[0:S, :])]), MK + ["scn", "NU", "one"], ["F2"], 1024, [2])
+        vtt(T.t1[0:S, :], b2[0:S, :], T.mk[0:S, :], A.mult, ["F2"] + MK, ["t1"], 512, [2])
+        mm(grp(b3[:, 224:336], [(T.DYN[0:S, 256:384], T.I64[0:S, 0:S]), (T.DYN[0:S, 384:512], T.IB[0:S, 0:S])])
+           + grp(b3[:, 336:448], [(T.DYN[0:S, 0:128], T.I64[0:S, 0:S]), (T.DYN[0:S, 128:256], T.IB[0:S, 0:S])]),
+           ["DYN0", "DYN1", "DYN2", "DYN3", "I64", "IB"], ["Tn"], 448, [3])
+        act(T.nB[:], b3[:, 224:336], ["Tn"], ["nB"], S, [3], f=AF.Copy, bias=-float(W - 1 + BOTH))
+        act(T.lB[:], b3[:, 336:448], ["Tn"], ["lB"], S, [3], f=AF.Copy, bias=-float(W - 1 + SEG * t + BOTH))
+        lst = grp(b3[:, 0:224], [(T.mk[0:S, 128 * h:128 * h + 128], T.RR[0:S, 224 * h:224 * h + 224]) for h in range(4)]
+                  + [(T.t1[0:S, 128 * h:128 * h + 128], T.RR[0:S, 896:1120]) for h in range(4)])
+        mm(lst[:4], MK + RRS, ["Tp0"], 896, [3])
+        mm(lst[4:], ["t1", "Tp0"] + RRS, ["Tp"], 896, [3])
+        vts(T.z[:], b3[:, 0:S], -71.5, -16384.0, A.is_gt, A.mult, ["Tp"], ["z"], S, [3])
+        vtt(T.y[:], b3[:, S:224], T.z[:], A.add, ["Tp", "Tp0", "z"], ["y"], S, [3])
+        vtt(T.mo[:], T.y[:], T.nB[:], A.max, ["y", "nB"], ["mo"], 2 * S)
+        vts(T.moff[:], T.mo[:], float(W - 1), None, A.add, None, ["mo"], ["moff"], S)
+        vtt(T.xo[:, 0:S], T.y[:], T.lB[:], A.max, ["y", "lB", "xop"], ["xo"], 2 * S)
+        op("V", lambda: V.transpose(T.xv[:], T.xo[:]), ["xo", "xop"], ["xv"], FIX + CY * 128)
+        lst = []
+        for mh in range(7):
+            b, d = divmod(mh, 2)
+            lst += grp(b4[:, 304 + mh:416:7], [(T.MF[:, 128 * (2 * d + e):128 * (2 * d + e) + 128], T.xv[:, 32 * b + 16 * e:32 * b + 16 * e + 16]) for e in range(2)])
+        mm(lst, ["xv", "MF"], ["XW"], 3584, [4])
+        vts(T.xoff[:, S * t:S * t + S], b4[:, 304:416], float(W - 1 + SEG * t), None, A.add, None, ["XW"], ["xoff%d" % t], S, [4])
+        PCS = ["pc2", "pc3", "pc4", "pc5", "pc10", "pc11"]
+        for c in range(4):
+            bk = (b0, b1)[c % 2]; res = F0 if c % 2 == 0 else ["F1"]
+            mm([(bk[:, S * j:S * j + S], PAYC[0:S, :, 4 * c + j], T.IB[0:S, 0:S], True, True) for j in range(4)],
+               PCS + ["IB"], res, 448, [c % 2])
+            for j in range(4):
+                act(T.PAY[:, 4 * c + j::16], bk[:, S * j:S * j + S], res + ["BC"], ["pay%d" % (4 * c + j)], S, [c % 2], bias=T.BC[:, t:t + 1], scale=UNIT)
+        cp(DEFE, TB[:, W:W + 512], T.DEF[:], ["DEF"], ["TBp"], 512)
+        nsp = NSP if t else 1; cw = S // nsp
+        for c in range(nsp):
+            act(TB[:, :].indirect(T.moff[:, cw * c:cw * c + cw]), T.PAY[:, 16 * cw * c:16 * cw * (c + 1)], ["moff"] + ["pay%d" % k for k in range(16)],
+                TBN + ["TBp"], CS * K / nsp, f=AF.Tanh, extra=1300.0 if t == 0 else 0.0)
+        act(T.GS[:], TB[:, W:W + 512], ["TBp", "BC5"], ["GS"], 512, bias=T.BC[:, 5 + t:6 + t] if t < 3 else 0.0)
+        op("V", lambda: V.transpose(T.VT[:], TB[:, W:W + 512]), ["TBp"], ["VT"], FIX + CY * 512)
+        for q, r0 in enumerate((4, 10)):
+            if q == 1 and t == 0:
+                continue
+            vcp(T.VB[:, q], T.VT[:, :, r0:r0 + 2], ["VT"], ["VB%d" % q], 64)
+            lst = []
+            for xh in range(2):
+                prs = []
+                for e in range(2):
+                    c = 128 * (2 * xh + e)
+                    prs += [(T.MM[:, 512 + c:640 + c], T.VB[:, q, 2 * e::4]), (T.MM[:, c:c + 128], T.VB[:, q, 2 * e + 1::4])]
+                lst += grp(b4[:, 32 * q + xh:32 * q + 32:2], prs)
+            mm(lst, ["VB%d" % q] + MMS, ["LL%d" % q], 512, [4])
+        nl = T.nl16[:, 32 * t:32 * t + 32]
+        vts(nl, b4[:, 0:32], -float(BOTH), None, A.add, None, ["LL0"], ["nl%d" % t], 32, [4])
+        act(TB[:, :].indirect(nl), T.GS[:], ["nl%d" % t, "GS"], TBN + ["TBp"], CS * 512, f=AF.Tanh)
+        vtt(T.hv1[:], b4[:, 0:32], T.hoff[:], A.subtract, ["LL0", "hoff"], ["hva"], 32, [4])
+        vtt(T.PO[:, 4 * t:4 * t + 4, 128:136], T.hv1[:], T.hcap[:], A.min, ["hva", "hcap"], ["hv%d" % t], 64)
+        if t > 0:
+            vts(T.ll16[:, 32 * t:32 * t + 32], b4[:, 32:64], -float(BOTH), None, A.add, None, ["LL1"], ["ll%d" % t], 32, [4])
+        if t == RO - 1:
+            dma("Y", T.cl32[:, 0:240], TB[2::16, 0:W], ["TB2"], ["cl0"], 300.0)
+            dma("Y", T.cl32[:, 240:480], TB[3::16, 0:W], ["TB3"], ["cl1"], 600.0)
+            act(T.cl[:, 0:240], T.cl32[:, 0:240], ["cl0", "clp0"], ["cb0"], 240)
+            act(T.cl[:, 256:496], T.cl32[:, 240:480], ["cl1", "clp1"], ["cb1"], 240)
+            op("V", lambda: V.transpose(T.VF[:], T.cl[:]), ["cb0", "cb1", "clp0", "clp1"], ["VF"], FIX + CY * 256)
+            lst = []
+            for y1 in range(15):
+                b, d = divmod(y1, 2); prs = []
+                for e in range(2):
+                    c = 128 * (2 * d + e); o = 32 * b + 16 * e
+                    prs += [(T.MM[:, 512 + c:640 + c], T.VF[:, o:o + 16]), (T.MM[:, c:c + 128], T.VF[:, 256 + o:256 + o + 16])]
+                lst += grp(b4[:, 64 + y1:304:15], prs)
+            mm(lst, ["VF"] + MMS, ["AS"], 3840, [4])
+            vts(T.fo[:], b4[:, 64:304], -float(BOTH), None, A.add, None, ["AS"], ["fo"], 240, [4])
+            return
+        dma("Y", T.dG[t], TB[RG[t]::16, 0:W], ["TBg"], ["dG%d" % t])
+        es = topo.engines(me, T.cores[peers[0]])
+        tr = RemoteDMATransfer(dst_ids=[dst_id(r) for r in peers], dma_engine_mask=mask_of(es), remote_sem=T.sem["rG%d" % t], srcs=[T.dG[t]],
+                               dsts=[T.dL[3 * t + slot(rank, r)] for r in peers])
+        i = op("G", lambda: g.remote_dma_fused([tr], local_sem=T.sem.ls), ["dG%d" % t], [], 700.0, kind="rem", ls=len(es))
+        recv("rG%d" % t, 3 * len(es), [i], ["dL%d" % t], REM_T + 1500)
+        for j in range(3):
+            dma("YSY"[j], TB[10 + j::16, 0:W], T.dL[3 * t + j], ["dL%d" % t], ["TBf%d" % j], 300.0 * j)
+        dma("Y", TB[0::16, 0:W], T.dW[:], ["dW"], ["TBw"], 300.0)
+        dma("Y", TB[1::16, 0:W], T.ac[:], ["ac"], ["TBa"], 600.0)
+        if t == 2:
+            return
+        dma("Y", T.cc[:], TB[6 + t::16, 0:W], ["TBc"], ["cc"], 900.0)
+        for j in range(3):
+            dma("Y", T.gl[:, 240 * j:240 * j + 240], T.dL[3 * t + j], ["dL%d" % t], ["gl%d" % j], 1000.0 + 300.0 * j)
+        dma("Y", T.gl[:, 720:960], T.dG[t], ["dG%d" % t], ["gl3"], 900.0)
+        vts(T.cap[:], T.gl[:, 720:960], -100.0, 102.0, A.mult, A.add, ["gl3"], ["cap"], 240)
+        mm(grp(b4[:, 64:304], [(T.IF[:], T.ac[:]), (T.IF[:], T.cc[:]), (T.IF[:], T.cc[:])] + [(T.IF[:], T.gl[:, 240 * j:240 * j + 240]) for j in range(3)]),
+           ["IF", "ac", "cc", "gl0", "gl1", "gl2"], ["AS"], 5760, [4])
+        vtt(T.ac[:], b4[:, 64:304], T.cap[:], A.min, ["AS", "cap"], ["ac"], 240, [4])
+
+    def data(t):
+        a0 = W + SEG * t; x0 = a0 + 512
+        nl = T.nl16[:, 32 * t:32 * t + 32]
+        HW = T.H[:, :]
+        lists = {r: T.HL[:, 32 * t + 8 * r:32 * t + 8 * r + 8] for r in range(N)}
+        lres = {r: "HL%d_%d" % (t, r) for r in range(N)}
+        c0 = 128 if t == 0 else 0
+        if t > 0:
+            cp("V", T.Bg[:], T.B[:, :].indirect(nl), ["Ba", "Bb", "Bd", "nl%d" % t], ["Bg"], CG * 512)
+        sent = {}
+        for r in peers + [rank]:
+            o = 32 * t + 8 * r
+            if t > 0:
+                vtt(T.PO[:, 4 * t + r, 0:128], LOG[:, 0:a0].indirect(T.ll16[:, o:o + 8]), T.Bg[:, 128 * r:128 * r + 128], A.subtract,
+                    logres(t, False) + ["ll%d" % t, "Bg"], ["PO%d_%d" % (t, r)], CG * 128)
+            if r != rank:
+                j = slot(rank, r)
+                sent[j], n = send1(r, T.PL[:, 3 * t + j, c0:136], T.PO[:, 4 * t + r, c0:136], "rP%d_%d" % (t, j), ["PO%d_%d" % (t, r), "hv%d" % t])
+        for j in range(3):
+            recv("rP%d_%d" % (t, j), n, [sent[j]], ["PL%d_%d" % (t, j)], REM_T + 1500)
+        for i, r in enumerate([rank] + peers[::-1]):
+            if r == rank:
+                rs = ["PO%d_%d" % (t, r), "hv%d" % t]; buf, bi = T.PO, 4 * t + r
+            else:
+                j = slot(r, rank); rs = ["PL%d_%d" % (t, j)]; buf, bi = T.PL, 3 * t + j
+            vcp(lists[r], buf[:, bi, 128:136], rs, [lres[r]], 8)
+            if t > 0:
+                if HOME_S:
+                    act(T.ht[:, 128 * i:128 * i + 128], HW.indirect(lists[r]), ["H", "Hd", lres[r]], ["ht%d" % i], CG * 128)
+                    vtt(HW.indirect(lists[r]), T.ht[:, 128 * i:128 * i + 128], buf[:, bi, 0:128], A.add, ["ht%d" % i, lres[r]] + rs, ["H", "Hd"], CS * 128)
+                else:
+                    vtt(T.ht[:, 128 * i:128 * i + 128], HW.indirect(lists[r]), buf[:, bi, 0:128], A.add, ["H", "Hd", lres[r]] + rs, ["ht%d" % i], CG * 128)
+                    vcp(HW.indirect(lists[r]), T.ht[:, 128 * i:128 * i + 128], ["ht%d" % i, lres[r]], ["H", "Hd"], CS * 128)
+        sent = []
+        for i, r in enumerate(peers):
+            c = 128 * (3 * t + i)
+            cp("V" if i % 2 == 0 else "S", T.AO[:, c:c + 128], HW.indirect(lists[r]), ["H", "Hd", lres[r]], ["AO%d_%d" % (t, i)], CG * 128)
+            s, n = send1(r, LOG[:, a0 + 128 * rank:a0 + 128 * rank + 128], T.AO[:, c:c + 128], "rA%d" % t, ["AO%d_%d" % (t, i)])
+            sent.append(s)
+        cp("S", LOG[:, a0 + 128 * rank:a0 + 128 * rank + 128], HW.indirect(lists[rank]), ["H", "Hd", lres[rank]], ["A%d_o" % t], CG * 128)
+        recv("rA%d" % t, 3 * n, sent, ["A%d_r" % t], REM_T + 1500)
+        if t == RO - 1:
+            dma("Y", T.yh[:], T.H[:, 0:M], ["H"], ["yh"], 1500.0)
+        now[1] = 1
+        for hf in range(2):
+            o = S * t + 56 * hf
+            cp(("SV" if t == RO - 1 else XG)[hf], x[:, 896 * hf:896 * hf + 896], LOG[:, 0:x0].indirect(T.xoff[:, o:o + 56]), logres(t, True) + ["xoff%d" % t], ["x%d" % hf], CG * 896)
+        now[1] = 2
+        lst = grp(b5[:, 0:S], [(T.BO[0:16, :], T.tgf[0:16, S * t:S * t + S])] + [(T.BO[:], T.PR[:, S * k:S * k + S]) for k in range(8)])
+        mm(lst[:1], ["BO", "tgf"], ["p0", "st1"], 448, [5])
+        for c in range(4):
+            if t == RO - 1:
+                o = S * t + 14 * c
+                vtt(T.PR[:, 224 * c:224 * c + 224], LOG[:, 0:x0].indirect(T.xoff[:, o:o + 14]), x[:, 896 + 224 * c:1120 + 224 * c], A.mult,
+                    logres(t, True) + ["xoff%d" % t, "x1"], ["PR%d" % c], CG * 224)
+            else:
+                vtt(T.PR[:, 224 * c:224 * c + 224], x[:, 224 * c:224 * c + 224], x[:, 896 + 224 * c:1120 + 224 * c], A.mult, ["x0", "x1"], ["PR%d" % c], 448)
+            mm(lst[1 + 2 * c:3 + 2 * c], ["BO", "PR%d" % c, "p%d" % c], ["p%d" % (c + 1)], 896, [5])
+        act(T.e[:], b5[:, 0:S], ["p0", "p1", "p2", "p3", "p4"], ["e"], S, [5], f=AF.Tanh, scale=-1.0 / 128.0)
+        for j in range(4):
+            vts(b6[:, S * j:S * j + S], T.e[:], 1.0 / 32.0, None, A.mult, None, ["e"], ["E%d" % j], S, [6])
+        for c in range(4):
+            bk, bn = ((b7, 7), (b5, 5))[c % 2]; pk = (4 * c + 8) % 16
+            vtt(bk[:, 0:448], b6[:, 0:448], x[:, S * pk:S * pk + 448], A.mult, ["E0", "E1", "E2", "E3", "x0", "x1"],
+                ["st%d" % (c % 2)] + (["p0", "p1", "p2", "p3", "p4"] if bn == 5 else []), 448, [6, bn])
+            vtt(LOG[:, x0 + 448 * c:x0 + 448 * c + 448], bk[:, 0:448], x[:, 448 * c:448 * c + 448], A.add, ["st%d" % (c % 2), "x0", "x1"],
+                ["X%d_%d" % (t, c)], 448, [bn])
+        if t < RO - 1:
+            vcp(T.B[:, :].indirect(nl), LOG[:, a0:a0 + 512], ["nl%d" % t, "A%d_o" % t, "A%d_r" % t], ["Ba", "Bb", "Bd"], CS * 512)
+
+    for t in range(RO):
+        now[0] = "c%d" % t
+        control(t)
+        now[0] = "d%d" % t; now[1] = 0
+        data(t)
+    now[0] = "f"
+    for c in range(8):
+        cp("VS"[c % 2], T.YO[:, 480 * c:480 * c + 480], LOG[:, :].indirect(T.fo[:, 30 * c:30 * c + 30]), logres(RO, False) + ["fo"], ["YO%d" % c], CG * 480)
+        dma("Y", T.yr[:, 480 * c:480 * c + 480], T.YO[:, 480 * c:480 * c + 480], ["YO%d" % c], ["yr%d" % c], 1000.0)
+    return ops
+
+
+def order(ops):
+    n = len(ops); lastw = {}; readers = {}; bank = {}
+    for i, o in enumerate(ops):
+        d = set()
+        for r in o["r"]:
+            if r in lastw:
+                d.add(lastw[r])
+        for w in o["w"]:
+            if w in lastw:
+                d.add(lastw[w])
+            d.update(readers.get(w, ()))
+        for b in o["banks"]:
+            st = bank.setdefault(b, {"eng": None, "cur": [], "prev": []})
+            if st["eng"] != o["eng"]:
+                st["prev"] = st["cur"]; st["cur"] = []; st["eng"] = o["eng"]
+            d.update(st["prev"]); st["cur"].append(i)
+        for r in o["r"]:
+            readers.setdefault(r, []).append(i)
+        for w in o["w"]:
+            lastw[w] = i; readers[w] = []
+        d.discard(i)
+        o["deps"] = d
+    succ = [[] for _ in range(n)]
+    for i, o in enumerate(ops):
+        o["all"] = set(o["deps"]) | set(o.get("after", ()))
+        for j in o["all"]:
+            succ[j].append(i)
+    pr = [0.0] * n
+    for i in range(n - 1, -1, -1):
+        pr[i] = ops[i]["cost"] + ops[i]["lat"] + max([pr[j] + WAKE for j in succ[i]] + [0.0])
+    def place(bump):
+        busy = {}; fin = [0.0] * n; start = [0.0] * n
+        left = [len(o["all"]) for o in ops]; ready = [i for i in range(n) if left[i] == 0]
+        while ready:
+            i = max(ready, key=lambda j: pr[j] + bump[j])
+            ready.remove(i); o = ops[i]
+            t = max([fin[j] + (0.0 if o["kind"] == "recv" or (o["eng"] == "P" and ops[j]["eng"] == "P") else WAKE) for j in o["all"]] + [0.0])
+            if o["eng"]:
+                iv = busy.setdefault(o["eng"], []); k = 0
+                while k < len(iv) and iv[k][1] <= t:
+                    k += 1
+                while k < len(iv) and iv[k][0] < t + o["cost"]:
+                    t = max(t, iv[k][1]); k += 1
+                iv.insert(k, (t, t + o["cost"]))
+            start[i] = t; fin[i] = t + o["cost"] + o["lat"]
+            for j in succ[i]:
+                left[j] -= 1
+                if left[j] == 0:
+                    ready.append(j)
+        return max(fin), start, fin
+    if "seq" not in PLAN:
+        x = [SEED]
+
+        def rnd(k):
+            x[0] = (x[0] * 1103515245 + 12345) % 2147483648
+            return (x[0] >> 8) % k
+        first = place([-1e6 if o["tag"][0] == "d" else 0.0 for o in ops])[1]
+        mark = {}
+        for i, o in enumerate(ops):
+            mark.setdefault(o["tag"], first[i])
+        cur = []
+        for i, o in enumerate(ops):
+            tg = o["tag"]; want = first[i]
+            if tg[0] == "d" and int(tg[1]) < RO:
+                t = int(tg[1]); st = o.get("stage", 0)
+                if st == 0 or t == RO - 1:
+                    want = mark["c%dVnl" % t] + 300.0
+                elif st == 1:
+                    want = mark["c%dVam" % (t + 1)]
+                else:
+                    want = mark["c%dVmoff" % (t + 1)] + LEAD
+                want += i
+            cur.append(-want - pr[i])
+        best = place(cur); at = best[0]
+        for it in range(TRIES):
+            bump = list(cur); i = rnd(n); k = (1, 4, 12, 40)[rnd(4)]; d = (rnd(41) - 20) * (100, 400, 1500)[rnd(3)]
+            for j in range(i, min(n, i + 1 + rnd(k))):
+                bump[j] += d
+            res = place(bump)
+            if res[0] <= at + HEAT * (1.0 - it / TRIES) * rnd(100) / 100.0:
+                cur = [-res[1][j] - pr[j] for j in range(n)]; at = res[0]
+                if at < best[0]:
+                    best = res
+        PLAN["seq"] = sorted(range(n), key=lambda i: (best[1][i], i)); PLAN["t"] = best
+    for i, o in enumerate(ops):
+        o["start"] = PLAN["t"][1][i]; o["fin"] = PLAN["t"][2][i]
+    return PLAN["seq"]
+
+
+def rank_program(g, core, T, topo):
+    rank = T.rank_of(core)
+    if rank is None:
+        return
+    ops = build(g, T, topo, rank)
+    seq = order(ops)
+    Q = {"V": g.vector, "S": g.scalar, "P": g.tensor, "G": g, "Y": g.sync}
+    need = set()
+    for o in ops:
+        o["waits"] = [j for j in o["deps"] if not (o["eng"] == "P" and ops[j]["eng"] == "P")]
+        need.update(o["waits"])
+    cnt = {"cV": 0, "cS": 0, "cP": 0, "cG": 0}; nd = 0; ev = {}; ls = 0
+    for i in seq:
+        o = ops[i]
+        if o["kind"] == "c" and i in need:
+            s = "c" + o["eng"]; cnt[s] += 1; ev[i] = (s, cnt[s])
+        elif o["kind"] == "dma":
+            ev[i] = ("d%d" % nd, 16); nd += 1
+        elif o["kind"] == "recv":
+            ev[i] = (o["sem"], o["cnt"])
+    waited = {q: {} for q in Q}; top = {}
+    for i in seq:
+        o = ops[i]
+        if o["kind"] == "recv":
+            continue
+        want = {}
+        for j in o["waits"]:
+            s, c = ev[j]; want[s] = max(want.get(s, 0), c)
+        for s, c in want.items():
+            if waited[o["eng"]].get(s, 0) < c:
+                Q[o["eng"]].wait_ge(T.sem[s], c); waited[o["eng"]][s] = c; top[s] = max(top.get(s, 0), c)
+        ins = o["fn"]()
+        if o["kind"] == "dma":
+            ins.then_inc(T.sem[ev[i][0]], 16)
+        elif o["kind"] == "rem":
+            ls += o["ls"]
+        elif i in ev:
+            ins.then_inc(T.sem[ev[i][0]], 1)
+    for s, c in sorted(set(ev.values())):
+        if top.get(s, 0) < c:
+            g.wait_ge(T.sem[s], c); top[s] = c
+    g.wait_ge(T.sem.ls, ls)

@@ -26,7 +26,7 @@ SCRATCH = {
     "RR": _sb([5 * 224], BF), "SB": _sb([128], BF), "SX": _sb([128], BF), "MM": _sb([1024], BF), "sgm": _sb([512], BF),
     "PAYC": _sb([128, 16], BF), "PAY": _sb([K], F32),
     "zz": _sb([256], F32), "am": _sb([256], I32), "sc": _sb([8, 2, 16], F32), "sel": _sb([128], F32), "best": _sb([128], F32),
-    "nd": _sb([128], F32), "n1d": _sb([128], F32), "nhd": _sb([128], F32), "tq": _sb([512], F32), "key": _sb([128], I32),
+    "nd": _sb([128], F32), "nhd": _sb([128], F32), "tq": _sb([512], F32), "key": _sb([128], BF),
     "mk": _sb([512], BF), "scn": _sb([512], BF), "t1": _sb([512], BF),
     "nB": _sb([S], F32), "lB": _sb([S], F32), "z": _sb([S], F32), "y": _sb([S], F32), "mo": _sb([S], F32), "xo": _sb([128], F32), "xv": _sb([128], F32), "MF": _sb([512], F32),
     "moff": _sb([S], U16), "xoff": _sb([RO * S], U16),
@@ -40,18 +40,18 @@ SCRATCH = {
 for _b in range(8):
     SCRATCH["b%d" % _b] = ("psum", [128, 512], F32)
 NDMA = 56
-SEMAPHORES = (["cV", "cS", "cP", "cG", "ls"] + ["d%d" % i for i in range(NDMA)] + ["rG%d" % t for t in range(3)]
+SEMAPHORES = (["cV", "cS", "cP", "cG", "ls"] + ["d%d" % i for i in range(NDMA)] + ["rG%d_%d" % (t, j) for t in range(3) for j in range(3)]
               + ["rA%d" % t for t in range(4)] + ["rP%d_%d" % (t, j) for t in range(4) for j in range(3)])
 
-CY, CG, CS, FIX, WAKE, PECY = 1.04, 1.55, 3.9, 60.0, 110.0, 0.6
-DMA_T, REM_T = 2200.0, 2600.0
+CY, CG, CS, FIX, WAKE, PECY = 0.9, 1.56, 3.8, 55.0, 70.0, 0.48
+DMA_T, REM_T = 1900.0, 2200.0
 HOME_S, NSP = True, 4
-CAND, XG, DEFE, TRIES = "SVSV", "SS", "V", 3000
+CAND, XG, DEFE, TRIES = "SVSV", "SS", "V", 12000
 OFF, UNIT, SAT = 32, 2.0 ** -13, 20.0
 BOTH = 65 * OFF
 PLAN = {}
-SEED = 12345
-LEAD, HEAT = 100.0, 300.0
+SEED = 5
+LEAD, HEAT = 100.0, 200.0
 
 
 def build(g, T, topo, rank):
@@ -132,9 +132,9 @@ def build(g, T, topo, rank):
     def mask_of(es):
         return sum(1 << e for e in es)
 
-    def send1(r, out, a, sem, rd):
+    def send1(r, out, a, sem, rd, wr=()):
         ad = topo.addr(T.cores[r]); mk = topo.mask(me, T.cores[r]); n = len(topo.engines(me, T.cores[r]))
-        return op("G", lambda: g.remote_dma(out, a, T.sem[sem], T.sem.ls, ad[1], ad[0], mk), rd, [], 500.0, kind="rem", ls=n), n
+        return op("G", lambda: g.remote_dma(out, a, T.sem[sem], T.sem.ls, ad[1], ad[0], mk), rd, wr, 500.0, kind="rem", ls=n), n
 
     def recv(sem, cnt, after, w, lat):
         op(None, None, [], w, 0.0, kind="recv", sem=sem, cnt=cnt, after=after, lat=lat)
@@ -174,9 +174,7 @@ def build(g, T, topo, rank):
     dma("S", T0[5::16, :], T.dig[0:120, 256:512], ["digl"], ["T05"], 600.0)
     act(T.dig32[:], T.dig[:], ["digh", "digl"], ["dig32"], 512, scale=UNIT)
     for c in range(4):
-        act(TB[:, M * c:M * c + M], T0[:, M * c:M * c + M], T0N, TBN, M, scale=UNIT)
-    dma("Y", TB[2::16, 0:W], T.dig32[0:120, 0:256], ["dig32"], ["TB2"], 300.0)
-    dma("Y", TB[3::16, 0:W], T.dig32[0:120, 256:512], ["dig32"], ["TB3"], 600.0)
+        act(TB[:, M * c:M * c + M], T0[:, M * c:M * c + M], T0N, TBN, M, scale=UNIT, f=AF.Tanh, extra=1300.0 * (c == 0))
     vcp(T.bto[:, 0:224], T.bt32[:, 0:224], ["bt32"], ["bto0"], 224)
     vcp(T.bto[:, 224:896], T.bt32[:, 224:896], ["bt32"], ["bto1", "bto2", "bto3"], 672)
     asel(T.IB[:], T.one[:], [[-1, 128]], A.is_equal, 0, 1, ["one"], ["IB"], 128)
@@ -241,16 +239,19 @@ def build(g, T, topo, rank):
     vms(T.cl[:, 240:256], 0.0, ["clp0"], 16)
     vms(T.cl[:, 496:512], 0.0, ["clp1"], 16)
     dma("G", T.H[:, 0:M], T.e0[:, rank * M:(rank + 1) * M], ["gate"], ["H"], 2000.0)
-    dma("G", LOG[:, 0:W], T.e0[:], ["gate"], ["L0"], 9000.0)
+    dma("G", LOG[:, 0:W // 2], T.e0[:, 0:W // 2], ["gate"], ["L0a"], 4000.0)
+    dma("Y", TB[2::16, 0:W], T.dig32[0:120, 0:256], ["dig32", "L0a"], ["TB2", "row2"], 300.0)
+    dma("Y", TB[3::16, 0:W], T.dig32[0:120, 256:512], ["dig32", "L0a"], ["TB3", "row3"], 600.0)
+    dma("G", LOG[:, W // 2:W], T.e0[:, W // 2:W], ["row2", "row3"], ["L0"], 4000.0)
     dma("G", T.dW[:], T.wt[:], ["gate"], ["dW"], 500.0)
-    vcp(T.B[:, 0:W // 2], LOG[:, 0:W // 2], ["L0"], ["Ba"], W // 2)
+    vcp(T.B[:, 0:W // 2], LOG[:, 0:W // 2], ["L0a"], ["Ba"], W // 2)
     vcp(T.B[:, W // 2:W], LOG[:, W // 2:W], ["L0"], ["Bb"], W // 2)
-    keep = ops[-5:]
+    keep = ops[-8:]
     for o in keep:
         ops.remove(o)
 
     def logres(t, ans):
-        r = ["L0"]
+        r = ["L0", "L0a"]
         for u in range(t):
             r += ["A%d_%s" % (u, h) for h in ("o", "r")] + ["X%d_%d" % (u, c) for c in range(4)]
         if ans:
@@ -260,9 +261,10 @@ def build(g, T, topo, rank):
     def control(t):
         for s in range(2):
             for hf in range(2):
-                c = 224 * t + S * s + 56 * hf; o = K * s + 896 * hf
-                cp(CAND[2 * s + hf], T.rep[:, o:o + 896], (TB if t else T0)[:, 0:W].indirect(T.bto[:, c:c + 56]),
-                   (TBN if t else T0N) + ["bto%d" % t], ["rep%d%d" % (s, hf)] + (["gate"] if (t, s, hf) == (0, 0, 0) else []), CG * 896)
+                for u, (k0, k1) in enumerate(((0, 6), (6, 8)) if s else ((0, 8),)):
+                    c = 224 * t + S * s + 56 * hf + 7 * k0; o = K * s + 896 * hf + S * k0; nk = k1 - k0
+                    cp(CAND[2 * s + hf], T.rep[:, o:o + S * nk], (TB if t else T0)[:, 0:W].indirect(T.bto[:, c:c + 7 * nk]),
+                       (TBN if t else T0N) + ["bto%d" % t], ["rep%d%d" % (s + u, hf)] + (["gate"] if (t, s, hf) == (0, 0, 0) else []), CG * S * nk)
         if t == 0:
             ops.extend(keep)
 
@@ -271,12 +273,13 @@ def build(g, T, topo, rank):
         for s in range(2):
             for hf in range(2):
                 sa = T.SB[:, 0:16] if t == 0 else T.SA[:, 16 * t - 16:16 * t]
-                mm([(b0[0:S, 16 * s + k::32], ch(s, k), sa, True, True) for k in range(8 * hf, 8 * hf + 8)],
-                   ["rep%d%d" % (s, hf), "SB"] + ([] if t == 0 else ["SA%da" % (t - 1), "SA%db" % (t - 1)]), ["F0_%d%d" % (s, hf)], 512, [0])
-        F0 = ["F0_00", "F0_01", "F0_10", "F0_11"]
+                for u, (k0, k1) in enumerate(((0, 6), (6, 8)) if s else ((0, 8),)):
+                    mm([(b0[0:S, 16 * s + k::32], ch(s, k), sa, True, True) for k in range(8 * hf + k0, 8 * hf + k1)],
+                       ["rep%d%d" % (s + u, hf), "SB"] + ([] if t == 0 else ["SA%da" % (t - 1), "SA%db" % (t - 1)]), ["F0_%d%d" % (s + u, hf)], 64 * (k1 - k0), [0])
+        F0 = ["F0_00", "F0_01", "F0_10", "F0_11", "F0_20", "F0_21"]
         sp, sn = (T.SX[:, 32:64], T.SX[:, 64:96]) if t == 0 else (T.SX[:, 96:128], T.SX[:, 0:32])
         SXS = ["SXd", "SXa", "SXb0", "SXb1", "SXc0", "SXc1"]
-        REP = ["rep00", "rep01", "rep10", "rep11"]
+        REP = ["rep00", "rep01", "rep10", "rep11", "rep20", "rep21"]
         lst = []
         for k in range(16):
             lst += grp(b2[0:S, k::16], [(ch(1, k), sp), (ch(0, k), sn)])
@@ -293,16 +296,15 @@ def build(g, T, topo, rank):
         vts(T.nd[0:S, :], T.best[0:S, :], 4.0, -1000.0, A.is_lt, A.mult, ["best"], ["nd"], 128)
         for q in (2, 3, 0, 1):
             vtt(T.tq[0:S, 128 * q:128 * q + 128], b2[0:S, 128 * q:128 * q + 128], T.sel[0:S, :], A.mult, ["F2", "sel"], ["tq%d" % q], 128, [2])
-        vtt(T.n1d[0:S, :], b1[0:S, 256:384], T.nd[0:S, :], A.add, ["F1", "nd"], ["n1d"], 128, [1])
-        vtt(T.nhd[0:S, :], T.tq[0:S, 256:384], T.n1d[0:S, :], A.add, ["tq2", "n1d"], ["nhd"], 256)
-        vts(T.key[0:S, :], T.nhd[0:S, :], 1.0 / 15.0, -(7.0 + OFF) / 15.0, A.mult, A.add, ["nhd"], ["key"], 128)
-        for h in range(4):
-            vts(T.mk[0:S, 128 * h:128 * h + 128], T.key[0:S, :], float(h), None, A.is_equal, None, ["key"], ["mk%d" % h], 128)
-        MK = ["mk0", "mk1", "mk2", "mk3"]
-        op("V", lambda: V.tensor_tensor_scan(T.scn[0:S, :], T.sgm[0:S, :], T.mk[0:S, :], 0.0, A.mult, A.add), MK + ["sgm"], ["scn"], FIX + CY * 256)
         for q, r in ((2, 4), (3, 5), (0, 10), (1, 11)):
             vtt(prow(r), b1[0:S, 128 * q:128 * q + 128], T.tq[0:S, 128 * q:128 * q + 128], A.add, ["F1", "tq%d" % q], ["pc%d" % r], 128, [1])
             act(T.DYN[0:S, 128 * q:128 * q + 128], prow(r), ["pc%d" % r], ["DYN%d" % q], 128)
+        vts(T.nhd[0:S, :], prow(4), 1.0 / 15.0, 130.0 - (7.0 + OFF) / 15.0, A.mult, A.add, ["pc4"], ["nhd"], 128)
+        vtt(T.key[0:S, :], T.nhd[0:S, :], T.nd[0:S, :], A.add, ["nhd", "nd"], ["key"], 256)
+        for h in range(4):
+            vts(T.mk[0:S, 128 * h:128 * h + 128], T.key[0:S, :], 130.0 + h, None, A.is_equal, None, ["key"], ["mk%d" % h], 64)
+        MK = ["mk0", "mk1", "mk2", "mk3"]
+        op("V", lambda: V.tensor_tensor_scan(T.scn[0:S, :], T.sgm[0:S, :], T.mk[0:S, :], 0.0, A.mult, A.add), MK + ["sgm"], ["scn"], FIX + CY * 256)
         mm(grp(b2[0:S, :], [(T.NU[0:S, 0:S], T.mk[0:S, :]), (T.one[0:S, 0:S], T.scn[0:S, :])]), MK + ["scn", "NU", "one"], ["F2"], 1024, [2])
         vtt(T.t1[0:S, :], b2[0:S, :], T.mk[0:S, :], A.mult, ["F2"] + MK, ["t1"], 512, [2])
         mm(grp(b3[:, 224:336], [(T.DYN[0:S, 256:384], T.I64[0:S, 0:S]), (T.DYN[0:S, 384:512], T.IB[0:S, 0:S])])
@@ -337,7 +339,7 @@ def build(g, T, topo, rank):
         nsp = NSP if t else 1; cw = S // nsp
         for c in range(nsp):
             act(TB[:, :].indirect(T.moff[:, cw * c:cw * c + cw]), T.PAY[:, 16 * cw * c:16 * cw * (c + 1)], ["moff"] + ["pay%d" % k for k in range(16)],
-                TBN + ["TBp"], CS * K / nsp, f=AF.Tanh, extra=1300.0 if t == 0 else 0.0)
+                TBN + ["TBp"], CS * K / nsp, f=AF.Tanh)
         act(T.GS[:], TB[:, W:W + 512], ["TBp", "BC5"], ["GS"], 512, bias=T.BC[:, 5 + t:6 + t] if t < 3 else 0.0)
         op("V", lambda: V.transpose(T.VT[:], TB[:, W:W + 512]), ["TBp"], ["VT"], FIX + CY * 512)
         for q, r0 in enumerate((4, 10)):
@@ -376,21 +378,21 @@ def build(g, T, topo, rank):
             vts(T.fo[:], b4[:, 64:304], -float(BOTH), None, A.add, None, ["AS"], ["fo"], 240, [4])
             return
         dma("Y", T.dG[t], TB[RG[t]::16, 0:W], ["TBg"], ["dG%d" % t])
-        es = topo.engines(me, T.cores[peers[0]])
-        tr = RemoteDMATransfer(dst_ids=[dst_id(r) for r in peers], dma_engine_mask=mask_of(es), remote_sem=T.sem["rG%d" % t], srcs=[T.dG[t]],
-                               dsts=[T.dL[3 * t + slot(rank, r)] for r in peers])
-        i = op("G", lambda: g.remote_dma_fused([tr], local_sem=T.sem.ls), ["dG%d" % t], [], 700.0, kind="rem", ls=len(es))
-        recv("rG%d" % t, 3 * len(es), [i], ["dL%d" % t], REM_T + 1500)
-        for j in range(3):
-            dma("YSY"[j], TB[10 + j::16, 0:W], T.dL[3 * t + j], ["dL%d" % t], ["TBf%d" % j], 300.0 * j)
-        dma("Y", TB[0::16, 0:W], T.dW[:], ["dW"], ["TBw"], 300.0)
-        dma("Y", TB[1::16, 0:W], T.ac[:], ["ac"], ["TBa"], 600.0)
+        for i, r in enumerate(peers):
+            j = slot(rank, r)
+            s, n = send1(r, T.dL[3 * t + j], T.dG[t], "rG%d_%d" % (t, j), ["dG%d" % t] + ["ord%d" % (i - 1)] * (i > 0), ["ord%d" % i])
+            recv("rG%d_%d" % (t, j), n, [s], ["dL%d_%d" % (t, j)], REM_T + 900 + 300 * i)
+        for j in (2, 1, 0):
+            dma("Y", TB[10 + j::16, 0:W], T.dL[3 * t + j], ["dL%d_%d" % (t, j)], ["TBf%d" % j], 200.0)
+        dma("Y", TB[0::16, 0:W], T.dW[:], ["dW", "dG%d" % t], ["TBw"], 300.0)
+        dma("Y", TB[1::16, 0:W], T.ac[:], ["ac", "dG%d" % t], ["TBa"], 600.0)
         if t == 2:
             return
-        dma("Y", T.cc[:], TB[6 + t::16, 0:W], ["TBc"], ["cc"], 900.0)
+        aft = ["TBf0", "TBf1", "TBf2"]
+        dma("Y", T.cc[:], TB[6 + t::16, 0:W], ["TBc"] + aft, ["cc"], 900.0)
         for j in range(3):
-            dma("Y", T.gl[:, 240 * j:240 * j + 240], T.dL[3 * t + j], ["dL%d" % t], ["gl%d" % j], 1000.0 + 300.0 * j)
-        dma("Y", T.gl[:, 720:960], T.dG[t], ["dG%d" % t], ["gl3"], 900.0)
+            dma("Y", T.gl[:, 240 * j:240 * j + 240], T.dL[3 * t + j], ["dL%d_%d" % (t, j)] + aft, ["gl%d" % j], 1000.0 + 300.0 * j)
+        dma("Y", T.gl[:, 720:960], T.dG[t], ["dG%d" % t] + aft, ["gl3"], 900.0)
         vts(T.cap[:], T.gl[:, 720:960], -100.0, 102.0, A.mult, A.add, ["gl3"], ["cap"], 240)
         mm(grp(b4[:, 64:304], [(T.IF[:], T.ac[:]), (T.IF[:], T.cc[:]), (T.IF[:], T.cc[:])] + [(T.IF[:], T.gl[:, 240 * j:240 * j + 240]) for j in range(3)]),
            ["IF", "ac", "cc", "gl0", "gl1", "gl2"], ["AS"], 5760, [4])
@@ -404,13 +406,16 @@ def build(g, T, topo, rank):
         lres = {r: "HL%d_%d" % (t, r) for r in range(N)}
         c0 = 128 if t == 0 else 0
         if t > 0:
-            cp("V", T.Bg[:], T.B[:, :].indirect(nl), ["Ba", "Bb", "Bd", "nl%d" % t], ["Bg"], CG * 512)
+            if t < RO - 1:
+                cp("V", T.Bg[:], T.B[:, :].indirect(nl), ["Ba", "Bb", "Bd", "nl%d" % t], ["Bg%d" % r for r in range(N)], CG * 512)
         sent = {}
         for r in peers + [rank]:
             o = 32 * t + 8 * r
+            if t == RO - 1:
+                cp("S", T.Bg[:, 128 * r:128 * r + 128], T.B[:, :].indirect(T.nl16[:, o:o + 8]), ["Ba", "Bb", "Bd", "nl%d" % t], ["Bg%d" % r], CG * 128)
             if t > 0:
                 vtt(T.PO[:, 4 * t + r, 0:128], LOG[:, 0:a0].indirect(T.ll16[:, o:o + 8]), T.Bg[:, 128 * r:128 * r + 128], A.subtract,
-                    logres(t, False) + ["ll%d" % t, "Bg"], ["PO%d_%d" % (t, r)], CG * 128)
+                    logres(t, False) + ["ll%d" % t, "Bg%d" % r], ["PO%d_%d" % (t, r)], CG * 128)
             if r != rank:
                 j = slot(rank, r)
                 sent[j], n = send1(r, T.PL[:, 3 * t + j, c0:136], T.PO[:, 4 * t + r, c0:136], "rP%d_%d" % (t, j), ["PO%d_%d" % (t, r), "hv%d" % t])
@@ -438,11 +443,18 @@ def build(g, T, topo, rank):
         cp("S", LOG[:, a0 + 128 * rank:a0 + 128 * rank + 128], HW.indirect(lists[rank]), ["H", "Hd", lres[rank]], ["A%d_o" % t], CG * 128)
         recv("rA%d" % t, 3 * n, sent, ["A%d_r" % t], REM_T + 1500)
         if t == RO - 1:
-            dma("Y", T.yh[:], T.H[:, 0:M], ["H"], ["yh"], 1500.0)
+            dma("Y", T.yh[:], T.H[:, 0:M], ["H", "A%d_r" % t], ["yh"], 1500.0)
         now[1] = 1
+        X1 = ["x10", "x11", "x12", "x13"]; XX = ["x0"] + X1
         for hf in range(2):
             o = S * t + 56 * hf
-            cp(("SV" if t == RO - 1 else XG)[hf], x[:, 896 * hf:896 * hf + 896], LOG[:, 0:x0].indirect(T.xoff[:, o:o + 56]), logres(t, True) + ["xoff%d" % t], ["x%d" % hf], CG * 896)
+            if hf == 1 and t == RO - 1:
+                for c in range(4):
+                    cp("S", x[:, 896 + 224 * c:1120 + 224 * c], LOG[:, 0:x0].indirect(T.xoff[:, o + 14 * c:o + 14 * c + 14]),
+                       logres(t, True) + ["xoff%d" % t], ["x1%d" % c], CG * 224)
+            else:
+                cp(XG[hf], x[:, 896 * hf:896 * hf + 896], LOG[:, 0:x0].indirect(T.xoff[:, o:o + 56]), logres(t, True) + ["xoff%d" % t],
+                   ["x0"] if hf == 0 else X1, CG * 896)
         now[1] = 2
         lst = grp(b5[:, 0:S], [(T.BO[0:16, :], T.tgf[0:16, S * t:S * t + S])] + [(T.BO[:], T.PR[:, S * k:S * k + S]) for k in range(8)])
         mm(lst[:1], ["BO", "tgf"], ["p0", "st1"], 448, [5])
@@ -450,18 +462,27 @@ def build(g, T, topo, rank):
             if t == RO - 1:
                 o = S * t + 14 * c
                 vtt(T.PR[:, 224 * c:224 * c + 224], LOG[:, 0:x0].indirect(T.xoff[:, o:o + 14]), x[:, 896 + 224 * c:1120 + 224 * c], A.mult,
-                    logres(t, True) + ["xoff%d" % t, "x1"], ["PR%d" % c], CG * 224)
+                    logres(t, True) + ["xoff%d" % t, "x1%d" % c], ["PR%d" % c], CG * 224)
             else:
-                vtt(T.PR[:, 224 * c:224 * c + 224], x[:, 224 * c:224 * c + 224], x[:, 896 + 224 * c:1120 + 224 * c], A.mult, ["x0", "x1"], ["PR%d" % c], 448)
+                vtt(T.PR[:, 224 * c:224 * c + 224], x[:, 224 * c:224 * c + 224], x[:, 896 + 224 * c:1120 + 224 * c], A.mult, XX, ["PR%d" % c], 448)
             mm(lst[1 + 2 * c:3 + 2 * c], ["BO", "PR%d" % c, "p%d" % c], ["p%d" % (c + 1)], 896, [5])
         act(T.e[:], b5[:, 0:S], ["p0", "p1", "p2", "p3", "p4"], ["e"], S, [5], f=AF.Tanh, scale=-1.0 / 128.0)
         for j in range(4):
             vts(b6[:, S * j:S * j + S], T.e[:], 1.0 / 32.0, None, A.mult, None, ["e"], ["E%d" % j], S, [6])
         for c in range(4):
             bk, bn = ((b7, 7), (b5, 5))[c % 2]; pk = (4 * c + 8) % 16
-            vtt(bk[:, 0:448], b6[:, 0:448], x[:, S * pk:S * pk + 448], A.mult, ["E0", "E1", "E2", "E3", "x0", "x1"],
+            if t == RO - 1 and c < 2:
+                bk = (b0, b1)[c]; pr = ["PR%d" % (2 * c), "PR%d" % (2 * c + 1)]
+                res = ["F0_00", "F0_01", "F0_10", "F0_11", "F0_20", "F0_21"] if c == 0 else ["F1"]
+                lst = grp(bk[:, 0:448], [(T.IF[:], x[:, 448 * c:448 * c + 448]), (T.IF[:], T.PR[:, 448 * c:448 * c + 448])])
+                mm(lst[:1], ["IF", "p4"] + XX, res, 1792, [c])
+                vtt(T.PR[:, 448 * c:448 * c + 448], b6[:, 0:448], x[:, S * pk:S * pk + 448], A.mult, ["E0", "E1", "E2", "E3"] + XX, pr, 448, [6])
+                mm(lst[1:], ["IF"] + pr + res, ["ad%d" % c], 1792, [c])
+                act(LOG[:, x0 + 448 * c:x0 + 448 * c + 448], bk[:, 0:448], res + ["ad%d" % c], ["X%d_%d" % (t, c)], 448, [c])
+                continue
+            vtt(bk[:, 0:448], b6[:, 0:448], x[:, S * pk:S * pk + 448], A.mult, ["E0", "E1", "E2", "E3"] + XX,
                 ["st%d" % (c % 2)] + (["p0", "p1", "p2", "p3", "p4"] if bn == 5 else []), 448, [6, bn])
-            vtt(LOG[:, x0 + 448 * c:x0 + 448 * c + 448], bk[:, 0:448], x[:, 448 * c:448 * c + 448], A.add, ["st%d" % (c % 2), "x0", "x1"],
+            vtt(LOG[:, x0 + 448 * c:x0 + 448 * c + 448], bk[:, 0:448], x[:, 448 * c:448 * c + 448], A.add, ["st%d" % (c % 2)] + XX,
                 ["X%d_%d" % (t, c)], 448, [bn])
         if t < RO - 1:
             vcp(T.B[:, :].indirect(nl), LOG[:, a0:a0 + 512], ["nl%d" % t, "A%d_o" % t, "A%d_r" % t], ["Ba", "Bb", "Bd"], CS * 512)
@@ -510,24 +531,36 @@ def order(ops):
         pr[i] = ops[i]["cost"] + ops[i]["lat"] + max([pr[j] + WAKE for j in succ[i]] + [0.0])
     def place(bump):
         busy = {}; fin = [0.0] * n; start = [0.0] * n
-        left = [len(o["all"]) for o in ops]; ready = [i for i in range(n) if left[i] == 0]
+        key = [pr[j] + bump[j] for j in range(n)]; rdy = [0.0] * n
+        left = list(nin); ready = list(roots);
         while ready:
-            i = max(ready, key=lambda j: pr[j] + bump[j])
-            ready.remove(i); o = ops[i]
-            t = max([fin[j] + (0.0 if o["kind"] == "recv" or (o["eng"] == "P" and ops[j]["eng"] == "P") else WAKE) for j in o["all"]] + [0.0])
-            if o["eng"]:
-                iv = busy.setdefault(o["eng"], []); k = 0
-                while k < len(iv) and iv[k][1] <= t:
+            i = ready[0]
+            for j in ready:
+                if key[j] > key[i]:
+                    i = j
+            ready.remove(i)
+            t = rdy[i]; e, c, lat = flat[i]
+            if e:
+                iv = busy.setdefault(e, []); k = len(iv)
+                while k > 0 and iv[k - 1][1] > t:
+                    k -= 1
+                while k < len(iv) and iv[k][0] < t + c:
+                    if iv[k][1] > t:
+                        t = iv[k][1]
                     k += 1
-                while k < len(iv) and iv[k][0] < t + o["cost"]:
-                    t = max(t, iv[k][1]); k += 1
-                iv.insert(k, (t, t + o["cost"]))
-            start[i] = t; fin[i] = t + o["cost"] + o["lat"]
-            for j in succ[i]:
+                iv.insert(k, (t, t + c))
+            start[i] = t; f = t + c + lat; fin[i] = f
+            for j, wk in out[i]:
+                if f + wk > rdy[j]:
+                    rdy[j] = f + wk
                 left[j] -= 1
                 if left[j] == 0:
                     ready.append(j)
         return max(fin), start, fin
+    nin = [len(o["all"]) for o in ops]; roots = [i for i in range(n) if nin[i] == 0]
+    flat = [(o["eng"], o["cost"], o["lat"]) for o in ops]
+    out = [[(j, 0.0 if ops[j]["kind"] == "recv" or ops[i]["kind"] == "rem" or (ops[j]["eng"] == "P" and ops[i]["eng"] == "P") else WAKE)
+            for j in succ[i]] for i in range(n)]
     if "seq" not in PLAN:
         x = [SEED]
 
@@ -576,7 +609,7 @@ def rank_program(g, core, T, topo):
     Q = {"V": g.vector, "S": g.scalar, "P": g.tensor, "G": g, "Y": g.sync}
     need = set()
     for o in ops:
-        o["waits"] = [j for j in o["deps"] if not (o["eng"] == "P" and ops[j]["eng"] == "P")]
+        o["waits"] = [j for j in o["deps"] if not (o["eng"] == "P" and ops[j]["eng"] == "P") and ops[j]["kind"] != "rem"]
         need.update(o["waits"])
     cnt = {"cV": 0, "cS": 0, "cP": 0, "cG": 0}; nd = 0; ev = {}; ls = 0
     for i in seq:
@@ -593,7 +626,7 @@ def rank_program(g, core, T, topo):
         if o["kind"] == "recv":
             continue
         want = {}
-        for j in o["waits"]:
+        for j in sorted(o["waits"]):
             s, c = ev[j]; want[s] = max(want.get(s, 0), c)
         for s, c in want.items():
             if waited[o["eng"]].get(s, 0) < c:

@@ -2,8 +2,9 @@ from concourse.bass import DstId, RemoteDMATransfer
 from concourse.mybir import AluOpType as A, ActivationFunctionType as AF
 
 N, W, M, K, S, RO = 4, 3840, 960, 1792, 112, 4
-SEG = 2304
-NLOG = W + RO * SEG
+SEG = 4096
+L0 = 2 * W - 512
+NLOG = L0 + RO * SEG
 F32, BF, I32, U16 = "float32", "bfloat16", "int32", "uint16"
 
 
@@ -12,57 +13,71 @@ def _sb(shape, dtype):
 
 
 SCRATCH = {
-    "bt32": _sb([896], I32), "bto": _sb([896], U16), "lag32": _sb([240], I32), "ac": _sb([240], F32),
-    "a0": _sb([240], BF), "cap": _sb([240], F32), "cc": _sb([240], F32), "gl": _sb([4 * 240], F32),
-    "dG": ("dram", [3, 128, 240], F32), "dL": ("dram", [9, 128, 240], F32), "dW": ("dram", [8, W], F32),
-    "TB0": _sb([W], BF), "dig32": _sb([512], F32), "IF": _sb([128], F32), "big": _sb([128], BF), "VB": _sb([2, 64], BF), "cl32": _sb([480], F32),
-    "cf": _sb([16], F32), "GM": _sb([16], BF), "SA": _sb([48], BF), "DYN": _sb([512], BF),
-    "TB": _sb([W + 512], F32), "DEF": _sb([512], F32), "rep": _sb([2 * K], BF),
-    "ion": _sb([256], F32), "dig": _sb([512], BF),
-    "iop": _sb([128], I32), "iop2": _sb([256], I32), "iob": _sb([128], I32), "iob2": _sb([128], I32),
+    "bt32": _sb([896], I32), "bto": _sb([896], U16), "lag32": _sb([240], I32), "ac": _sb([240], F32), "a0": _sb([240], BF),
+    "cap": _sb([240], BF), "tk": _sb([240], F32), "gr": _sb([240], F32), "FL": _sb([720], BF),
+    "dW": ("dram", [8, W], F32), "EB": _sb([N, M], BF),
+    "TB0": _sb([W], BF), "TB": _sb([2 * W], F32), "LS": _sb([K + 512], F32), "DEF": _sb([512], F32), "rep": _sb([2 * K], BF),
+    "IF": _sb([128], F32), "IE": _sb([128], F32), "I2": _sb([128], F32), "big": _sb([128], BF), "zer": _sb([128], BF), "VB": _sb([192], BF),
+    "dig": _sb([512], BF), "iop": _sb([128], I32), "iop2": _sb([256], I32), "iob": _sb([128], I32),
     "BO": _sb([128], F32), "BC": _sb([8], F32), "bci": _sb([8], F32), "bct": _sb([8], F32),
-    "rowf": _sb([1], F32), "hoff": _sb([32], F32), "hcap0": _sb([32], F32), "hcap": _sb([32], F32),
-    "one": _sb([128], BF), "neg": _sb([128], BF), "IB": _sb([128], BF), "I64": _sb([128], BF), "NU": _sb([128], BF),
-    "RR": _sb([5 * 224], BF), "SB": _sb([128], BF), "SX": _sb([128], BF), "MM": _sb([1024], BF), "sgm": _sb([512], BF),
-    "PAYC": _sb([128, 16], BF), "PAY": _sb([K], F32),
-    "zz": _sb([256], F32), "am": _sb([256], I32), "sc": _sb([8, 2, 16], F32), "sel": _sb([128], F32), "best": _sb([128], F32),
-    "nd": _sb([128], F32), "nhd": _sb([128], F32), "tq": _sb([512], F32), "key": _sb([128], BF),
-    "mk": _sb([512], BF), "scn": _sb([512], BF), "t1": _sb([512], BF),
-    "nB": _sb([S], F32), "lB": _sb([S], F32), "z": _sb([S], F32), "y": _sb([S], F32), "mo": _sb([S], F32), "xo": _sb([128], F32), "xv": _sb([128], F32), "MF": _sb([512], F32),
-    "moff": _sb([S], U16), "xoff": _sb([RO * S], U16),
-    "GS": _sb([512], F32), "VT": _sb([32, 16], F32), "hv1": _sb([32], F32),
-    "nl16": _sb([RO * 32], U16), "ll16": _sb([RO * 32], U16), "HL": _sb([RO * 32], U16),
-    "LOG": _sb([NLOG], F32), "B": _sb([W + 512], F32), "H": _sb([M + 128], F32), "Bg": _sb([512], F32),
-    "PO": _sb([16, 136], F32), "PL": _sb([12, 136], F32), "AO": _sb([12 * 128], F32), "ht": _sb([512], F32),
-    "x": _sb([K], F32), "PR": _sb([K // 2], F32), "e": _sb([S], F32), "tgb": _sb([448], BF), "tgf": _sb([448], F32),
-    "cl": _sb([512], BF), "VF": _sb([512], BF), "fo": _sb([240], U16), "YO": _sb([W], F32),
+    "rowf": _sb([2], F32), "hoff": _sb([32], F32), "hcap": _sb([32], F32), "hv1": _sb([32], F32), "nl16": _sb([32], U16), "cix": _sb([S], F32), "DR": _sb([RO * S + S], BF),
+    "one": _sb([128], BF), "neg": _sb([128], BF), "IB": _sb([128], BF), "I64": _sb([128], BF), "I128": _sb([128], BF),
+    "IW": _sb([128], BF), "NU": _sb([128], BF), "RR": _sb([4 * S], BF), "SB": _sb([128], BF), "SX": _sb([96], BF),
+    "MM": _sb([512], BF), "MF": _sb([512], F32), "sgm": _sb([512], BF),
+    "PAYC": _sb([128, 16], BF), "PAY": _sb([K], F32), "DYN": _sb([768], BF),
+    "am": _sb([256], BF), "sc": _sb([128], F32), "sel": _sb([128], BF), "best": _sb([128], F32),
+    "nhd": _sb([128], BF), "tq": _sb([768], BF), "key": _sb([128], BF),
+    "mk": _sb([512], BF), "scn": _sb([512], BF), "u": _sb([512], BF), "t1": _sb([512], BF),
+    "nB": _sb([S], F32), "o1": _sb([S], F32), "o2": _sb([S], F32), "co": _sb([S], F32), "xo": _sb([128], F32), "xv": _sb([128], F32),
+    "moff": _sb([S], U16), "coff": _sb([S], U16), "xoff": _sb([RO * S], U16),
+    "VT": _sb([32, 16], F32), "n0": _sb([32], F32), "c1": _sb([32], F32), "bz": _sb([32], F32), "lb": _sb([64], F32),
+    "lb16": _sb([RO * 64], U16), "HL": _sb([RO * 32], U16),
+    "LOG": _sb([NLOG], F32), "H": _sb([M + 128], F32),
+    "PO": _sb([12, 136], F32), "PL": _sb([9, 136], F32), "AO": _sb([9 * 128], F32), "ht": _sb([512], F32),
+    "PR": _sb([K // 2], F32), "e": _sb([S], F32), "tgf": _sb([448], F32), "nmc": _sb([240], F32), "fo": _sb([240], U16),
 }
 for _b in range(8):
     SCRATCH["b%d" % _b] = ("psum", [128, 512], F32)
-NDMA = 56
-SEMAPHORES = (["cV", "cS", "cP", "cG", "ls"] + ["d%d" % i for i in range(NDMA)] + ["rG%d_%d" % (t, j) for t in range(3) for j in range(3)]
-              + ["rA%d" % t for t in range(4)] + ["rP%d_%d" % (t, j) for t in range(4) for j in range(3)])
+NDMA = 64
+SEMAPHORES = (["cV", "cS", "cP", "cG", "ls"] + ["d%d" % i for i in range(NDMA)] + ["rG%d_%d" % (t, r) for t in range(3) for r in range(N)]
+              + ["rE"] + ["rA%d" % t for t in range(1, RO)] + ["rP%d_%d" % (t, j) for t in range(1, RO) for j in range(3)])
 
-CY, CG, CS, FIX, WAKE, PECY = 0.9, 1.56, 3.8, 55.0, 70.0, 0.48
-DMA_T, REM_T = 1900.0, 2200.0
-HOME_S, NSP = True, 4
-CAND, XG, DEFE, TRIES = "SVSV", "SS", "V", 12000
 OFF, UNIT, SAT = 32, 2.0 ** -13, 20.0
 BOTH = 65 * OFF
+PRAW = 4097
+YB = 20224
+HALF = 2 * (YB + 128) + 384
+
+KS, PAYE, L1E, SMALL, PEADD = (8, 8, 8, 8), ("SVVV", "SVVV", "SVVV", "SVSS"), "VVVV", "VSSSSV", (0, 0, 0, 1)
+C1E, C2E, GBE = ("SSSS", "SSSS", "SSSS"), ("", "VVVV", "VSSS", "SSSS"), "SSV"
+XG, BGE, AOE = ("VS", "VV", "VV", "SV"), "S", "SSS"
+C1K = ((9.0, 10.4, 11.8, 13.2),) * 3
+C2K = ((), (10.7, 12.1, 13.5, 15.0), (10.7, 15.0, 16.5, 18.0), (10.0, 11.4, 12.8, 14.2))
+LISTK = (0, 16.6, 19.5, 15.7)
+DATAK = ((0, 0, (), 0, 14.0, 16.5, 15.0, 17.0, (18.0, 19.5, 20.1, 21.0)),
+         (18.5, 19.2, (21.5, 24.9, 26.2), 26.6, 36.2, 37.5, 38.9, 38.7, (40.5, 41.4, 42.3, 44.2)),
+         (22.0, 23.0, (26.55, 27.75, 28.55), 29.0, 34.2, 35.5, 36.9, 36.9, (38.0, 38.9, 39.75, 39.9)),
+         (19.0, 21.0, (23.0, 23.8, 24.6), 25.0, 29.0, 29.5, 30.5, 31.0, (32.0, 32.5, 33.0, 33.5)))
+FIX, WAKE = 55.0, 60.0
+PACES = ((0.9, 1.5, 3.4, 0.48, 1.9, 4.5, 1600.0, 2100.0), (0.83, 1.2, 2.0, 0.42, 3.0, 9.0, 1800.0, 2400.0), (1.1, 1.9, 5.5, 0.55, 2.3, 6.0, 1800.0, 2400.0))
+EARLY, PASSES, LATE = 0.2, 3000, (0.0, 3.0, 6.0, 12.0, 24.0, 48.0)
+MOVES, HEAT, WEIGHT, SEED = 25000, 60.0, (0.4, 0.3, 0.3), 12
 PLAN = {}
-SEED = 5
-LEAD, HEAT = 100.0, 200.0
 
 
-def build(g, T, topo, rank):
-    ops = []; now = ["s", 0]
+def build(g, T, topo, rank, pace):
+    CY, CG, CS, PECY, LKB, RKB, DMA_T, REM_T = pace
+    ops = []; now = ["s", None]
     V, SC, PE = g.vector, g.scalar, g.tensor
     me = T.cores[rank]
+
+    def at(k):
+        now[1] = k
 
     def op(eng, fn, r, w, cost, banks=(), lat=0.0, kind="c", **kw):
         d = {"eng": eng, "fn": fn, "r": list(r), "w": list(w), "cost": cost, "banks": list(banks), "lat": lat, "kind": kind}
         d.update(kw)
-        d["stage"] = now[1]
+        d["turn"] = now[1]
         d["tag"] = now[0] + str(eng) + "".join(ch for ch in (list(w) or list(r))[-1] if not ch.isdigit())
         ops.append(d)
         return len(ops) - 1
@@ -90,11 +105,17 @@ def build(g, T, topo, rank):
             kw["scale"] = scale
         op("S", lambda: SC.activation(out, a, f, **kw), r, w, FIX + extra + CY * max(cyc, 64), banks)
 
-    def cp(eng, out, a, r, w, cyc):
+    def cp(eng, out, a, r, w, cyc, banks=()):
         if eng == "V":
-            vcp(out, a, r, w, cyc)
+            vcp(out, a, r, w, cyc, banks)
         else:
-            act(out, a, r, w, cyc)
+            act(out, a, r, w, cyc, banks)
+
+    def shifted(eng, out, a, c, r, w, cyc, banks):
+        if eng == "V":
+            vts(out, a, float(c), None, A.add, None, r, w, cyc, banks)
+        else:
+            act(out, a, r, w, cyc, banks, f=AF.Copy, bias=float(c))
 
     def mm(lst, r, w, cyc, banks):
         def fn():
@@ -107,9 +128,9 @@ def build(g, T, topo, rank):
     def grp(o, prs):
         return [(o, l, rh, i == 0, i == len(prs) - 1) for i, (l, rh) in enumerate(prs)]
 
-    def dma(q, out, a, r, w, extra=0.0):
+    def dma(q, out, a, r, w, kb, behind=()):
         e = {"Y": g.sync, "S": g.scalar, "G": g}[q]
-        op(q, lambda: e.dma_start(out, a), r, w, 1000.0 if q == "G" else 100.0, lat=DMA_T + extra, kind="dma")
+        return op(q, lambda: e.dma_start(out, a), r, w, 1000.0 if q == "G" else 80.0, lat=DMA_T, kind="dma", move=LKB * kb, behind=behind)
 
     def iota(out, pat, base, cm, w, n, flag=False):
         if flag:
@@ -117,8 +138,11 @@ def build(g, T, topo, rank):
         else:
             op("G", lambda: g.iota(out, pat, base, cm), [], w, 130 + 2 * CY * n)
 
-    def asel(out, a, pat, cmp, base, cm, r, w, n):
-        op("G", lambda: g.affine_select(out, a, pat, cmp, 0.0, base, cm), r, w, 170 + 2 * CY * n)
+    def asel(out, a, pat, cmp, base, cm, r, w, n, fill=0.0):
+        op("G", lambda: g.affine_select(out, a, pat, cmp, fill, base, cm), r, w, 170 + 2 * CY * n)
+
+    def diag(out, n, c, w):
+        asel(out, T.zer[:, 0:n], [[-1, n]], A.not_equal, 0, 1, ["zer"], w, n, float(c))
 
     peers = [(rank + j) % N for j in range(1, N)]
 
@@ -129,377 +153,519 @@ def build(g, T, topo, rank):
         a = topo.addr(T.cores[r])
         return DstId(rid=a[0], pnc=a[1])
 
-    def mask_of(es):
-        return sum(1 << e for e in es)
-
     def send1(r, out, a, sem, rd, wr=()):
         ad = topo.addr(T.cores[r]); mk = topo.mask(me, T.cores[r]); n = len(topo.engines(me, T.cores[r]))
-        return op("G", lambda: g.remote_dma(out, a, T.sem[sem], T.sem.ls, ad[1], ad[0], mk), rd, wr, 500.0, kind="rem", ls=n), n
+        return op("G", lambda: g.remote_dma(out, a, T.sem[sem], T.sem.ls, ad[1], ad[0], mk), rd, wr, 500.0, kind="rem", ls=n,
+                  lat=REM_T, move=RKB * 68), n
 
-    def recv(sem, cnt, after, w, lat):
-        op(None, None, [], w, 0.0, kind="recv", sem=sem, cnt=cnt, after=after, lat=lat)
+    def send_all(outs, a, sem, rd, kb, first=0.0):
+        es = [e for e in topo.engines(me, T.cores[peers[0]]) if all(e in topo.engines(me, T.cores[r]) for r in peers)]
+        tr = RemoteDMATransfer(dst_ids=[dst_id(r) for r in peers], dma_engine_mask=sum(1 << e for e in es), remote_sem=T.sem[sem],
+                               src=a, dsts=outs)
+        return op("G", lambda: g.remote_dma_fused([tr], local_sem=T.sem.ls), rd, [], 500.0 + first, kind="rem", ls=len(es),
+                  lat=REM_T, move=RKB * 3 * kb), len(es)
 
-    TB, LOG, PAYC, x = T.TB, T.LOG, T.PAYC, T.x
+    def recv(sem, cnt, after, w):
+        op(None, None, [], w, 0.0, kind="recv", sem=sem, cnt=cnt, after=after)
+
+    TB, LOG, PAYC, LS = T.TB, T.LOG, T.PAYC, T.LS
     b0, b1, b2, b3, b4, b5, b6, b7 = [T["b%d" % i] for i in range(8)]
-    TBN = ["TBw", "TBa", "TB2", "TB3", "TB4", "TB5", "TBo", "TBc", "TBg", "TBf0", "TBf1", "TBf2"]
-    RG = (9, 13, 14)
+    TB1 = ["TBw", "TBa", "TBp", "TBq", "TBn", "TBm", "TBo"]; TB2 = ["TCp", "TCg"]
 
     def prow(r):
         return PAYC[0:S, r::16, :]
 
-    dma("Y", T.lag32[:], T.lag[:], [], ["lag32"])
-    dma("Y", T.bt32[:], T.bt[:], [], ["bt32"], 600.0)
-    dma("Y", T.tgb[0:16, :], T.tg[:], [], ["tgb"])
+    dma("Y", T.lag32[:], T.lag[:], [], ["lag32"], 120)
+    dma("S", T.bt32[:, 0:224], T.bt[:, 0:224], [], ["bt32"], 112)
+    dma("Y", T.EB[:, rank], T.e0[:, rank * M:(rank + 1) * M], [], ["EBo"], 240)
     T0 = T.TB0; T0N = ["T0w", "T0a", "T04", "T05", "T0o"]
+    ZS = ["PR0", "PR1", "PR2"]
+    at(-5.0)
+    vms(T.PR[:, 0:480], 0.0, ZS, 480)
+    for c in range(8):
+        at(-4.0 + 0.5 * c if c < 4 else 2.7 + 0.5 * c)
+        act(TB[:, 480 * c:480 * c + 480], T.PR[:, 0:480], ZS, ["TBz%d" % c], 480, f=AF.Tanh, extra=1300.0 * (c == 0))
+    at(None)
     vms(T0[:], 0.0, T0N, W // 2)
     iota(T.iop2[:, 2:3], [[0, 1]], 0, 1, ["iop2b"], 1)
+    iota(T.ht[:, 0:256], [[1, 4], [0, 64]], OFF, 4, ["ht0", "ht1"], 256, True)
     iota(T.dig[:, 256:512], [[0, 4], [1, 64]], OFF, 0, ["digl"], 256, True)
-    iota(T.ion[:], [[1, 4], [0, 64]], OFF, 4, ["ion"], 256, True)
     iota(T.iob[:], [[1, 128]], 128, -1, ["iob"], 128)
     vms(T.one[:], 1.0, ["one"], 64)
     vms(T.neg[:], -1.0, ["neg"], 64)
+    vms(T.zer[:], 0.0, ["zer"], 64)
     asel(T.SB[:], T.one[:], [[-1, 16], [-16, 8]], A.is_equal, 0, 1, ["one"], ["SB"], 128)
-    vts(T.iob2[:], T.iob[:], 15, None, A.bitwise_and, None, ["iob"], ["iob2"], 128)
-    vts(T.BO[:], T.iob2[:], 0.0, None, A.is_equal, None, ["iob2"], ["BO"], 128)
-    vts(T.iop2[:, 4:5], T.iop2[:, 2:3], 15, None, A.bitwise_and, None, ["iop2b"], ["iop2c"], 1)
-    vcp(T.rowf[:], T.iop2[:, 4:5], ["iop2c"], ["rowf"], 1)
     vts(T.iop2[:, 0:1], T.iop2[:, 2:3], 1.0 / 15.0, -7.0 / 15.0, A.mult, A.add, ["iop2b"], ["iop2a"], 1)
-    vts(T.bct[:, 0:1], T.iop2[:, 0:1], -60.0, None, A.mult, None, ["iop2a"], ["bct0"], 1)
-    vts(T.dig[:, 0:256], T.ion[:], T.bct[:, 0:1], None, A.add, None, ["ion", "bct0"], ["digh"], 256)
+    vts(T.bct[:, 0:1], T.iop2[:, 0:1], -60.0 * UNIT, None, A.mult, None, ["iop2a"], ["bct0"], 1)
+    act(T.dig[:, 0:256], T.ht[:, 0:256], ["ht0", "ht1", "bct0"], ["digh"], 256, bias=T.bct[:, 0:1], scale=UNIT)
+    act(T.dig[:, 256:512], T.dig[:, 256:512], ["digl"], ["digl"], 256, scale=UNIT)
     vcp(T.a0[:], T.lag32[:], ["lag32"], ["a0"], 240)
-    act(T.ac[:], T.a0[:], ["a0"], ["ac"], 240)
-    dma("Y", T0[0::16, :], T.wt[:], [], ["T0w"], 300.0)
-    dma("S", T0[1::16, :], T.a0[:], ["a0"], ["T0a"], 300.0)
-    dma("Y", T0[4::16, :], T.dig[0:120, 0:256], ["digh"], ["T04"], 600.0)
-    dma("S", T0[5::16, :], T.dig[0:120, 256:512], ["digl"], ["T05"], 600.0)
-    act(T.dig32[:], T.dig[:], ["digh", "digl"], ["dig32"], 512, scale=UNIT)
-    for c in range(4):
-        act(TB[:, M * c:M * c + M], T0[:, M * c:M * c + M], T0N, TBN, M, scale=UNIT, f=AF.Tanh, extra=1300.0 * (c == 0))
+    early = [dma("Y", T0[0::16, :], T.wt[:], [], ["T0w"], 60), dma("Y", T0[1::16, :], T.a0[:], ["a0"], ["T0a"], 80),
+             dma("Y", T0[4::16, :], T.dig[0:120, 0:256], ["digh"], ["T04"], 80), dma("Y", T0[5::16, :], T.dig[0:120, 256:512], ["digl"], ["T05"], 80)]
     vcp(T.bto[:, 0:224], T.bt32[:, 0:224], ["bt32"], ["bto0"], 224)
-    vcp(T.bto[:, 224:896], T.bt32[:, 224:896], ["bt32"], ["bto1", "bto2", "bto3"], 672)
-    asel(T.IB[:], T.one[:], [[-1, 128]], A.is_equal, 0, 1, ["one"], ["IB"], 128)
+    act(T.ac[:], T.a0[:], ["a0"], ["ac"], 240)
+    vts(T.iop2[:, 128:256], T.iob[:], 15, None, A.bitwise_and, None, ["iob"], ["iopd"], 128)
+    vts(T.BO[:], T.iop2[:, 128:256], 0.0, None, A.is_equal, None, ["iopd"], ["BO"], 128)
+    vts(T.iop2[:, 4:5], T.iop2[:, 2:3], 15, None, A.bitwise_and, None, ["iop2b"], ["iop2c"], 1)
+    vcp(T.rowf[:, 0:1], T.iop2[:, 4:5], ["iop2c"], ["rowf"], 1)
+    diag(T.IB[:], 128, 1, ["IB"])
     asel(T.NU[:], T.neg[:], [[-1, 128]], A.is_gt, 0, 1, ["neg"], ["NU"], 128)
-    asel(T.IF[:], T.BO[:], [[-1, 128]], A.is_equal, 0, 1, ["BO"], ["IF"], 128)
-    act(T.SX[:, 0:32], T.SB[:, 16:48], ["SB"], ["SXa"], 32, scale=-1.0 / UNIT)
-    act(T.SX[:, 96:128], T.SB[:, 16:48], ["SB"], ["SXd"], 32, scale=1.0 / UNIT)
-    for j in range(2):
-        act(T.SX[:, 32 + 16 * j:48 + 16 * j], T.SB[:, 32:48], ["SB"], ["SXb%d" % j], 16)
-        act(T.SX[:, 64 + 16 * j:80 + 16 * j], T.SB[:, 32:48], ["SB"], ["SXc%d" % j], 16, scale=-1.0)
-    act(T.I64[:], T.IB[:], ["IB"], ["I64"], 128, scale=64.0)
-    for h in range(5):
-        act(T.RR[:, 224 * h:224 * h + S], T.IB[:, 0:S], ["IB"], ["RR%da" % h], S, scale=-200.0 if h < 4 else 1.0)
-        act(T.RR[:, 224 * h + S:224 * h + 224], T.IB[:, 0:S], ["IB"], ["RR%db" % h], S, scale=128.0 * h if h < 4 else 1.0)
-    RRS = ["RR%d%s" % (h, s) for h in range(5) for s in "ab"]
+    asel(T.NU[:], T.NU[:], [[-1, 128]], A.not_equal, 0, 1, ["NU"], ["NU"], 128, -256.0)
+    act(T.IF[:], T.IB[:], ["IB"], ["IF"], 128)
+    act(T.IE[:], T.IB[:], ["IB"], ["IE"], 128, scale=1.0 / 32.0)
+    act(T.I2[:], T.IB[:], ["IB"], ["I2"], 128, scale=2.0)
+    act(T.SX[:, 0:32], T.SB[:, 16:48], ["SB"], ["SXa"], 32, scale=1.0 / UNIT)
+    act(T.SX[:, 32:64], T.SB[:, 16:48], ["SB"], ["SXb"], 32, scale=-1.0 / UNIT)
+    act(T.SX[:, 64:80], T.SB[:, 64:80], ["SB"], ["SXc"], 16, scale=1.0 / UNIT)
+    act(T.SX[:, 80:96], T.SB[:, 64:80], ["SB"], ["SXd"], 16, scale=-1.0 / UNIT)
+    diag(T.I64[:], 128, 64, ["I64"])
+    diag(T.IW[:], 128, W // 2, ["IW"])
+    diag(T.I128[:], 128, 128, ["I128"])
+    for h in range(4):
+        diag(T.RR[:, S * h:S * h + S], S, (YB + 128 + 128 * h) // 2, ["RR%d" % h])
+    RRS = ["RR%d" % h for h in range(4)]
+    iota(T.DR[0:1, 0:RO * S], [[-SEG, RO], [0, S]], 0, 0, ["DR"], RO * S, True)
+    vms(T.DR[0:1, RO * S:RO * S + S], float(YB + 1 - L0 - PRAW - HALF), ["DR2"], 64)
     vms(T.sgm[:], 1.0, ["sgm"], 256)
     vms(T.sgm[:, 0::16], 0.0, ["sgm"], 32)
-    vms(PAYC[:], 0.0, ["pc2", "pc3", "pc4", "pc5", "pc10", "pc11"], 1024)
-    iota(T.iop[:], [[0, 8], [S, 16]], W + 512, 1, ["iop"], 128)
-    vts(T.iop2[:, 128:256], T.iop[:], 6, None, A.arith_shift_right, None, ["iop"], ["iopd"], 128)
+    PCS = ["pc%d" % r for r in range(2, 10)]
+    vms(PAYC[:], 0.0, PCS, 1024)
+    iota(T.iop[:], [[0, 8], [S, 16]], L0 + 512 + K + PRAW - 129 * OFF, 1, ["iop"], 128)
+    vts(T.iop2[:, 128:256], T.iop[:], 7, None, A.arith_shift_right, None, ["iop"], ["iopd"], 128)
     vts(prow(2), T.iop2[0:S, 128:256], float(OFF), None, A.add, None, ["iopd"], ["pc2"], 128)
-    vts(T.iop2[:, 128:256], T.iop[:], 63, None, A.bitwise_and, None, ["iop"], ["iopd"], 128)
+    vts(T.iop2[:, 128:256], T.iop[:], 127, None, A.bitwise_and, None, ["iop"], ["iopd"], 128)
     vts(prow(3), T.iop2[0:S, 128:256], float(OFF), None, A.add, None, ["iopd"], ["pc3"], 128)
-    iota(T.bci[:, 0:4], [[SEG // 64, 4]], 0, 0, ["bci"], 4, True)
+    iota(T.bci[:, 0:4], [[SEG // 128, 4]], 0, 0, ["bci"], 4, True)
     vts(T.bct[:, 4:8], T.bci[:, 0:4], T.BO[:, 2:3], UNIT, A.mult, A.mult, ["bci", "BO"], ["bct1"], 4)
-    act(T.bci[:, 4:8], T.BO[:, 6:10], ["BO"], ["bci2"], 4, scale=SAT)
+    act(T.bci[:, 4:8], T.BO[:, 10:14], ["BO"], ["bci2"], 4, scale=SAT)
     vtt(T.BC[:, 0:4], T.bci[:, 4:8], T.bct[:, 4:8], A.add, ["bci2", "bct1"], ["BC"], 8)
-    vcp(T.cf[:, 0:1], T.BO[:, 9:10], ["BO"], ["cf0"], 1)
-    vcp(T.cf[:, 1:3], T.BO[:, 13:15], ["BO"], ["cf1"], 2)
-    vtt(T.bct[:, 1:4], T.BO[:, 6:9], T.cf[:, 0:3], A.add, ["BO", "cf0", "cf1"], ["bct2"], 8)
-    act(T.BC[:, 5:8], T.bct[:, 1:4], ["bct2"], ["BC5"], 4, scale=SAT)
-    vtt(T.cf[:, 4:6], T.BO[:, 10:12], T.BO[:, 1:13:11], A.add, ["BO"], ["cf4"], 8)
-    vtt(T.cf[:, 6:7], T.cf[:, 4:5], T.cf[:, 5:6], A.add, ["cf4"], ["cf6"], 8)
-    vts(T.cf[:, 8:11], T.BO[:, 6:9], 2.0, T.cf[:, 6:7], A.mult, A.add, ["BO", "cf6"], ["cf8"], 8)
-    vts(T.cf[:, 12:15], T.cf[:, 0:3], -100.0, None, A.mult, None, ["cf0", "cf1"], ["cf12"], 8)
-    vtt(T.cf[:, 8:11], T.cf[:, 8:11], T.cf[:, 12:15], A.add, ["cf8", "cf12"], ["cf8"], 8)
-    asel(T.GM[:, 8:16], T.one[:, 0:8], [[-16, 8]], A.is_ge, 0, 1, ["one"], ["GM0"], 8)
-    asel(T.GM[:, 0:8], T.GM[:, 8:16], [[16, 8]], A.is_ge, 15, -1, ["GM0"], ["GM"], 8)
-    for t in range(3):
-        act(T.SA[:, 16 * t:16 * t + 8], T.SB[:, 0:8], ["SB"], ["SA%da" % t], 8)
-        act(T.SA[:, 16 * t + 8:16 * t + 16], T.GM[:, 0:8], ["GM", "cf8"], ["SA%db" % t], 8, scale=T.cf[:, 8 + t:9 + t])
-    vtt(T.cf[:, 3:4], T.BO[:, 10:11], T.BO[:, 11:12], A.add, ["BO"], ["cf3"], 2)
-    act(T.cf[:, 7:8], T.BO[:, 4:5], ["BO"], ["cf7"], 1, scale=UNIT * (W // 64))
-    vts(T.BC[:, 4:5], T.cf[:, 3:4], UNIT * OFF, T.cf[:, 7:8], A.mult, A.add, ["cf3", "cf7"], ["BC4"], 1)
-    act(T.DEF[:], T0[:, 0:512], T0N + ["BC4"], ["DEF"], 512, bias=T.BC[:, 4:5], scale=UNIT)
+    act(T.BC[:, 4:5], T.BO[:, 4:5], ["BO"], ["BC4"], 1, scale=UNIT * (W // 64))
+    iota(T.hcap[:], [[0, 4], [16, 8]], M, 0, ["hcap"], 32, True)
+    vts(T.hcap[:], T.hcap[:], T.rowf[:, 0:1], None, A.add, None, ["hcap", "rowf"], ["hcap"], 32)
     vms(T.big[:], 1.0 / UNIT, ["big"], 64)
+    for c, v, nm in ((5, -127.5, "c128"), (6, 4.0e6, "c4"), (7, 130.0 - (7.0 + OFF) / 15.0, "c130")):
+        vms(T.BC[:, c:c + 1], v, [nm], 1)
     iota(T.hoff[:], [[M, 4], [0, 8]], BOTH, 0, ["hoff"], 32, True)
-    iota(T.hcap0[:], [[0, 4], [16, 8]], M, 0, ["hcap0"], 32, True)
-    vts(T.hcap[:], T.hcap0[:], T.rowf[:], None, A.add, None, ["hcap0", "rowf"], ["hcap"], 32)
+    iota(T.cix[:], [[16, S]], YB + 1 - K - HALF, 0, ["cix"], S, True)
+    vts(T.cix[:], T.cix[:], T.rowf[:, 0:1], None, A.add, None, ["cix", "rowf"], ["cix"], S)
     for xh in range(2):
         for e in range(2):
             c = 128 * (2 * xh + e)
             asel(T.MM[:, c:c + 128], T.big[:], [[-32, 4], [1000 - 16, 2], [-1, 16]], A.is_equal, 16 * (e - xh) - 1000 * e, 1,
                  ["big"], ["MM%d" % (2 * xh + e)], 128)
-    act(T.MM[:, 512:1024], T.MM[:, 0:512], ["MM0", "MM1", "MM2", "MM3"], ["MM4"], 512, scale=64.0)
-    act(T.MF[:], T.MM[:, 0:512], ["MM0", "MM1", "MM2", "MM3"], ["MF"], 512, scale=UNIT)
+    MM1 = ["MM0", "MM1", "MM2", "MM3"]
     vms(T.xo[:, S:128], 0.0, ["xop"], 16)
-    MMS = ["MM0", "MM1", "MM2", "MM3", "MM4"]
-    vts(T.tgf[0:16, :], T.tgb[0:16, :], -128.0, None, A.mult, None, ["tgb"], ["tgf"], 448)
     vms(T.H[:, M:M + 128], 0.0, ["Hd"], 128)
-    vms(T.B[:, W:W + 512], 0.0, ["Bd"], 512)
-    vms(T.cl[:, 240:256], 0.0, ["clp0"], 16)
-    vms(T.cl[:, 496:512], 0.0, ["clp1"], 16)
-    dma("G", T.H[:, 0:M], T.e0[:, rank * M:(rank + 1) * M], ["gate"], ["H"], 2000.0)
-    dma("G", LOG[:, 0:W // 2], T.e0[:, 0:W // 2], ["gate"], ["L0a"], 4000.0)
-    dma("Y", TB[2::16, 0:W], T.dig32[0:120, 0:256], ["dig32", "L0a"], ["TB2", "row2"], 300.0)
-    dma("Y", TB[3::16, 0:W], T.dig32[0:120, 256:512], ["dig32", "L0a"], ["TB3", "row3"], 600.0)
-    dma("G", LOG[:, W // 2:W], T.e0[:, W // 2:W], ["row2", "row3"], ["L0"], 4000.0)
-    dma("G", T.dW[:], T.wt[:], ["gate"], ["dW"], 500.0)
-    vcp(T.B[:, 0:W // 2], LOG[:, 0:W // 2], ["L0a"], ["Ba"], W // 2)
-    vcp(T.B[:, W // 2:W], LOG[:, W // 2:W], ["L0"], ["Bb"], W // 2)
-    keep = ops[-8:]
-    for o in keep:
-        ops.remove(o)
+    iota(T.nmc[:], [[1, 240]], PRAW, 0, ["nmc"], 240, True)
+    act(T.rowf[:, 1:2], T.rowf[:, 0:1], ["rowf"], ["rowu"], 1, scale=240.0 * UNIT)
+    act(T.nmc[:], T.nmc[:], ["nmc", "rowu"], ["nmc"], 240, bias=T.rowf[:, 1:2], scale=UNIT)
+    DEFS = ["DEF"]
 
-    def logres(t, ans):
-        r = ["L0", "L0a"]
+    def mm_big(k, c):
+        return T.EB[:, peers[k], c:c + 128]
+
+    def loads():
+        at(1.0)
+        d = dma("Y", TB[2::8, W:2 * W], T.PR[:, 0:480], ZS + ["bto0"], ["TCp", "TCg"], 240, early)
+        d = dma("Y", TB[12::16, W:2 * W], T.PR[:, 0:240], ZS, ["TCg2"], 120, [d])
+        dma("Y", TB[3::8, W:2 * W], T.PR[:, 0:480], ZS, ["TCp2", "zr"], 240, [d])
+        dma("Y", T.bt32[:, 224:896], T.bt[:, 224:896], ["gate0"], ["bt32b"], 336)
+        dma("Y", T.t1[0:16, 0:448], T.tg[:], ["gate0"], ["t1"], 14)
+        at(2.0)
+        s0, n0 = send_all([T.EB[:, rank] for r in peers], T.EB[:, rank], "rE", ["EBo", "IW", "I64", "NU", "zr"], 240, 2500.0)
+        recv("rE", 3 * n0, [s0], ["EBr"])
+        dma("G", LOG[:, 0:W], T.e0[:], ["zr"], ["L0"], 1920)
+        dma("G", T.dW[:], T.wt[:], ["zr"], ["dW"], 120)
+        at(5.0)
+        act(LS[:, 0:512], T.dig[:], ["digh", "digl"], ["LS"], 512)
+        at(14.8)
+        act(T.DEF[:], T0[:, 0:512], T0N + ["BC4"], DEFS, 512, bias=T.BC[:, 4:5])
+        at(9.6)
+        vts(T.MF[:], T.MM[:, 0:512], UNIT, None, A.mult, None, MM1, ["MF"], 512)
+        at(10.5)
+        vcp(T.bto[:, 224:896], T.bt32[:, 224:896], ["bt32b"], ["bto1", "bto2", "bto3"], 672)
+        vts(T.tgf[0:16, :], T.t1[0:16, 0:448], -128.0, None, A.mult, None, ["t1"], ["tgf"], 448)
+        for h in range(N):
+            cp(L1E[h], LOG[:, W + M * h:W + M * h + M], T.EB[:, h], ["EBo", "EBr"], ["L1%d" % h], M)
+        at(17.5)
+        act(T.H[:, 0:M], T.EB[:, rank], ["EBo"], ["H"], M)
+        act(T.EB[:, peers[0], 0:512], T.MM[:], MM1, ["EBr", "MM4"], 512, scale=64.0)
+        act(T.EB[:, peers[1], 0:512], T.MM[:], MM1, ["EBr", "MM5"], 512, scale=128.0)
+
+    def logres(t, ans, stepped=True):
+        r = ["L0"] + ["L1%d" % h for h in range(N)]
         for u in range(t):
-            r += ["A%d_%s" % (u, h) for h in ("o", "r")] + ["X%d_%d" % (u, c) for c in range(4)]
-        if ans:
+            r += (["A%d_%s" % (u, h) for h in ("o", "r") if u] + ["X%d_%d" % (u, c) for c in range(4) if stepped or u < t - 1]
+                  + ["x%d_%d" % (u, c) for c in range(5)])
+        if ans and t:
             r += ["A%d_o" % t, "A%d_r" % t]
         return r
 
+    later = []
+
     def control(t):
-        for s in range(2):
-            for hf in range(2):
-                for u, (k0, k1) in enumerate(((0, 6), (6, 8)) if s else ((0, 8),)):
-                    c = 224 * t + S * s + 56 * hf + 7 * k0; o = K * s + 896 * hf + S * k0; nk = k1 - k0
-                    cp(CAND[2 * s + hf], T.rep[:, o:o + S * nk], (TB if t else T0)[:, 0:W].indirect(T.bto[:, c:c + 7 * nk]),
-                       (TBN if t else T0N) + ["bto%d" % t], ["rep%d%d" % (s + u, hf)] + (["gate"] if (t, s, hf) == (0, 0, 0) else []), CG * S * nk)
+        last = t == RO - 1; a = 24.0 * t
+        pieces = [(s, hf, u, k0, k1) for s in range(2) for hf, (lo, hi) in enumerate(((0, KS[t]), (KS[t], 16)))
+                  for u, (k0, k1) in enumerate(((lo, hi - 2), (hi - 2, hi)) if s else ((lo, hi),))]
+        for s, hf, u, k0, k1 in pieces:
+            c = 224 * t + S * s + 7 * k0; o = K * s + S * k0; nk = k1 - k0
+            at(a + (0.0, 1.3, 2.3)[s + u])
+            cp("SV"[hf], T.rep[:, o:o + S * nk], (TB if t else T0)[:, 0:W].indirect(T.bto[:, c:c + 7 * nk]),
+               (TB1 if t else T0N) + ["bto%d" % t], ["rep%d%d" % (s + u, hf)] + (["gate%d" % t] if (s, hf) == (0, 0) else []), CG * S * nk)
         if t == 0:
-            ops.extend(keep)
+            loads()
+        else:
+            at(a + 1.0)
+            if last:
+                dma("Y", TB[:, W + 512:W + 1024], T.DEF[:], DEFS + ["gate%d" % t], TB2 + ["LS"], 256)
+            else:
+                dma("Y", LS[:, K:K + 512], T.DEF[:], DEFS + ["gate%d" % t], ["LS"], 256)
 
         def ch(s, k):
             return T.rep[:, K * s + S * k:K * s + S * k + S]
-        for s in range(2):
-            for hf in range(2):
-                sa = T.SB[:, 0:16] if t == 0 else T.SA[:, 16 * t - 16:16 * t]
-                for u, (k0, k1) in enumerate(((0, 6), (6, 8)) if s else ((0, 8),)):
-                    mm([(b0[0:S, 16 * s + k::32], ch(s, k), sa, True, True) for k in range(8 * hf + k0, 8 * hf + k1)],
-                       ["rep%d%d" % (s + u, hf), "SB"] + ([] if t == 0 else ["SA%da" % (t - 1), "SA%db" % (t - 1)]), ["F0_%d%d" % (s + u, hf)], 64 * (k1 - k0), [0])
+        for s, hf, u, k0, k1 in pieces:
+            at(a + (1.3, 2.3, 2.5)[s + u])
+            mm([(b0[0:S, 256 * s + k:256 * s + 256:16], ch(s, k), T.SB[:, 0:16], True, True) for k in range(k0, k1)],
+               ["rep%d%d" % (s + u, hf), "SB"], ["F0_%d%d" % (s + u, hf)], 64 * (k1 - k0), [0])
         F0 = ["F0_00", "F0_01", "F0_10", "F0_11", "F0_20", "F0_21"]
-        sp, sn = (T.SX[:, 32:64], T.SX[:, 64:96]) if t == 0 else (T.SX[:, 96:128], T.SX[:, 0:32])
-        SXS = ["SXd", "SXa", "SXb0", "SXb1", "SXc0", "SXc1"]
-        REP = ["rep00", "rep01", "rep10", "rep11", "rep20", "rep21"]
+        REP0 = ["rep00", "rep01"]; REP = REP0 + ["rep10", "rep11", "rep20", "rep21"]
+        at(a + 1.4)
+        mm([(b1[0:S, k::16], ch(0, k), T.SX[:, 0:32], True, True) for k in range(16)], REP0 + ["SXa"], ["F1"], 1024, [1])
+        at(a + 2.6)
         lst = []
         for k in range(16):
-            lst += grp(b2[0:S, k::16], [(ch(1, k), sp), (ch(0, k), sn)])
-        mm(lst, REP + SXS, ["F2"], 2048, [2])
-        mm([(b1[0:S, k::16], ch(0, k), sp, True, True) for k in range(16)], REP + SXS, ["F1"], 1024, [1])
-        if t == 0:
-            vcp(T.am[0:S, :], b0[0:S, 256:512], F0, ["am"], 256, [0])
+            lst += grp(b2[0:S, k::16], [(ch(1, k), T.SX[:, 0:32]), (ch(0, k), T.SX[:, 32:64])])
+        mm(lst, REP + ["SXa", "SXb"], ["F2"], 2048, [2])
+        if t > 0:
+            at(a + 2.65)
+            mm([(b3[0:S, k:256:16], ch(0, k), T.SX[:, 64:80], True, True) for k in range(16)], REP0 + ["SXc"], ["G1", "Tn", "Tp"], 1024, [3])
+            at(a + 2.7)
+            lst = []
+            for k in range(16):
+                lst += grp(b3[0:S, 256 + k:512:16], [(ch(1, k), T.SX[:, 64:80]), (ch(0, k), T.SX[:, 80:96])])
+            mm(lst, REP + ["SXc", "SXd"], ["G2", "Tp"], 2048, [3])
+        at(a + 2.6)
+        cp(SMALL[0], T.am[0:S, :], b0[0:S, 128:384], F0, ["am"], 256, [0])
+        vtt(T.sc[0:S, :], b0[0:S, 0:128], T.am[0:S, 0:128], A.mult, F0 + ["am"], ["sc"], 128, [0])
+        vtt(b0[0:S, 384:512], b0[0:S, 384:512], T.am[0:S, 128:256], A.mult, F0 + ["am"], ["sc1"], 128, [0])
+        vtt(T.best[0:S, :], b0[0:S, 384:512], T.sc[0:S, :], A.max, ["sc", "sc1"], ["best"], 128, [0])
+        vtt(T.sel[0:S, :], b0[0:S, 384:512], T.sc[0:S, :], A.is_gt, ["sc", "sc1"], ["sel"], 128, [0])
+        at(a + 3.6)
+        if SMALL[1] == "V":
+            vts(b0[0:S, 0:128], T.best[0:S, :], 4.0, -1000.0, A.is_lt, A.mult, ["best", "sc"], ["nd"], 128, [0])
         else:
-            vts(T.zz[0:S, :], b0[0:S, 256:512], -1.0, 2.0, A.mult, A.min, F0, ["zz"], 256, [0])
-            vtt(T.am[0:S, :], b0[0:S, 256:512], T.zz[0:S, :], A.max, F0 + ["zz"], ["am"], 256, [0])
-        vtt(T.sc[0:S], b0[0:S, 0:256], T.am[0:S, :], A.mult, F0 + ["am"], ["sc"], 256, [0])
-        vtt(T.sel[0:S, :], T.sc[0:S, :, 1, :], T.sc[0:S, :, 0, :], A.is_gt, ["sc"], ["sel"], 256)
-        vtt(T.best[0:S, :], T.sc[0:S, :, 1, :], T.sc[0:S, :, 0, :], A.max, ["sc"], ["best"], 256)
-        vts(T.nd[0:S, :], T.best[0:S, :], 4.0, -1000.0, A.is_lt, A.mult, ["best"], ["nd"], 128)
-        for q in (2, 3, 0, 1):
-            vtt(T.tq[0:S, 128 * q:128 * q + 128], b2[0:S, 128 * q:128 * q + 128], T.sel[0:S, :], A.mult, ["F2", "sel"], ["tq%d" % q], 128, [2])
-        for q, r in ((2, 4), (3, 5), (0, 10), (1, 11)):
-            vtt(prow(r), b1[0:S, 128 * q:128 * q + 128], T.tq[0:S, 128 * q:128 * q + 128], A.add, ["F1", "tq%d" % q], ["pc%d" % r], 128, [1])
+            act(b0[0:S, 0:128], T.best[0:S, :], ["best", "sc", "c4"], ["nd"], 128, [0], f=AF.Relu, scale=-1.0e6, bias=T.BC[0:S, 6:7])
+        picks = [(2, 4, 3.7, 3.8, 4.2), (3, 5, 3.9, 5.3, 5.4)]
+        if t:
+            picks += [(0, 6, 4.0, 5.5, 15.2), (1, 7, 4.1, 5.6, 15.2), (4, 8, 5.4, 5.8, 15.2), (5, 9, 5.7, 5.9, 15.2)]
+        for q, r, k1, k2, k3 in picks:
+            c = 128 * (q % 4); at(a + k1)
+            vtt(T.tq[0:S, 128 * q:128 * q + 128], b2[0:S, c:c + 128] if q < 4 else b3[0:S, 256 + c:384 + c], T.sel[0:S, :], A.mult,
+                ["F2" if q < 4 else "G2", "sel"], ["tq%d" % q], 128, [2 if q < 4 else 3])
+        for q, r, k1, k2, k3 in picks:
+            c = 128 * (q % 4); at(a + k2)
+            vtt(prow(r), (b1 if q < 4 else b3)[0:S, c:c + 128], T.tq[0:S, 128 * q:128 * q + 128], A.add, ["F1" if q < 4 else "G1", "tq%d" % q],
+                ["pc%d" % r], 128, [1 if q < 4 else 3])
+            at(a + (min(k3, 6.0) if t in (1, RO - 1) else k3))
             act(T.DYN[0:S, 128 * q:128 * q + 128], prow(r), ["pc%d" % r], ["DYN%d" % q], 128)
-        vts(T.nhd[0:S, :], prow(4), 1.0 / 15.0, 130.0 - (7.0 + OFF) / 15.0, A.mult, A.add, ["pc4"], ["nhd"], 128)
-        vtt(T.key[0:S, :], T.nhd[0:S, :], T.nd[0:S, :], A.add, ["nhd", "nd"], ["key"], 256)
+        at(a + 4.05)
+        if SMALL[2] == "V":
+            vts(T.nhd[0:S, :], prow(4), 1.0 / 15.0, 130.0 - (7.0 + OFF) / 15.0, A.mult, A.add, ["pc4"], ["nhd"], 64)
+        else:
+            act(T.nhd[0:S, :], prow(4), ["pc4", "c130"], ["nhd"], 128, scale=1.0 / 15.0, bias=T.BC[0:S, 7:8])
+        at(a + 4.3)
+        vtt(T.key[0:S, :], b0[0:S, 0:128], T.nhd[0:S, :], A.add, ["nhd", "nd"], ["key"], 128, [0])
         for h in range(4):
             vts(T.mk[0:S, 128 * h:128 * h + 128], T.key[0:S, :], 130.0 + h, None, A.is_equal, None, ["key"], ["mk%d" % h], 64)
         MK = ["mk0", "mk1", "mk2", "mk3"]
         op("V", lambda: V.tensor_tensor_scan(T.scn[0:S, :], T.sgm[0:S, :], T.mk[0:S, :], 0.0, A.mult, A.add), MK + ["sgm"], ["scn"], FIX + CY * 256)
-        mm(grp(b2[0:S, :], [(T.NU[0:S, 0:S], T.mk[0:S, :]), (T.one[0:S, 0:S], T.scn[0:S, :])]), MK + ["scn", "NU", "one"], ["F2"], 1024, [2])
-        vtt(T.t1[0:S, :], b2[0:S, :], T.mk[0:S, :], A.mult, ["F2"] + MK, ["t1"], 512, [2])
-        mm(grp(b3[:, 224:336], [(T.DYN[0:S, 256:384], T.I64[0:S, 0:S]), (T.DYN[0:S, 384:512], T.IB[0:S, 0:S])])
-           + grp(b3[:, 336:448], [(T.DYN[0:S, 0:128], T.I64[0:S, 0:S]), (T.DYN[0:S, 128:256], T.IB[0:S, 0:S])]),
-           ["DYN0", "DYN1", "DYN2", "DYN3", "I64", "IB"], ["Tn"], 448, [3])
-        act(T.nB[:], b3[:, 224:336], ["Tn"], ["nB"], S, [3], f=AF.Copy, bias=-float(W - 1 + BOTH))
-        act(T.lB[:], b3[:, 336:448], ["Tn"], ["lB"], S, [3], f=AF.Copy, bias=-float(W - 1 + SEG * t + BOTH))
-        lst = grp(b3[:, 0:224], [(T.mk[0:S, 128 * h:128 * h + 128], T.RR[0:S, 224 * h:224 * h + 224]) for h in range(4)]
-                  + [(T.t1[0:S, 128 * h:128 * h + 128], T.RR[0:S, 896:1120]) for h in range(4)])
-        mm(lst[:4], MK + RRS, ["Tp0"], 896, [3])
-        mm(lst[4:], ["t1", "Tp0"] + RRS, ["Tp"], 896, [3])
-        vts(T.z[:], b3[:, 0:S], -71.5, -16384.0, A.is_gt, A.mult, ["Tp"], ["z"], S, [3])
-        vtt(T.y[:], b3[:, S:224], T.z[:], A.add, ["Tp", "Tp0", "z"], ["y"], S, [3])
-        vtt(T.mo[:], T.y[:], T.nB[:], A.max, ["y", "nB"], ["mo"], 2 * S)
-        vts(T.moff[:], T.mo[:], float(W - 1), None, A.add, None, ["mo"], ["moff"], S)
-        vtt(T.xo[:, 0:S], T.y[:], T.lB[:], A.max, ["y", "lB", "xop"], ["xo"], 2 * S)
-        op("V", lambda: V.transpose(T.xv[:], T.xo[:]), ["xo", "xop"], ["xv"], FIX + CY * 128)
-        lst = []
-        for mh in range(7):
-            b, d = divmod(mh, 2)
-            lst += grp(b4[:, 304 + mh:416:7], [(T.MF[:, 128 * (2 * d + e):128 * (2 * d + e) + 128], T.xv[:, 32 * b + 16 * e:32 * b + 16 * e + 16]) for e in range(2)])
-        mm(lst, ["xv", "MF"], ["XW"], 3584, [4])
-        vts(T.xoff[:, S * t:S * t + S], b4[:, 304:416], float(W - 1 + SEG * t), None, A.add, None, ["XW"], ["xoff%d" % t], S, [4])
-        PCS = ["pc2", "pc3", "pc4", "pc5", "pc10", "pc11"]
-        for c in range(4):
-            bk = (b0, b1)[c % 2]; res = F0 if c % 2 == 0 else ["F1"]
-            mm([(bk[:, S * j:S * j + S], PAYC[0:S, :, 4 * c + j], T.IB[0:S, 0:S], True, True) for j in range(4)],
-               PCS + ["IB"], res, 448, [c % 2])
-            for j in range(4):
-                act(T.PAY[:, 4 * c + j::16], bk[:, S * j:S * j + S], res + ["BC"], ["pay%d" % (4 * c + j)], S, [c % 2], bias=T.BC[:, t:t + 1], scale=UNIT)
-        cp(DEFE, TB[:, W:W + 512], T.DEF[:], ["DEF"], ["TBp"], 512)
-        nsp = NSP if t else 1; cw = S // nsp
-        for c in range(nsp):
-            act(TB[:, :].indirect(T.moff[:, cw * c:cw * c + cw]), T.PAY[:, 16 * cw * c:16 * cw * (c + 1)], ["moff"] + ["pay%d" % k for k in range(16)],
-                TBN + ["TBp"], CS * K / nsp, f=AF.Tanh)
-        act(T.GS[:], TB[:, W:W + 512], ["TBp", "BC5"], ["GS"], 512, bias=T.BC[:, 5 + t:6 + t] if t < 3 else 0.0)
-        op("V", lambda: V.transpose(T.VT[:], TB[:, W:W + 512]), ["TBp"], ["VT"], FIX + CY * 512)
-        for q, r0 in enumerate((4, 10)):
-            if q == 1 and t == 0:
-                continue
-            vcp(T.VB[:, q], T.VT[:, :, r0:r0 + 2], ["VT"], ["VB%d" % q], 64)
-            lst = []
-            for xh in range(2):
-                prs = []
-                for e in range(2):
-                    c = 128 * (2 * xh + e)
-                    prs += [(T.MM[:, 512 + c:640 + c], T.VB[:, q, 2 * e::4]), (T.MM[:, c:c + 128], T.VB[:, q, 2 * e + 1::4])]
-                lst += grp(b4[:, 32 * q + xh:32 * q + 32:2], prs)
-            mm(lst, ["VB%d" % q] + MMS, ["LL%d" % q], 512, [4])
-        nl = T.nl16[:, 32 * t:32 * t + 32]
-        vts(nl, b4[:, 0:32], -float(BOTH), None, A.add, None, ["LL0"], ["nl%d" % t], 32, [4])
-        act(TB[:, :].indirect(nl), T.GS[:], ["nl%d" % t, "GS"], TBN + ["TBp"], CS * 512, f=AF.Tanh)
-        vtt(T.hv1[:], b4[:, 0:32], T.hoff[:], A.subtract, ["LL0", "hoff"], ["hva"], 32, [4])
-        vtt(T.PO[:, 4 * t:4 * t + 4, 128:136], T.hv1[:], T.hcap[:], A.min, ["hva", "hcap"], ["hv%d" % t], 64)
+        lst = grp(b2[0:S, :], [(T.NU[0:S, 0:S], T.mk[0:S, :]), (T.one[0:S, 0:S], T.scn[0:S, :])])
+        mm(lst[:1], MK + ["NU"], ["F2"], 512, [2])
+        mm(lst[1:], ["scn", "one", "F2"], ["cnt"], 512, [2])
+        at(a + 6.0)
+        act(T.u[0:S, :], b2[0:S, :], ["cnt", "c128"], ["u"], 512, [2], f=AF.Sign, scale=-1.0, bias=T.BC[0:S, 5:6])
+        nm = [(T.DYN[0:S, 256:384], T.I64[0:S, 0:S]), (T.DYN[0:S, 384:512], T.IB[0:S, 0:S])]
+        if not last:
+            at(a + 7.0)
+            lst = grp(b4[:, 0:S], nm + [(T.u[0:S, 128 * h:128 * h + 128], T.IW[0:S, 0:S]) for h in range(4)])
+            mm(lst, ["DYN2", "DYN3", "I64", "IB", "IW", "u"], ["m1"], 6 * S, [4])
+            vts(T.moff[:], b4[:, 0:S], float(2 * W - BOTH), None, A.add, None, ["m1"], ["moff"], S, [4])
         if t > 0:
-            vts(T.ll16[:, 32 * t:32 * t + 32], b4[:, 32:64], -float(BOTH), None, A.add, None, ["LL1"], ["ll%d" % t], 32, [4])
-        if t == RO - 1:
-            dma("Y", T.cl32[:, 0:240], TB[2::16, 0:W], ["TB2"], ["cl0"], 300.0)
-            dma("Y", T.cl32[:, 240:480], TB[3::16, 0:W], ["TB3"], ["cl1"], 600.0)
-            act(T.cl[:, 0:240], T.cl32[:, 0:240], ["cl0", "clp0"], ["cb0"], 240)
-            act(T.cl[:, 256:496], T.cl32[:, 240:480], ["cl1", "clp1"], ["cb1"], 240)
-            op("V", lambda: V.transpose(T.VF[:], T.cl[:]), ["cb0", "cb1", "clp0", "clp1"], ["VF"], FIX + CY * 256)
-            lst = []
-            for y1 in range(15):
-                b, d = divmod(y1, 2); prs = []
-                for e in range(2):
-                    c = 128 * (2 * d + e); o = 32 * b + 16 * e
-                    prs += [(T.MM[:, 512 + c:640 + c], T.VF[:, o:o + 16]), (T.MM[:, c:c + 128], T.VF[:, 256 + o:256 + o + 16])]
-                lst += grp(b4[:, 64 + y1:304:15], prs)
-            mm(lst, ["VF"] + MMS, ["AS"], 3840, [4])
-            vts(T.fo[:], b4[:, 64:304], -float(BOTH), None, A.add, None, ["AS"], ["fo"], 240, [4])
-            return
-        dma("Y", T.dG[t], TB[RG[t]::16, 0:W], ["TBg"], ["dG%d" % t])
-        for i, r in enumerate(peers):
-            j = slot(rank, r)
-            s, n = send1(r, T.dL[3 * t + j], T.dG[t], "rG%d_%d" % (t, j), ["dG%d" % t] + ["ord%d" % (i - 1)] * (i > 0), ["ord%d" % i])
-            recv("rG%d_%d" % (t, j), n, [s], ["dL%d_%d" % (t, j)], REM_T + 900 + 300 * i)
-        for j in (2, 1, 0):
-            dma("Y", TB[10 + j::16, 0:W], T.dL[3 * t + j], ["dL%d_%d" % (t, j)], ["TBf%d" % j], 200.0)
-        dma("Y", TB[0::16, 0:W], T.dW[:], ["dW", "dG%d" % t], ["TBw"], 300.0)
-        dma("Y", TB[1::16, 0:W], T.ac[:], ["ac", "dG%d" % t], ["TBa"], 600.0)
-        if t == 2:
-            return
-        aft = ["TBf0", "TBf1", "TBf2"]
-        dma("Y", T.cc[:], TB[6 + t::16, 0:W], ["TBc"] + aft, ["cc"], 900.0)
-        for j in range(3):
-            dma("Y", T.gl[:, 240 * j:240 * j + 240], T.dL[3 * t + j], ["dL%d_%d" % (t, j)] + aft, ["gl%d" % j], 1000.0 + 300.0 * j)
-        dma("Y", T.gl[:, 720:960], T.dG[t], ["dG%d" % t] + aft, ["gl3"], 900.0)
-        vts(T.cap[:], T.gl[:, 720:960], -100.0, 102.0, A.mult, A.add, ["gl3"], ["cap"], 240)
-        mm(grp(b4[:, 64:304], [(T.IF[:], T.ac[:]), (T.IF[:], T.cc[:]), (T.IF[:], T.cc[:])] + [(T.IF[:], T.gl[:, 240 * j:240 * j + 240]) for j in range(3)]),
-           ["IF", "ac", "cc", "gl0", "gl1", "gl2"], ["AS"], 5760, [4])
-        vtt(T.ac[:], b4[:, 64:304], T.cap[:], A.min, ["AS", "cap"], ["ac"], 240, [4])
+            at(a + (6.5 if last else 8.0))
+            vts(T.t1[0:S, :], b2[0:S, :], 128.0, 0.0, A.add, A.min, ["cnt"], ["t1"], 512, [2])
+            at(a + (7.0 if last else 8.5))
+            mm(grp(b2[:, 0:S], [(T.u[0:S, 128 * h:128 * h + 128], T.RR[0:S, S * h:S * h + S]) for h in range(4)]
+                   + [(T.t1[0:S, 128 * h:128 * h + 128], T.IB[0:S, 0:S]) for h in range(4)]), ["u", "t1", "IB"] + RRS, ["F2", "cnt", "y"], 8 * S, [2])
+            if last:
+                at(a + 6.8)
+                mm(grp(b3[:, 0:S], nm), ["DYN2", "DYN3", "I64", "IB"], ["G1", "Tn"], 2 * S, [3])
+                act(T.cix[:], b3[:, 0:S], ["Tn"], ["cix"], S, [3], f=AF.Copy, bias=float(YB + 1 - HALF - W - 512 - BOTH))
+            at(a + (7.5 if last else 10.0))
+            vtt(T.co[:], b2[:, 0:S], T.cix[:], A.max, ["y", "cix"], ["co"], S, [2])
+            vts(T.coff[:], T.co[:], -float(YB + 1 - HALF - (W + 512 if last else K)), None, A.add, None, ["co"], ["coff"], S)
+        for c in range(4):
+            bk = (b0, b1)[c % 2]; res = F0 + ["sc1", "nd"] if c % 2 == 0 else ["F1"]
+            at(a + (6.1, 7.7, 8.2, 8.7)[c])
+            mm([(bk[:, k:448:16], PAYC[0:S, :, k], T.IB[0:S, 28 * c:28 * c + 28], True, True) for k in range(16)], PCS + ["IB"], res, 1024, [c % 2])
+            out = T.PAY[:, 448 * c:448 * c + 448]
+            if PAYE[t][c] == "S":
+                if c:
+                    at(a + (C2K if last else C1K)[t][c] - 0.1)
+                act(out, bk[:, 0:448], res + ["BC"], ["pay%d" % c], 448, [c % 2], bias=T.BC[:, t:t + 1], scale=UNIT)
+            else:
+                vts(out, bk[:, 0:448], UNIT, T.BC[:, t:t + 1], A.mult, A.add, res + ["BC"], ["pay%d" % c], 448, [c % 2])
 
-    def data(t):
-        a0 = W + SEG * t; x0 = a0 + 512
-        nl = T.nl16[:, 32 * t:32 * t + 32]
+        def places(k):
+            at(a + k)
+            shift = YB + 1 - HALF - L0 - SEG * t if t else 0
+            if t == 0:
+                vts(T.xo[:, 0:S], b4[:, 0:S], float(2 * W - BOTH), None, A.add, None, ["m1", "xop"], ["xo"], S, [4])
+            else:
+                if not last:
+                    mm(grp(b3[:, 0:S], nm), ["DYN2", "DYN3", "I64", "IB"], ["G1", "Tn"], 2 * S, [3])
+                shifted(SMALL[4], T.nB[:], b3[:, 0:S], shift - BOTH, ["Tn"], ["nB"], S, [3])
+                lst = []
+                for j, q in enumerate((0, 4)):
+                    lst += grp(b3[:, S + S * j:2 * S + S * j], [(T.one[0:1, :], T.DR[0:1, S * t:S * t + S]), (T.one[0:1, :], T.DR[0:1, RO * S:RO * S + S]), (T.DYN[0:S, 128 * q:128 * q + 128], T.I128[0:S, 0:S]),
+                                                                 (T.DYN[0:S, 128 * q + 128:128 * q + 256], T.IB[0:S, 0:S])])
+                mm(lst, ["DYN0", "DYN1", "DYN4", "DYN5", "I128", "IB", "one", "DR", "DR2"], ["G1", "G2", "Tp"], 8 * S, [3])
+                vtt(T.o1[:], b3[:, S:2 * S], T.nB[:], A.max, ["Tp", "nB"], ["o1"], S, [3])
+                vtt(T.o2[:], b3[:, 2 * S:3 * S], T.o1[:], A.max, ["Tp", "o1"], ["o2"], S, [3])
+                vtt(T.xo[:, 0:S], b2[:, 0:S], T.o2[:], A.max, ["y", "o2", "xop"], ["xo"], S, [2])
+            op("V", lambda: V.transpose(T.xv[:], T.xo[:]), ["xo", "xop"], ["xv"], FIX + CY * 128)
+            lst = []
+            for mh in range(7):
+                b, d = divmod(mh, 2)
+                lst += grp(b4[:, 304 + mh:416:7], [(T.MF[:, 128 * (2 * d + e):128 * (2 * d + e) + 128], T.xv[:, 32 * b + 16 * e:32 * b + 16 * e + 16]) for e in range(2)])
+            mm(lst[:6], ["xv", "MF"], ["XW0", "XW"], 1536, [4])
+            mm(lst[6:], ["xv", "MF"], ["XW"], 2048, [4])
+            at(a + k + 2.0)
+            vts(T.xoff[:, S * t:S * t + S], b4[:, 304:416], -float(shift), None, A.add, None, ["XW0", "XW"], ["xoff%d" % t], S, [4])
+
+        def scatter(engs, turns, win, off, rd, wr):
+            cw = S // len(engs)
+            for c, en in enumerate(engs):
+                out = win.indirect(off[:, cw * c:cw * c + cw]); src = T.PAY[:, 16 * cw * c:16 * cw * (c + 1)]
+                pay = ["pay%d" % c]
+                at(a + turns[c])
+                if en == "S":
+                    act(out, src, rd + pay, wr, CS * 16 * cw, f=AF.Tanh)
+                else:
+                    vcp(out, src, rd + pay, wr, CS * 16 * cw)
+
+        def by_name():
+            scatter(C1E[t], C1K[t], TB[:, 0:2 * W], T.moff, ["moff"], TB1 + TB2 + (["TCp2", "TCg2"] + ["TBz%d" % c for c in range(8)] if t == 0 else []) + ["C1"])
+
+        def by_list():
+            if last:
+                scatter(C2E[t], C2K[t], TB[:, 0:W + 1024], T.coff, ["coff"], TB1 + ["LS", "C2"])
+            else:
+                scatter(C2E[t], C2K[t], LS[:, :], T.coff, ["coff"], ["LS", "C2"])
+            at(a + LISTK[t])
+            lists = TB[:, W + 512:W + 1024] if last else LS[:, K:K + 512]
+            op("V", lambda: V.transpose(T.VT[:], lists), ["LS"], ["VT"], FIX + CY * 512)
+            vcp(T.VB[:], T.VT[:, :, 4:10], ["VT"], ["VB"], 192)
+            for q, big in ((0, 0), (2, 1), (1, 1)):
+                lst = []
+                for xh in range(2):
+                    prs = []
+                    for e in range(2):
+                        c = 128 * (2 * xh + e)
+                        prs += [(mm_big(big, c), T.VB[:, 6 * e + 2 * q::12]), (T.MM[:, c:c + 128], T.VB[:, 6 * e + 2 * q + 1::12])]
+                    lst += grp(b4[:, 128 + 32 * q + xh:160 + 32 * q:2], prs)
+                mm(lst, ["VB", "MM4", "MM5"] + MM1, ["LL%d" % q], 512, [4])
+            at(a + LISTK[t] + 1.0)
+            shifted(SMALL[5], T.n0[:], b4[:, 128:160], PRAW - BOTH, ["LL0"], ["n0"], 32, [4])
+            shifted(SMALL[5], T.bz[:], b4[:, 192:224], -K, ["LL2"], ["bz"], 32, [4])
+            vtt(T.c1[:], b4[:, 192:224], T.n0[:], A.max, ["LL2", "n0"], ["c1"], 32, [4])
+            vtt(T.lb[:, 32:64], T.bz[:], T.n0[:], A.max, ["bz", "n0"], ["lbb"], 64)
+            vtt(T.lb[:, 0:32], b4[:, 160:192], T.c1[:], A.max, ["LL1", "c1"], ["lba"], 32, [4])
+            vtt(T.hv1[:], b4[:, 128:160], T.hoff[:], A.subtract, ["LL0", "hoff"], ["hv1"], 32, [4])
+            vts(T.lb16[:, 64 * t:64 * t + 64], T.lb[:], -float(PRAW), None, A.add, None, ["lba", "lbb"], ["ll%d" % t], 64)
+            vtt(T.PO[:, 4 * t - 4:4 * t, 128:136], T.hv1[:], T.hcap[:], A.min, ["hv1", "hcap"], ["hv%d" % t], 64)
+
+        def closing(_):
+            at(a + 20.0)
+            vts(T.nl16[:], T.n0[:], -float(PRAW), None, A.add, None, ["n0", "PO%d_%d" % (t, peers[2])], ["nl"], 32)
+            act(TB[:, 0:W + 512].indirect(T.nl16[:]), TB[:, W + 512:W + 1024], ["nl", "LS"], TB1 + ["C1"], CS * 512, f=AF.Tanh)
+            at(a + 22.0)
+            c32, cb, fm, fd = W + 1024, 2160, W + 1984, 3120
+            for j, r in enumerate((2, 3, 8, 9)):
+                dma("Y", TB[:, c32 + 240 * j:c32 + 240 * j + 240], TB[r::16, 0:W], ["TBo", "TBp", "TBq"], ["cl%d" % j], 130)
+            at(a + 25.2)
+            for j in range(2):
+                o = cb + 480 * j
+                act(T0[:, o:o + 480], TB[:, c32 + 480 * j:c32 + 480 * j + 480], ["cl%d" % (2 * j), "cl%d" % (2 * j + 1)], ["cb%d" % j], 480)
+                mm(grp(b0[:, 240 * j:240 * j + 240], [(T.I128[:], T0[:, o:o + 240]), (T.IB[:], T0[:, o + 240:o + 480])]),
+                   ["cb%d" % j, "I128", "IB"], F0 + ["fv%d" % j], 480, [0])
+            vtt(TB[:, fm:fm + 240], b0[:, 0:240], T.nmc[:], A.max, ["fv0", "nmc"] + F0, ["fm0"], 240, [0])
+            vtt(TB[:, fm + 240:fm + 480], b0[:, 240:480], TB[:, fm:fm + 240], A.max, ["fv1", "fm0"] + F0, ["fm1"], 240, [0])
+            act(T0[:, fd:fd + 240], TB[:, fm + 240:fm + 480], ["fm1"], ["fd0"], 240)
+            vtt(T0[:, fd + 256:fd + 496], TB[:, fm + 240:fm + 480], T0[:, fd:fd + 240], A.subtract, ["fm1", "fd0"], ["fd1"], 480)
+            op("V", lambda: V.transpose(T.EB[:, peers[2], 0:512], T0[:, fd:fd + 512]), ["fd0", "fd1"], ["EBr", "VF"], FIX + CY * 256)
+            for part in range(3):
+                lst = []
+                for y1 in range(5 * part, 5 * part + 5):
+                    b, d = divmod(y1, 2); prs = []
+                    for e in range(2):
+                        c = 128 * (2 * d + e); o = 32 * b + 16 * e
+                        prs += [(T.MM[:, c:c + 128], T.EB[:, peers[2], o:o + 16]), (T.MM[:, c:c + 128], T.EB[:, peers[2], 256 + o:256 + o + 16])]
+                    lst += grp(b4[:, 64 + y1:304:15], prs)
+                mm(lst, ["VF"] + MM1, ["LL0", "LL1", "LL2", "m1", "AS%d" % part], 1280, [4])
+            at(a + 30.7)
+            vts(T.fo[:], b4[:, 64:304], -float(PRAW), None, A.add, None, ["AS0", "AS1", "AS2", "LL0"], ["fo"], 240, [4])
+
+        if last:
+            by_list()
+            places(20.5)
+            later.append(closing)
+            return
+        if t != 1:
+            places((9.7, 0, 16.4)[t])
+        by_name()
+        at(a + 14.6)
+        d = dma("Y", T.gr[:], TB[10 + t::16, W:2 * W], ["TCg"], ["gr"], 130)
+        d = dma("Y", T.tk[:], TB[10 + t::16, 0:W], ["TBo"], ["tk"], 130, [d])
+        dma("Y", TB[8::16, 0:W], TB[2::16, W:2 * W], ["TCp"], ["TBp"], 120, [d])
+        dma("Y", TB[9::16, 0:W], TB[3::16, W:2 * W], ["TCp"], ["TBq"], 120, [d])
+        dma("Y", TB[0::16, 0:W], T.dW[:], ["dW"], ["TBw"], 120, [d])
+        if t == 0:
+            dma("Y", TB[4::16, 0:W], LS[0:120, 0:256], ["LS", "C1"], ["TBn"], 130, [d])
+            dma("Y", TB[5::16, 0:W], LS[0:120, 256:512], ["LS", "C1"], ["TBm"], 130, [d])
+        at(a + 16.3)
+        gb = T0[:, 1440 + 240 * t:1680 + 240 * t]
+
+        def land(j):
+            return T0[:, 720 * t - 720 + 240 * j:720 * t - 480 + 240 * j] if t else T.FL[:, 240 * j:240 * j + 240]
+        cp(GBE[t], gb, T.gr[:], ["gr"], (T0N if t == 0 else []) + ["gb%d" % t], 240)
+        s, n = send_all([land(slot(rank, r)) for r in peers], gb, "rG%d_%d" % (t, rank), ["gb%d" % t], 70)
+        for r in peers:
+            recv("rG%d_%d" % (t, r), n, [s], ["FL%d_%d" % (t, r)])
+        at(a + 17.0)
+        if SMALL[3] == "V":
+            vts(T.cap[:], gb, -100.0, 102.0, A.mult, A.add, ["gb%d" % t], ["cap"], 120)
+        else:
+            act(T.cap[:], gb, ["gb%d" % t], ["cap"], 240, f=AF.Copy, scale=-100.0, bias=102.0)
+        lst = grp(b0[:, 0:240], [(T.IF[:], T.ac[:]), (T.I2[:], T.tk[:]), (T.IB[:], gb), (T.IB[:], gb)] + [(T.IB[:], land(j)) for j in range(3)])
+        at(a + 13.9)
+        mm(lst[:1], ["IF", "ac"], F0 + ["sc1", "nd", "AS"], 960, [0])
+        at(a + 16.4)
+        mm(lst[1:4], ["I2", "IB", "tk", "gb%d" % t], ["AS"], 1440, [0])
+        at(a + 19.4)
+        mm(lst[4:], ["IB", "AS"] + ["FL%d_%d" % (t, r) for r in peers], ["AS1"], 720, [0])
+        vtt(T.ac[:], b0[:, 0:240], T.cap[:], A.min, ["AS", "AS1", "cap"] + F0, ["ac"], 240, [0])
+        dma("Y", TB[1::16, 0:W], T.ac[:], ["ac"], ["TBa"], 130)
+        if t > 0:
+            by_list()
+        if t == 1:
+            places(20.0)
+
+    def exchange(t):
+        last = t == RO - 1; a = 24.0 * t
+        kp, ko, kr, ka = DATAK[t][:4]
+        a0 = L0 + SEG * t
         HW = T.H[:, :]
         lists = {r: T.HL[:, 32 * t + 8 * r:32 * t + 8 * r + 8] for r in range(N)}
         lres = {r: "HL%d_%d" % (t, r) for r in range(N)}
-        c0 = 128 if t == 0 else 0
-        if t > 0:
-            if t < RO - 1:
-                cp("V", T.Bg[:], T.B[:, :].indirect(nl), ["Ba", "Bb", "Bd", "nl%d" % t], ["Bg%d" % r for r in range(N)], CG * 512)
         sent = {}
+        at(a + kp)
         for r in peers + [rank]:
-            o = 32 * t + 8 * r
-            if t == RO - 1:
-                cp("S", T.Bg[:, 128 * r:128 * r + 128], T.B[:, :].indirect(T.nl16[:, o:o + 8]), ["Ba", "Bb", "Bd", "nl%d" % t], ["Bg%d" % r], CG * 128)
-            if t > 0:
-                vtt(T.PO[:, 4 * t + r, 0:128], LOG[:, 0:a0].indirect(T.ll16[:, o:o + 8]), T.Bg[:, 128 * r:128 * r + 128], A.subtract,
-                    logres(t, False) + ["ll%d" % t, "Bg%d" % r], ["PO%d_%d" % (t, r)], CG * 128)
+            o = 64 * t + 8 * r
+            i = (r - rank) % N; bg = T.ht[:, 128 * i:128 * i + 128]
+            cp(BGE, bg, LOG[:, 0:a0 - K].indirect(T.lb16[:, o + 32:o + 40]), logres(t, False, False) + ["ll%d" % t], ["ht%d" % i], CG * 128)
+            vtt(T.PO[:, 4 * t - 4 + r, 0:128], LOG[:, 0:a0].indirect(T.lb16[:, o:o + 8]), bg, A.subtract,
+                logres(t, False) + ["ll%d" % t, "ht%d" % i], ["PO%d_%d" % (t, r)], CG * 128)
             if r != rank:
                 j = slot(rank, r)
-                sent[j], n = send1(r, T.PL[:, 3 * t + j, c0:136], T.PO[:, 4 * t + r, c0:136], "rP%d_%d" % (t, j), ["PO%d_%d" % (t, r), "hv%d" % t])
+                sent[j], n = send1(r, T.PL[:, 3 * t - 3 + j, :], T.PO[:, 4 * t - 4 + r, :], "rP%d_%d" % (t, j), ["PO%d_%d" % (t, r), "hv%d" % t])
         for j in range(3):
-            recv("rP%d_%d" % (t, j), n, [sent[j]], ["PL%d_%d" % (t, j)], REM_T + 1500)
+            recv("rP%d_%d" % (t, j), n, [sent[j]], ["PL%d_%d" % (t, j)])
         for i, r in enumerate([rank] + peers[::-1]):
             if r == rank:
-                rs = ["PO%d_%d" % (t, r), "hv%d" % t]; buf, bi = T.PO, 4 * t + r
+                rs = ["PO%d_%d" % (t, r), "hv%d" % t]; buf, bi = T.PO, 4 * t - 4 + r; at(a + ko)
             else:
-                j = slot(r, rank); rs = ["PL%d_%d" % (t, j)]; buf, bi = T.PL, 3 * t + j
+                j = slot(r, rank); rs = ["PL%d_%d" % (t, j)]; buf, bi = T.PL, 3 * t - 3 + j; at(a + kr[i - 1])
+            k = now[1]; at(k - (0.75 if last and i > 1 else 0.0))
             vcp(lists[r], buf[:, bi, 128:136], rs, [lres[r]], 8)
-            if t > 0:
-                if HOME_S:
-                    act(T.ht[:, 128 * i:128 * i + 128], HW.indirect(lists[r]), ["H", "Hd", lres[r]], ["ht%d" % i], CG * 128)
-                    vtt(HW.indirect(lists[r]), T.ht[:, 128 * i:128 * i + 128], buf[:, bi, 0:128], A.add, ["ht%d" % i, lres[r]] + rs, ["H", "Hd"], CS * 128)
-                else:
-                    vtt(T.ht[:, 128 * i:128 * i + 128], HW.indirect(lists[r]), buf[:, bi, 0:128], A.add, ["H", "Hd", lres[r]] + rs, ["ht%d" % i], CG * 128)
-                    vcp(HW.indirect(lists[r]), T.ht[:, 128 * i:128 * i + 128], ["ht%d" % i, lres[r]], ["H", "Hd"], CS * 128)
+            at(k)
+            act(T.ht[:, 128 * i:128 * i + 128], HW.indirect(lists[r]), ["H", "Hd", lres[r]], ["ht%d" % i], CG * 128)
+            at(now[1] + 0.15)
+            vtt(HW.indirect(lists[r]), T.ht[:, 128 * i:128 * i + 128], buf[:, bi, 0:128], A.add, ["ht%d" % i, lres[r]] + rs, ["H", "Hd"], CS * 128)
         sent = []
+        at(a + ka)
         for i, r in enumerate(peers):
-            c = 128 * (3 * t + i)
-            cp("V" if i % 2 == 0 else "S", T.AO[:, c:c + 128], HW.indirect(lists[r]), ["H", "Hd", lres[r]], ["AO%d_%d" % (t, i)], CG * 128)
+            c = 128 * (3 * t - 3 + i)
+            cp("VSV"[i] if last else AOE[i], T.AO[:, c:c + 128], HW.indirect(lists[r]), ["H", "Hd", lres[r]], ["AO%d_%d" % (t, i)], CG * 128)
             s, n = send1(r, LOG[:, a0 + 128 * rank:a0 + 128 * rank + 128], T.AO[:, c:c + 128], "rA%d" % t, ["AO%d_%d" % (t, i)])
             sent.append(s)
         cp("S", LOG[:, a0 + 128 * rank:a0 + 128 * rank + 128], HW.indirect(lists[rank]), ["H", "Hd", lres[rank]], ["A%d_o" % t], CG * 128)
-        recv("rA%d" % t, 3 * n, sent, ["A%d_r" % t], REM_T + 1500)
-        if t == RO - 1:
-            dma("Y", T.yh[:], T.H[:, 0:M], ["H", "A%d_r" % t], ["yh"], 1500.0)
-        now[1] = 1
-        X1 = ["x10", "x11", "x12", "x13"]; XX = ["x0"] + X1
-        for hf in range(2):
-            o = S * t + 56 * hf
-            if hf == 1 and t == RO - 1:
-                for c in range(4):
-                    cp("S", x[:, 896 + 224 * c:1120 + 224 * c], LOG[:, 0:x0].indirect(T.xoff[:, o + 14 * c:o + 14 * c + 14]),
-                       logres(t, True) + ["xoff%d" % t], ["x1%d" % c], CG * 224)
-            else:
-                cp(XG[hf], x[:, 896 * hf:896 * hf + 896], LOG[:, 0:x0].indirect(T.xoff[:, o:o + 56]), logres(t, True) + ["xoff%d" % t],
-                   ["x0"] if hf == 0 else X1, CG * 896)
-        now[1] = 2
+        recv("rA%d" % t, 3 * n, sent, ["A%d_r" % t])
+        if last:
+            dma("Y", T.yh[:], T.H[:, 0:M], ["H", "A%d_r" % t], ["yh"], 480)
+
+    def data(t):
+        last = t == RO - 1; a = 24.0 * t
+        k1, kq, k0, ke, ks = DATAK[t][4:]
+        x0 = L0 + SEG * t + 512; X0 = x0 + K
+
+        def x(o, n):
+            return LOG[:, x0 + o:x0 + o + n]
+        X1 = ["x%d_%d" % (t, c) for c in range(1, 5)]; XA = "x%d_0" % t; XX = [XA] + X1
+        rd = logres(t, True) + ["xoff%d" % t]; e1, e0 = XG[t]; np1 = 4 if last else 2; cw = 56 // np1
+        at(a + k1)
+        for c in range(np1):
+            o = S * t + 56 + cw * c
+            cp(e1, x(896 + 16 * cw * c, 16 * cw), LOG[:, 0:x0].indirect(T.xoff[:, o:o + cw]), rd, X1[4 // np1 * c:4 // np1 * (c + 1)], CG * 16 * cw)
         lst = grp(b5[:, 0:S], [(T.BO[0:16, :], T.tgf[0:16, S * t:S * t + S])] + [(T.BO[:], T.PR[:, S * k:S * k + S]) for k in range(8)])
         mm(lst[:1], ["BO", "tgf"], ["p0", "st1"], 448, [5])
+        at(a + kq)
         for c in range(4):
-            if t == RO - 1:
-                o = S * t + 14 * c
-                vtt(T.PR[:, 224 * c:224 * c + 224], LOG[:, 0:x0].indirect(T.xoff[:, o:o + 14]), x[:, 896 + 224 * c:1120 + 224 * c], A.mult,
-                    logres(t, True) + ["xoff%d" % t, "x1%d" % c], ["PR%d" % c], CG * 224)
-            else:
-                vtt(T.PR[:, 224 * c:224 * c + 224], x[:, 224 * c:224 * c + 224], x[:, 896 + 224 * c:1120 + 224 * c], A.mult, XX, ["PR%d" % c], 448)
+            o = S * t + 14 * c
+            vtt(T.PR[:, 224 * c:224 * c + 224], LOG[:, 0:x0].indirect(T.xoff[:, o:o + 14]), x(896 + 224 * c, 224), A.mult, rd + [X1[c]], ["PR%d" % c], CG * 224)
             mm(lst[1 + 2 * c:3 + 2 * c], ["BO", "PR%d" % c, "p%d" % c], ["p%d" % (c + 1)], 896, [5])
+        at(a + k0)
+        cp(e0, x(0, 896), LOG[:, 0:x0].indirect(T.xoff[:, S * t:S * t + 56]), rd, [XA], CG * 896)
+        at(a + ke)
         act(T.e[:], b5[:, 0:S], ["p0", "p1", "p2", "p3", "p4"], ["e"], S, [5], f=AF.Tanh, scale=-1.0 / 128.0)
-        for j in range(4):
-            vts(b6[:, S * j:S * j + S], T.e[:], 1.0 / 32.0, None, A.mult, None, ["e"], ["E%d" % j], S, [6])
-        for c in range(4):
-            bk, bn = ((b7, 7), (b5, 5))[c % 2]; pk = (4 * c + 8) % 16
-            if t == RO - 1 and c < 2:
-                bk = (b0, b1)[c]; pr = ["PR%d" % (2 * c), "PR%d" % (2 * c + 1)]
-                res = ["F0_00", "F0_01", "F0_10", "F0_11", "F0_20", "F0_21"] if c == 0 else ["F1"]
-                lst = grp(bk[:, 0:448], [(T.IF[:], x[:, 448 * c:448 * c + 448]), (T.IF[:], T.PR[:, 448 * c:448 * c + 448])])
-                mm(lst[:1], ["IF", "p4"] + XX, res, 1792, [c])
-                vtt(T.PR[:, 448 * c:448 * c + 448], b6[:, 0:448], x[:, S * pk:S * pk + 448], A.mult, ["E0", "E1", "E2", "E3"] + XX, pr, 448, [6])
-                mm(lst[1:], ["IF"] + pr + res, ["ad%d" % c], 1792, [c])
-                act(LOG[:, x0 + 448 * c:x0 + 448 * c + 448], bk[:, 0:448], res + ["ad%d" % c], ["X%d_%d" % (t, c)], 448, [c])
+        EE = ["E0", "E1", "E2", "E3"]
+        if last:
+            for j in range(4):
+                vts(b6[:, S * j:S * j + S], T.e[:], 1.0 / 32.0, None, A.mult, None, ["e"], ["E%d" % j], S, [6])
+        else:
+            mm([(b6[:, S * j:S * j + S], T.IE[:], T.e[:], True, True) for j in range(4)], ["IE", "e"], EE, 1792, [6])
+        for i, c in enumerate((2, 3, 0, 1) if PEADD[t] else (0, 1, 2, 3)):
+            bk, bn = ((b7, 7), (b5, 5))[1 if PEADD[t] and not last else c % 2]
+            own = [XA] if c < 2 else X1; other = X1 if c < 2 else [XA]; pk = (448 * c + 896) % K
+            if PEADD[t] and c >= 2:
+                bk, bn, res = ((b2, 2, ["F2", "cnt", "y"]) if last else (b7, 7, ["st0"])) if c == 2 else (b1, 1, ["F1"])
+                pr = ["PR%d" % (2 * c - 4), "PR%d" % (2 * c - 3)]; dd = T.PR[:, 448 * c - 896:448 * c - 448]
+                lst = grp(bk[:, 0:448], [(T.IF[:], x(448 * c, 448)), (T.IF[:], dd)])
+                at(a + ke + (-0.1 if last else 0.1))
+                mm(lst[:1], ["IF", "p4"] + own, res, 1792, [bn])
+                at(a + ks[i])
+                vtt(dd, b6[:, 0:448], x(pk, 448), A.mult, EE + other, pr, 448, [6])
+                mm(lst[1:], ["IF"] + pr + res, ["ad%d" % c], 1792, [bn])
+                act(LOG[:, X0 + 448 * c:X0 + 448 * c + 448], bk[:, 0:448], res + ["ad%d" % c], ["X%d_%d" % (t, c)], 448, [bn])
                 continue
-            vtt(bk[:, 0:448], b6[:, 0:448], x[:, S * pk:S * pk + 448], A.mult, ["E0", "E1", "E2", "E3"] + XX,
-                ["st%d" % (c % 2)] + (["p0", "p1", "p2", "p3", "p4"] if bn == 5 else []), 448, [6, bn])
-            vtt(LOG[:, x0 + 448 * c:x0 + 448 * c + 448], bk[:, 0:448], x[:, 448 * c:448 * c + 448], A.add, ["st%d" % (c % 2)] + XX,
-                ["X%d_%d" % (t, c)], 448, [bn])
-        if t < RO - 1:
-            vcp(T.B[:, :].indirect(nl), LOG[:, a0:a0 + 512], ["nl%d" % t, "A%d_o" % t, "A%d_r" % t], ["Ba", "Bb", "Bd"], CS * 512)
+            at(a + ks[i])
+            st = "st%d" % (bn == 5)
+            vtt(bk[:, 0:448], b6[:, 0:448], x(pk, 448), A.mult, EE + other, [st] + (["p0", "p1", "p2", "p3", "p4"] if bn == 5 else []), 448, [6, bn])
+            at(a + ks[i] + (0.6 if i % 2 == 0 else 0.0))
+            vtt(LOG[:, X0 + 448 * c:X0 + 448 * c + 448], bk[:, 0:448], x(448 * c, 448), A.add, [st] + own, ["X%d_%d" % (t, c)], 448, [bn])
 
-    for t in range(RO):
-        now[0] = "c%d" % t
-        control(t)
-        now[0] = "d%d" % t; now[1] = 0
-        data(t)
-    now[0] = "f"
+    for f, t in ((control, 0), (data, 0), (control, 1), (exchange, 1), (control, 2), (data, 1), (exchange, 2), (control, 3), (data, 2), (exchange, 3), (None, 3), (data, 3)):
+        now[0] = "%s%d" % ("c" if f is control else "d", t)
+        (f or later[0])(t)
+    now[0] = "f"; at(200.0)
     for c in range(8):
-        cp("VS"[c % 2], T.YO[:, 480 * c:480 * c + 480], LOG[:, :].indirect(T.fo[:, 30 * c:30 * c + 30]), logres(RO, False) + ["fo"], ["YO%d" % c], CG * 480)
-        dma("Y", T.yr[:, 480 * c:480 * c + 480], T.YO[:, 480 * c:480 * c + 480], ["YO%d" % c], ["yr%d" % c], 1000.0)
+        yo = TB[:, W + 480 * c:W + 480 * c + 480]
+        cp("VS"[c % 2], yo, LOG[:, :].indirect(T.fo[:, 30 * c:30 * c + 30]), logres(RO, False) + ["fo"], ["YO%d" % c], CG * 480)
+        dma("Y", T.yr[:, 480 * c:480 * c + 480], yo, ["YO%d" % c], ["yr%d" % c], 240)
     return ops
 
 
-def order(ops):
+def order(sets):
+    ops = sets[0]
     n = len(ops); lastw = {}; readers = {}; bank = {}
     for i, o in enumerate(ops):
         d = set()
@@ -521,82 +687,176 @@ def order(ops):
             lastw[w] = i; readers[w] = []
         d.discard(i)
         o["deps"] = d
+    if "seq" in PLAN:
+        return PLAN["seq"]
+    pre = [set(o["deps"]) | set(o.get("after", ())) | set(o.get("behind", ())) for o in ops]
     succ = [[] for _ in range(n)]
-    for i, o in enumerate(ops):
-        o["all"] = set(o["deps"]) | set(o.get("after", ()))
-        for j in o["all"]:
+    for i in range(n):
+        for j in pre[i]:
             succ[j].append(i)
-    pr = [0.0] * n
-    for i in range(n - 1, -1, -1):
-        pr[i] = ops[i]["cost"] + ops[i]["lat"] + max([pr[j] + WAKE for j in succ[i]] + [0.0])
-    def place(bump):
-        busy = {}; fin = [0.0] * n; start = [0.0] * n
-        key = [pr[j] + bump[j] for j in range(n)]; rdy = [0.0] * n
-        left = list(nin); ready = list(roots);
-        while ready:
-            i = ready[0]
-            for j in ready:
-                if key[j] > key[i]:
-                    i = j
-            ready.remove(i)
-            t = rdy[i]; e, c, lat = flat[i]
-            if e:
-                iv = busy.setdefault(e, []); k = len(iv)
-                while k > 0 and iv[k - 1][1] > t:
-                    k -= 1
-                while k < len(iv) and iv[k][0] < t + c:
-                    if iv[k][1] > t:
-                        t = iv[k][1]
-                    k += 1
-                iv.insert(k, (t, t + c))
-            start[i] = t; f = t + c + lat; fin[i] = f
-            for j, wk in out[i]:
-                if f + wk > rdy[j]:
-                    rdy[j] = f + wk
-                left[j] -= 1
-                if left[j] == 0:
-                    ready.append(j)
-        return max(fin), start, fin
-    nin = [len(o["all"]) for o in ops]; roots = [i for i in range(n) if nin[i] == 0]
-    flat = [(o["eng"], o["cost"], o["lat"]) for o in ops]
-    out = [[(j, 0.0 if ops[j]["kind"] == "recv" or ops[i]["kind"] == "rem" or (ops[j]["eng"] == "P" and ops[i]["eng"] == "P") else WAKE)
-            for j in succ[i]] for i in range(n)]
-    if "seq" not in PLAN:
-        x = [SEED]
 
-        def rnd(k):
-            x[0] = (x[0] * 1103515245 + 12345) % 2147483648
-            return (x[0] >> 8) % k
-        first = place([-1e6 if o["tag"][0] == "d" else 0.0 for o in ops])[1]
-        mark = {}
-        for i, o in enumerate(ops):
-            mark.setdefault(o["tag"], first[i])
-        cur = []
-        for i, o in enumerate(ops):
-            tg = o["tag"]; want = first[i]
-            if tg[0] == "d" and int(tg[1]) < RO:
-                t = int(tg[1]); st = o.get("stage", 0)
-                if st == 0 or t == RO - 1:
-                    want = mark["c%dVnl" % t] + 300.0
-                elif st == 1:
-                    want = mark["c%dVam" % (t + 1)]
-                else:
-                    want = mark["c%dVmoff" % (t + 1)] + LEAD
-                want += i
-            cur.append(-want - pr[i])
-        best = place(cur); at = best[0]
-        for it in range(TRIES):
-            bump = list(cur); i = rnd(n); k = (1, 4, 12, 40)[rnd(4)]; d = (rnd(41) - 20) * (100, 400, 1500)[rnd(3)]
-            for j in range(i, min(n, i + 1 + rnd(k))):
-                bump[j] += d
-            res = place(bump)
-            if res[0] <= at + HEAT * (1.0 - it / TRIES) * rnd(100) / 100.0:
-                cur = [-res[1][j] - pr[j] for j in range(n)]; at = res[0]
-                if at < best[0]:
-                    best = res
-        PLAN["seq"] = sorted(range(n), key=lambda i: (best[1][i], i)); PLAN["t"] = best
-    for i, o in enumerate(ops):
-        o["start"] = PLAN["t"][1][i]; o["fin"] = PLAN["t"][2][i]
+    def gap(i, j):
+        return 0.0 if ops[j]["kind"] == "recv" or (ops[j]["eng"] == "P" and ops[i]["eng"] == "P") else WAKE
+    above = [0] * n; ins = []
+    for j in range(n):
+        hard = [i for i in pre[j] if i not in ops[j].get("behind", ())]; far = 0
+        for i in hard:
+            far |= above[i]
+        ins.append([(i, gap(i, j)) for i in hard if not far >> i & 1])
+        above[j] = far | sum(1 << i for i in hard)
+    fls = [[(" VSPGY".index(o["eng"] or " "), o["cost"], o["lat"], o.get("move", 0.0)) for o in st] for st in sets]
+    began = [0.0] * n; why = [-1] * n; tail = [0, 0.0]
+
+    def replay(seq, fl):
+        free = [0.0] * 6; who = [-1] * 7; fin = [0.0] * n; dm = 0.0
+        for i in seq:
+            q, c, lat, mv = fl[i]; t = free[q]; w = who[q]
+            for j, wk in ins[i]:
+                if fin[j] + wk > t:
+                    t = fin[j] + wk; w = j
+            began[i] = t
+            t += c
+            if q:
+                free[q] = t; who[q] = i
+            if mv:
+                t += lat - 600.0
+                if dm > t:
+                    t = dm; w = who[6]
+                dm = t + mv; t = dm + 600.0; who[6] = i
+            fin[i] = t; why[i] = w
+        end = max(fin); tail[0] = fin.index(end); tail[1] = end
+        return end + EARLY * sum(fin) / n
+
+    def judge(seq):
+        return sum(replay(seq, fl) * wt for fl, wt in zip(fls[::-1], WEIGHT[::-1]))
+    turn = [o["turn"] for o in ops]
+    for i in range(n - 1, -1, -1):
+        if turn[i] is None:
+            turn[i] = min([turn[j] for j in succ[i]] + [1e3]) - 0.01
+    busy = {}; last = {}; rdy = [0.0] * n; start = [0.0] * n; left = [len(p) for p in pre]; ready = [i for i in range(n) if not left[i]]
+    while ready:
+        i = min(ready, key=lambda j: (turn[j], j)); ready.remove(i)
+        q, c, lat, mv = fls[0][i]; t = rdy[i]
+        if q:
+            if ops[i]["turn"] is not None:
+                t = max(t, last.get(q, 0.0))
+            iv = busy.setdefault(q, [])
+            for s0, s1 in iv:
+                if s0 < t + c and s1 > t:
+                    t = s1
+            iv.append((t, t + c)); iv.sort()
+            if ops[i]["turn"] is not None:
+                last[q] = t + c
+        start[i] = t
+        for j in succ[i]:
+            rdy[j] = max(rdy[j], t + c + (0.0 if i in ops[j].get("behind", ()) else lat + mv + gap(i, j)))
+            left[j] -= 1
+            if not left[j]:
+                ready.append(j)
+    seq = sorted(range(n), key=lambda i: start[i]); at = judge(seq); best = (at, seq); held = None
+    x = [SEED]
+
+    def rnd(k):
+        x[0] = (x[0] * 1103515245 + 12345) % 2147483648
+        return (x[0] >> 8) % k
+    outs = [[] for _ in range(n)]
+    for j in range(n):
+        for i, wk in ins[j]:
+            outs[i].append((j, wk))
+    mean = [(fls[0][i][0], sum(fl[i][1] * w for fl, w in zip(fls, WEIGHT)), sum((fl[i][2] + fl[i][3]) * w for fl, w in zip(fls, WEIGHT))) for i in range(n)]
+    bh = [list(o.get("behind", ())) for o in ops]; hb = [[j for j in succ[i] if i in bh[j]] for i in range(n)]
+
+    def pack(lst, back):
+        lo = [[] for _ in range(6)]; hi = [[] for _ in range(6)]; end = [0.0] * n; edges = outs if back else ins
+        for i in lst:
+            q, c, lat = mean[i]; t = 0.0
+            for j, wk in edges[i]:
+                f = end[j] + wk + (lat if back else mean[j][2])
+                if f > t:
+                    t = f
+            for j in (hb if back else bh)[i]:
+                if end[j] > t:
+                    t = end[j]
+            if q:
+                a0 = lo[q]; a1 = hi[q]; k = len(a0)
+                while k and a1[k - 1] > t:
+                    k -= 1
+                while k < len(a0) and a0[k] < t + c:
+                    t = a1[k]; k += 1
+                a0.insert(k, t); a1.insert(k, t + c)
+            end[i] = t + c
+        return end
+
+    def lawful(key):
+        key = list(key)
+        for j in range(n):
+            for i in pre[j]:
+                if key[i] > key[j]:
+                    key[j] = key[i]
+        return sorted(range(n), key=lambda j: key[j])
+    replay(seq, fls[0]); cur = list(began)
+    for late in LATE:
+        end = pack(lawful([turn[j] + (late if ops[j]["tag"][0] == "d" else 0.0) for j in range(n)]), False)
+        for again in range(3):
+            st = [end[j] - mean[j][1] for j in range(n)]
+            cand = lawful(st); val = judge(cand)
+            if val < at:
+                cur = st; at = val; best = (at, cand)
+            end = pack(sorted(range(n), key=lambda j: (-end[j] - mean[j][2], -j)), True)
+            end = pack(lawful([-e for e in end]), False)
+    for it in range(PASSES):
+        key = list(cur); i = rnd(n); d = (rnd(41) - 20) * (50, 200, 800)[rnd(3)]
+        for j in range(i, min(n, i + 1 + rnd((1, 4, 12, 40)[rnd(4)]))):
+            key[j] += d
+        end = pack(lawful(key), False)
+        if rnd(3) == 0:
+            end = pack(sorted(range(n), key=lambda j: (-end[j] - mean[j][2], -j)), True)
+            end = pack(lawful([-e for e in end]), False)
+        st = [end[j] - mean[j][1] for j in range(n)]
+        cand = lawful(st); val = judge(cand)
+        if val <= at + 3.0 * HEAT * (1.0 - it / PASSES) * rnd(100) / 100.0:
+            cur = st; at = val
+            if at < best[0]:
+                best = (at, cand)
+    at, seq = best
+    for it in range(MOVES):
+        if held is None:
+            held = []; pos = {j: k for k, j in enumerate(seq)}
+            for fl in fls[::-1]:
+                replay(seq, fl); j = tail[0]
+                while why[j] >= 0:
+                    if why[j] not in pre[j]:
+                        held.append((pos[why[j]], pos[j]))
+                    j = why[j]
+            every = [(pos[why[j]], pos[j]) for j in range(n) if why[j] >= 0 and why[j] not in pre[j]]
+        pick = held if rnd(2) else every
+        lo, hi = pick[rnd(len(pick))]; ln = hi - lo + (0, 0, rnd(10), rnd(60))[rnd(4)]
+        if rnd(2):
+            win = seq[lo:lo + ln + 1]; moved = {win[0]}
+            for j in win[1:]:
+                if not moved.isdisjoint(pre[j]):
+                    moved.add(j)
+            new = [j for j in win if j not in moved] + [j for j in win if j in moved]
+        else:
+            lo = max(0, hi - ln); win = seq[lo:hi + 1]; need = set(pre[win[-1]]); moved = {win[-1]}
+            for j in win[-2::-1]:
+                if j in need:
+                    moved.add(j); need.update(pre[j])
+            new = [j for j in win if j in moved] + [j for j in win if j not in moved]
+        cand = seq[:lo] + new + seq[lo + len(win):]
+        val = judge(cand)
+        if val <= at + HEAT * (1.0 - it / MOVES) * rnd(100) / 100.0:
+            seq = sorted(cand, key=lambda j: began[j]); held = None
+            at = val if seq == cand else judge(seq)
+            if at < best[0]:
+                best = (at, seq)
+    PLAN["seq"] = best[1]; PLAN["t"] = [replay(best[1], fl) * 0 + tail[1] for fl in fls]
+    PLAN["path"] = []
+    for fl in fls:
+        replay(best[1], fl); j = tail[0]; p = []
+        while j >= 0:
+            p.append((round(began[j]), ops[j]["tag"], why[j] in pre[j])); j = why[j]
+        PLAN["path"].append(p[::-1])
     return PLAN["seq"]
 
 
@@ -604,8 +864,8 @@ def rank_program(g, core, T, topo):
     rank = T.rank_of(core)
     if rank is None:
         return
-    ops = build(g, T, topo, rank)
-    seq = order(ops)
+    sets = [build(g, T, topo, rank, pace) for pace in PACES]
+    seq = order(sets); ops = sets[0]
     Q = {"V": g.vector, "S": g.scalar, "P": g.tensor, "G": g, "Y": g.sync}
     need = set()
     for o in ops:

from concourse.bass import DstId, RemoteDMATransfer
from concourse.mybir import AluOpType as A, ActivationFunctionType as AF

N, W, M, K, S, RO = 4, 3840, 960, 1792, 112, 4
SEG = 4096
L0 = 2 * W - 512
NLOG = L0 + RO * SEG
F32, BF, I32, U16 = "float32", "bfloat16", "int32", "uint16"


def _sb(shape, dtype):
    return ("sbuf", [128] + list(shape), dtype)


SCRATCH = {
    "bt32": _sb([896], I32), "bto": _sb([896], U16), "lag32": _sb([240], I32), "ac": _sb([240], F32), "a0": _sb([240], BF),
    "cap": _sb([240], BF), "tk": _sb([240], F32), "gr": _sb([240], F32), "FL": _sb([720], BF),
    "dW": ("dram", [8, W], F32), "EB": _sb([N, M], BF),
    "TB0": _sb([W], BF), "TB": _sb([2 * W], F32), "LS": _sb([K + 512], F32), "DEF": _sb([512], F32), "rep": _sb([2 * K], BF),
    "IF": _sb([128], F32), "IE": _sb([128], F32), "I2": _sb([128], F32), "big": _sb([128], BF), "zer": _sb([128], BF), "VB": _sb([192], BF),
    "dig": _sb([512], BF), "iop": _sb([128], I32), "iop2": _sb([256], I32), "iob": _sb([128], I32),
    "BO": _sb([128], F32), "BC": _sb([8], F32), "bci": _sb([8], F32), "bct": _sb([8], F32),
    "rowf": _sb([2], F32), "hoff": _sb([32], F32), "hcap": _sb([32], F32), "hv1": _sb([32], F32), "nl16": _sb([32], U16), "cix": _sb([S], F32), "DR": _sb([RO * S + S], BF),
    "one": _sb([128], BF), "neg": _sb([128], BF), "IB": _sb([128], BF), "I64": _sb([128], BF), "I128": _sb([128], BF),
    "IW": _sb([128], BF), "NU": _sb([128], BF), "RR": _sb([4 * S], BF), "SB": _sb([128], BF), "SX": _sb([96], BF),
    "MM": _sb([512], BF), "MF": _sb([512], F32), "sgm": _sb([512], BF),
    "PAYC": _sb([128, 16], BF), "PAY": _sb([K], F32), "DYN": _sb([768], BF),
    "am": _sb([256], BF), "sc": _sb([128], F32), "sel": _sb([128], BF), "best": _sb([128], F32),
    "nhd": _sb([128], BF), "tq": _sb([768], BF), "key": _sb([128], BF),
    "mk": _sb([512], BF), "scn": _sb([512], BF), "u": _sb([512], BF), "t1": _sb([512], BF),
    "nB": _sb([S], F32), "o1": _sb([S], F32), "o2": _sb([S], F32), "co": _sb([S], F32), "xo": _sb([128], F32), "xv": _sb([128], F32),
    "moff": _sb([S], U16), "coff": _sb([S], U16), "xoff": _sb([RO * S], U16),
    "VT": _sb([32, 16], F32), "n0": _sb([32], F32), "c1": _sb([32], F32), "bz": _sb([32], F32), "lb": _sb([64], F32),
    "lb16": _sb([RO * 64], U16), "HL": _sb([RO * 32], U16),
    "LOG": _sb([NLOG], F32), "H": _sb([M + 128], F32),
    "PO": _sb([12, 136], F32), "PL": _sb([9, 136], F32), "AO": _sb([9 * 128], F32), "ht": _sb([512], F32),
    "PR": _sb([K // 2], F32), "e": _sb([S], F32), "tgf": _sb([448], F32), "nmc": _sb([240], F32), "fo": _sb([240], U16),
}
for _b in range(8):
    SCRATCH["b%d" % _b] = ("psum", [128, 512], F32)
NDMA = 64
SEMAPHORES = (["cV", "cS", "cP", "cG", "ls"] + ["d%d" % i for i in range(NDMA)] + ["rG%d_%d" % (t, r) for t in range(3) for r in range(N)]
              + ["rE"] + ["rA%d" % t for t in range(1, RO)] + ["rP%d_%d" % (t, j) for t in range(1, RO) for j in range(3)])

OFF, UNIT, SAT = 32, 2.0 ** -13, 20.0
BOTH = 65 * OFF
PRAW = 4097
YB = 20224
HALF = 2 * (YB + 128) + 384

KS, PAYE, L1E, SMALL, PEADD = (8, 8, 8, 8), ("SVVV", "SVVV", "SVVV", "SVSS"), "VVVV", "VSSSSV", (0, 0, 0, 1)
C1E, C2E, GBE = ("SSSS", "SSSS", "SSSS"), ("", "VVVV", "VSSS", "SSSS"), "SSV"
XG, BGE, AOE = ("VS", "VV", "VV", "SV"), "S", "SSS"
C1K = ((9.0, 10.4, 11.8, 13.2),) * 3
C2K = ((), (10.7, 12.1, 13.5, 15.0), (10.7, 15.0, 16.5, 18.0), (10.0, 11.4, 12.8, 14.2))
LISTK = (0, 16.6, 19.5, 15.7)
DATAK = ((0, 0, (), 0, 14.0, 16.5, 15.0, 17.0, (18.0, 19.5, 20.1, 21.0)),
         (18.5, 19.2, (21.5, 24.9, 26.2), 26.6, 36.2, 37.5, 38.9, 38.7, (40.5, 41.4, 42.3, 44.2)),
         (22.0, 23.0, (26.55, 27.75, 28.55), 29.0, 34.2, 35.5, 36.9, 36.9, (38.0, 38.9, 39.75, 39.9)),
         (19.0, 21.0, (23.0, 23.8, 24.6), 25.0, 29.0, 29.5, 30.5, 31.0, (32.0, 32.5, 33.0, 33.5)))
FIX, WAKE = 55.0, 60.0
PACES = ((0.9, 1.5, 3.4, 0.48, 1.9, 4.5, 1600.0, 2100.0), (0.83, 1.2, 2.0, 0.42, 3.0, 9.0, 1800.0, 2400.0), (1.1, 1.9, 5.5, 0.55, 2.3, 6.0, 1800.0, 2400.0))
EARLY, PASSES, LATE = 0.2, 3000, (0.0, 3.0, 6.0, 12.0, 24.0, 48.0)
MOVES, HEAT, WEIGHT, SEED = 25000, 60.0, (0.4, 0.3, 0.3), 12
PLAN = {}


def build(g, T, topo, rank, pace):
    CY, CG, CS, PECY, LKB, RKB, DMA_T, REM_T = pace
    ops = []; now = ["s", None]
    V, SC, PE = g.vector, g.scalar, g.tensor
    me = T.cores[rank]

    def at(k):
        now[1] = k

    def op(eng, fn, r, w, cost, banks=(), lat=0.0, kind="c", **kw):
        d = {"eng": eng, "fn": fn, "r": list(r), "w": list(w), "cost": cost, "banks": list(banks), "lat": lat, "kind": kind}
        d.update(kw)
        d["turn"] = now[1]
        d["tag"] = now[0] + str(eng) + "".join(ch for ch in (list(w) or list(r))[-1] if not ch.isdigit())
        ops.append(d)
        return len(ops) - 1

    def vtt(out, a, b, o, r, w, cyc, banks=()):
        op("V", lambda: V.tensor_tensor(out, a, b, o), r, w, FIX + CY * max(cyc, 64), banks)

    def vts(out, a, s1, s2, o0, o1, r, w, cyc, banks=()):
        if o1 is None:
            op("V", lambda: V.tensor_scalar(out, a, s1, None, o0), r, w, FIX + CY * max(cyc, 64), banks)
        else:
            op("V", lambda: V.tensor_scalar(out, a, s1, s2, o0, o1), r, w, FIX + CY * max(cyc, 64), banks)

    def vcp(out, a, r, w, cyc, banks=()):
        op("V", lambda: V.tensor_copy(out, a), r, w, FIX + CY * max(cyc, 64), banks)

    def vms(ap, c, w, cyc):
        op("V", lambda: V.memset(ap, c), [], w, FIX + CY * max(cyc, 64))

    def act(out, a, r, w, cyc, banks=(), f=AF.Identity, bias=0.0, scale=1.0, extra=0.0):
        kw = {}
        if not (isinstance(bias, float) and bias == 0.0):
            kw["bias"] = bias
        if not (isinstance(scale, float) and scale == 1.0):
            kw["scale"] = scale
        op("S", lambda: SC.activation(out, a, f, **kw), r, w, FIX + extra + CY * max(cyc, 64), banks)

    def cp(eng, out, a, r, w, cyc, banks=()):
        if eng == "V":
            vcp(out, a, r, w, cyc, banks)
        else:
            act(out, a, r, w, cyc, banks)

    def shifted(eng, out, a, c, r, w, cyc, banks):
        if eng == "V":
            vts(out, a, float(c), None, A.add, None, r, w, cyc, banks)
        else:
            act(out, a, r, w, cyc, banks, f=AF.Copy, bias=float(c))

    def mm(lst, r, w, cyc, banks):
        def fn():
            ins = None
            for (o, l, rh, st, sp) in lst:
                ins = PE.matmul(o, l, rh, st, sp)
            return ins
        op("P", fn, r, w, 40.0 + PECY * cyc, banks)

    def grp(o, prs):
        return [(o, l, rh, i == 0, i == len(prs) - 1) for i, (l, rh) in enumerate(prs)]

    def dma(q, out, a, r, w, kb, behind=()):
        e = {"Y": g.sync, "S": g.scalar, "G": g}[q]
        return op(q, lambda: e.dma_start(out, a), r, w, 1000.0 if q == "G" else 80.0, lat=DMA_T, kind="dma", move=LKB * kb, behind=behind)

    def iota(out, pat, base, cm, w, n, flag=False):
        if flag:
            op("G", lambda: g.iota(out, pat, base, cm, allow_small_or_imprecise_dtypes=True), [], w, 130 + 2 * CY * n)
        else:
            op("G", lambda: g.iota(out, pat, base, cm), [], w, 130 + 2 * CY * n)

    def asel(out, a, pat, cmp, base, cm, r, w, n, fill=0.0):
        op("G", lambda: g.affine_select(out, a, pat, cmp, fill, base, cm), r, w, 170 + 2 * CY * n)

    def diag(out, n, c, w):
        asel(out, T.zer[:, 0:n], [[-1, n]], A.not_equal, 0, 1, ["zer"], w, n, float(c))

    peers = [(rank + j) % N for j in range(1, N)]

    def slot(src, dst):
        return (src - dst) % N - 1

    def dst_id(r):
        a = topo.addr(T.cores[r])
        return DstId(rid=a[0], pnc=a[1])

    def send1(r, out, a, sem, rd, wr=()):
        ad = topo.addr(T.cores[r]); mk = topo.mask(me, T.cores[r]); n = len(topo.engines(me, T.cores[r]))
        return op("G", lambda: g.remote_dma(out, a, T.sem[sem], T.sem.ls, ad[1], ad[0], mk), rd, wr, 500.0, kind="rem", ls=n,
                  lat=REM_T, move=RKB * 68), n

    def send_all(outs, a, sem, rd, kb, first=0.0):
        es = [e for e in topo.engines(me, T.cores[peers[0]]) if all(e in topo.engines(me, T.cores[r]) for r in peers)]
        tr = RemoteDMATransfer(dst_ids=[dst_id(r) for r in peers], dma_engine_mask=sum(1 << e for e in es), remote_sem=T.sem[sem],
                               src=a, dsts=outs)
        return op("G", lambda: g.remote_dma_fused([tr], local_sem=T.sem.ls), rd, [], 500.0 + first, kind="rem", ls=len(es),
                  lat=REM_T, move=RKB * 3 * kb), len(es)

    def recv(sem, cnt, after, w):
        op(None, None, [], w, 0.0, kind="recv", sem=sem, cnt=cnt, after=after)

    TB, LOG, PAYC, LS = T.TB, T.LOG, T.PAYC, T.LS
    b0, b1, b2, b3, b4, b5, b6, b7 = [T["b%d" % i] for i in range(8)]
    TB1 = ["TBw", "TBa", "TBp", "TBq", "TBn", "TBm", "TBo"]; TB2 = ["TCp", "TCg"]

    def prow(r):
        return PAYC[0:S, r::16, :]

    dma("Y", T.lag32[:], T.lag[:], [], ["lag32"], 120)
    dma("S", T.bt32[:, 0:224], T.bt[:, 0:224], [], ["bt32"], 112)
    dma("Y", T.EB[:, rank], T.e0[:, rank * M:(rank + 1) * M], [], ["EBo"], 240)
    T0 = T.TB0; T0N = ["T0w", "T0a", "T04", "T05", "T0o"]
    ZS = ["PR0", "PR1", "PR2"]
    at(-5.0)
    vms(T.PR[:, 0:480], 0.0, ZS, 480)
    for c in range(8):
        at(-4.0 + 0.5 * c if c < 4 else 2.7 + 0.5 * c)
        act(TB[:, 480 * c:480 * c + 480], T.PR[:, 0:480], ZS, ["TBz%d" % c], 480, f=AF.Tanh, extra=1300.0 * (c == 0))
    at(None)
    vms(T0[:], 0.0, T0N, W // 2)
    iota(T.iop2[:, 2:3], [[0, 1]], 0, 1, ["iop2b"], 1)
    iota(T.ht[:, 0:256], [[1, 4], [0, 64]], OFF, 4, ["ht0", "ht1"], 256, True)
    iota(T.dig[:, 256:512], [[0, 4], [1, 64]], OFF, 0, ["digl"], 256, True)
    iota(T.iob[:], [[1, 128]], 128, -1, ["iob"], 128)
    vms(T.one[:], 1.0, ["one"], 64)
    vms(T.neg[:], -1.0, ["neg"], 64)
    vms(T.zer[:], 0.0, ["zer"], 64)
    asel(T.SB[:], T.one[:], [[-1, 16], [-16, 8]], A.is_equal, 0, 1, ["one"], ["SB"], 128)
    vts(T.iop2[:, 0:1], T.iop2[:, 2:3], 1.0 / 15.0, -7.0 / 15.0, A.mult, A.add, ["iop2b"], ["iop2a"], 1)
    vts(T.bct[:, 0:1], T.iop2[:, 0:1], -60.0 * UNIT, None, A.mult, None, ["iop2a"], ["bct0"], 1)
    act(T.dig[:, 0:256], T.ht[:, 0:256], ["ht0", "ht1", "bct0"], ["digh"], 256, bias=T.bct[:, 0:1], scale=UNIT)
    act(T.dig[:, 256:512], T.dig[:, 256:512], ["digl"], ["digl"], 256, scale=UNIT)
    vcp(T.a0[:], T.lag32[:], ["lag32"], ["a0"], 240)
    early = [dma("Y", T0[0::16, :], T.wt[:], [], ["T0w"], 60), dma("Y", T0[1::16, :], T.a0[:], ["a0"], ["T0a"], 80),
             dma("Y", T0[4::16, :], T.dig[0:120, 0:256], ["digh"], ["T04"], 80), dma("Y", T0[5::16, :], T.dig[0:120, 256:512], ["digl"], ["T05"], 80)]
    vcp(T.bto[:, 0:224], T.bt32[:, 0:224], ["bt32"], ["bto0"], 224)
    act(T.ac[:], T.a0[:], ["a0"], ["ac"], 240)
    vts(T.iop2[:, 128:256], T.iob[:], 15, None, A.bitwise_and, None, ["iob"], ["iopd"], 128)
    vts(T.BO[:], T.iop2[:, 128:256], 0.0, None, A.is_equal, None, ["iopd"], ["BO"], 128)
    vts(T.iop2[:, 4:5], T.iop2[:, 2:3], 15, None, A.bitwise_and, None, ["iop2b"], ["iop2c"], 1)
    vcp(T.rowf[:, 0:1], T.iop2[:, 4:5], ["iop2c"], ["rowf"], 1)
    diag(T.IB[:], 128, 1, ["IB"])
    asel(T.NU[:], T.neg[:], [[-1, 128]], A.is_gt, 0, 1, ["neg"], ["NU"], 128)
    asel(T.NU[:], T.NU[:], [[-1, 128]], A.not_equal, 0, 1, ["NU"], ["NU"], 128, -256.0)
    act(T.IF[:], T.IB[:], ["IB"], ["IF"], 128)
    act(T.IE[:], T.IB[:], ["IB"], ["IE"], 128, scale=1.0 / 32.0)
    act(T.I2[:], T.IB[:], ["IB"], ["I2"], 128, scale=2.0)
    act(T.SX[:, 0:32], T.SB[:, 16:48], ["SB"], ["SXa"], 32, scale=1.0 / UNIT)
    act(T.SX[:, 32:64], T.SB[:, 16:48], ["SB"], ["SXb"], 32, scale=-1.0 / UNIT)
    act(T.SX[:, 64:80], T.SB[:, 64:80], ["SB"], ["SXc"], 16, scale=1.0 / UNIT)
    act(T.SX[:, 80:96], T.SB[:, 64:80], ["SB"], ["SXd"], 16, scale=-1.0 / UNIT)
    diag(T.I64[:], 128, 64, ["I64"])
    diag(T.IW[:], 128, W // 2, ["IW"])
    diag(T.I128[:], 128, 128, ["I128"])
    for h in range(4):
        diag(T.RR[:, S * h:S * h + S], S, (YB + 128 + 128 * h) // 2, ["RR%d" % h])
    RRS = ["RR%d" % h for h in range(4)]
    iota(T.DR[0:1, 0:RO * S], [[-SEG, RO], [0, S]], 0, 0, ["DR"], RO * S, True)
    vms(T.DR[0:1, RO * S:RO * S + S], float(YB + 1 - L0 - PRAW - HALF), ["DR2"], 64)
    vms(T.sgm[:], 1.0, ["sgm"], 256)
    vms(T.sgm[:, 0::16], 0.0, ["sgm"], 32)
    PCS = ["pc%d" % r for r in range(2, 10)]
    vms(PAYC[:], 0.0, PCS, 1024)
    iota(T.iop[:], [[0, 8], [S, 16]], L0 + 512 + K + PRAW - 129 * OFF, 1, ["iop"], 128)
    vts(T.iop2[:, 128:256], T.iop[:], 7, None, A.arith_shift_right, None, ["iop"], ["iopd"], 128)
    vts(prow(2), T.iop2[0:S, 128:256], float(OFF), None, A.add, None, ["iopd"], ["pc2"], 128)
    vts(T.iop2[:, 128:256], T.iop[:], 127, None, A.bitwise_and, None, ["iop"], ["iopd"], 128)
    vts(prow(3), T.iop2[0:S, 128:256], float(OFF), None, A.add, None, ["iopd"], ["pc3"], 128)
    iota(T.bci[:, 0:4], [[SEG // 128, 4]], 0, 0, ["bci"], 4, True)
    vts(T.bct[:, 4:8], T.bci[:, 0:4], T.BO[:, 2:3], UNIT, A.mult, A.mult, ["bci", "BO"], ["bct1"], 4)
    act(T.bci[:, 4:8], T.BO[:, 10:14], ["BO"], ["bci2"], 4, scale=SAT)
    vtt(T.BC[:, 0:4], T.bci[:, 4:8], T.bct[:, 4:8], A.add, ["bci2", "bct1"], ["BC"], 8)
    act(T.BC[:, 4:5], T.BO[:, 4:5], ["BO"], ["BC4"], 1, scale=UNIT * (W // 64))
    iota(T.hcap[:], [[0, 4], [16, 8]], M, 0, ["hcap"], 32, True)
    vts(T.hcap[:], T.hcap[:], T.rowf[:, 0:1], None, A.add, None, ["hcap", "rowf"], ["hcap"], 32)
    vms(T.big[:], 1.0 / UNIT, ["big"], 64)
    for c, v, nm in ((5, -127.5, "c128"), (6, 4.0e6, "c4"), (7, 130.0 - (7.0 + OFF) / 15.0, "c130")):
        vms(T.BC[:, c:c + 1], v, [nm], 1)
    iota(T.hoff[:], [[M, 4], [0, 8]], BOTH, 0, ["hoff"], 32, True)
    iota(T.cix[:], [[16, S]], YB + 1 - K - HALF, 0, ["cix"], S, True)
    vts(T.cix[:], T.cix[:], T.rowf[:, 0:1], None, A.add, None, ["cix", "rowf"], ["cix"], S)
    for xh in range(2):
        for e in range(2):
            c = 128 * (2 * xh + e)
            asel(T.MM[:, c:c + 128], T.big[:], [[-32, 4], [1000 - 16, 2], [-1, 16]], A.is_equal, 16 * (e - xh) - 1000 * e, 1,
                 ["big"], ["MM%d" % (2 * xh + e)], 128)
    MM1 = ["MM0", "MM1", "MM2", "MM3"]
    vms(T.xo[:, S:128], 0.0, ["xop"], 16)
    vms(T.H[:, M:M + 128], 0.0, ["Hd"], 128)
    iota(T.nmc[:], [[1, 240]], PRAW, 0, ["nmc"], 240, True)
    act(T.rowf[:, 1:2], T.rowf[:, 0:1], ["rowf"], ["rowu"], 1, scale=240.0 * UNIT)
    act(T.nmc[:], T.nmc[:], ["nmc", "rowu"], ["nmc"], 240, bias=T.rowf[:, 1:2], scale=UNIT)
    DEFS = ["DEF"]

    def mm_big(k, c):
        return T.EB[:, peers[k], c:c + 128]

    def loads():
        at(1.0)
        d = dma("Y", TB[2::8, W:2 * W], T.PR[:, 0:480], ZS + ["bto0"], ["TCp", "TCg"], 240, early)
        d = dma("Y", TB[12::16, W:2 * W], T.PR[:, 0:240], ZS, ["TCg2"], 120, [d])
        dma("Y", TB[3::8, W:2 * W], T.PR[:, 0:480], ZS, ["TCp2", "zr"], 240, [d])
        dma("Y", T.bt32[:, 224:896], T.bt[:, 224:896], ["gate0"], ["bt32b"], 336)
        dma("Y", T.t1[0:16, 0:448], T.tg[:], ["gate0"], ["t1"], 14)
        at(2.0)
        s0, n0 = send_all([T.EB[:, rank] for r in peers], T.EB[:, rank], "rE", ["EBo", "IW", "I64", "NU", "zr"], 240, 2500.0)
        recv("rE", 3 * n0, [s0], ["EBr"])
        dma("G", LOG[:, 0:W], T.e0[:], ["zr"], ["L0"], 1920)
        dma("G", T.dW[:], T.wt[:], ["zr"], ["dW"], 120)
        at(5.0)
        act(LS[:, 0:512], T.dig[:], ["digh", "digl"], ["LS"], 512)
        at(14.8)
        act(T.DEF[:], T0[:, 0:512], T0N + ["BC4"], DEFS, 512, bias=T.BC[:, 4:5])
        at(9.6)
        vts(T.MF[:], T.MM[:, 0:512], UNIT, None, A.mult, None, MM1, ["MF"], 512)
        at(10.5)
        vcp(T.bto[:, 224:896], T.bt32[:, 224:896], ["bt32b"], ["bto1", "bto2", "bto3"], 672)
        vts(T.tgf[0:16, :], T.t1[0:16, 0:448], -128.0, None, A.mult, None, ["t1"], ["tgf"], 448)
        for h in range(N):
            cp(L1E[h], LOG[:, W + M * h:W + M * h + M], T.EB[:, h], ["EBo", "EBr"], ["L1%d" % h], M)
        at(17.5)
        act(T.H[:, 0:M], T.EB[:, rank], ["EBo"], ["H"], M)
        act(T.EB[:, peers[0], 0:512], T.MM[:], MM1, ["EBr", "MM4"], 512, scale=64.0)
        act(T.EB[:, peers[1], 0:512], T.MM[:], MM1, ["EBr", "MM5"], 512, scale=128.0)

    def logres(t, ans, stepped=True):
        r = ["L0"] + ["L1%d" % h for h in range(N)]
        for u in range(t):
            r += (["A%d_%s" % (u, h) for h in ("o", "r") if u] + ["X%d_%d" % (u, c) for c in range(4) if stepped or u < t - 1]
                  + ["x%d_%d" % (u, c) for c in range(5)])
        if ans and t:
            r += ["A%d_o" % t, "A%d_r" % t]
        return r

    later = []

    def control(t):
        last = t == RO - 1; a = 24.0 * t
        pieces = [(s, hf, u, k0, k1) for s in range(2) for hf, (lo, hi) in enumerate(((0, KS[t]), (KS[t], 16)))
                  for u, (k0, k1) in enumerate(((lo, hi - 2), (hi - 2, hi)) if s else ((lo, hi),))]
        for s, hf, u, k0, k1 in pieces:
            c = 224 * t + S * s + 7 * k0; o = K * s + S * k0; nk = k1 - k0
            at(a + (0.0, 1.3, 2.3)[s + u])
            cp("SV"[hf], T.rep[:, o:o + S * nk], (TB if t else T0)[:, 0:W].indirect(T.bto[:, c:c + 7 * nk]),
               (TB1 if t else T0N) + ["bto%d" % t], ["rep%d%d" % (s + u, hf)] + (["gate%d" % t] if (s, hf) == (0, 0) else []), CG * S * nk)
        if t == 0:
            loads()
        else:
            at(a + 1.0)
            if last:
                dma("Y", TB[:, W + 512:W + 1024], T.DEF[:], DEFS + ["gate%d" % t], TB2 + ["LS"], 256)
            else:
                dma("Y", LS[:, K:K + 512], T.DEF[:], DEFS + ["gate%d" % t], ["LS"], 256)

        def ch(s, k):
            return T.rep[:, K * s + S * k:K * s + S * k + S]
        for s, hf, u, k0, k1 in pieces:
            at(a + (1.3, 2.3, 2.5)[s + u])
            mm([(b0[0:S, 256 * s + k:256 * s + 256:16], ch(s, k), T.SB[:, 0:16], True, True) for k in range(k0, k1)],
               ["rep%d%d" % (s + u, hf), "SB"], ["F0_%d%d" % (s + u, hf)], 64 * (k1 - k0), [0])
        F0 = ["F0_00", "F0_01", "F0_10", "F0_11", "F0_20", "F0_21"]
        REP0 = ["rep00", "rep01"]; REP = REP0 + ["rep10", "rep11", "rep20", "rep21"]
        at(a + 1.4)
        mm([(b1[0:S, k::16], ch(0, k), T.SX[:, 0:32], True, True) for k in range(16)], REP0 + ["SXa"], ["F1"], 1024, [1])
        at(a + 2.6)
        lst = []
        for k in range(16):
            lst += grp(b2[0:S, k::16], [(ch(1, k), T.SX[:, 0:32]), (ch(0, k), T.SX[:, 32:64])])
        mm(lst, REP + ["SXa", "SXb"], ["F2"], 2048, [2])
        if t > 0:
            at(a + 2.65)
            mm([(b3[0:S, k:256:16], ch(0, k), T.SX[:, 64:80], True, True) for k in range(16)], REP0 + ["SXc"], ["G1", "Tn", "Tp"], 1024, [3])
            at(a + 2.7)
            lst = []
            for k in range(16):
                lst += grp(b3[0:S, 256 + k:512:16], [(ch(1, k), T.SX[:, 64:80]), (ch(0, k), T.SX[:, 80:96])])
            mm(lst, REP + ["SXc", "SXd"], ["G2", "Tp"], 2048, [3])
        at(a + 2.6)
        cp(SMALL[0], T.am[0:S, :], b0[0:S, 128:384], F0, ["am"], 256, [0])
        vtt(T.sc[0:S, :], b0[0:S, 0:128], T.am[0:S, 0:128], A.mult, F0 + ["am"], ["sc"], 128, [0])
        vtt(b0[0:S, 384:512], b0[0:S, 384:512], T.am[0:S, 128:256], A.mult, F0 + ["am"], ["sc1"], 128, [0])
        vtt(T.best[0:S, :], b0[0:S, 384:512], T.sc[0:S, :], A.max, ["sc", "sc1"], ["best"], 128, [0])
        vtt(T.sel[0:S, :], b0[0:S, 384:512], T.sc[0:S, :], A.is_gt, ["sc", "sc1"], ["sel"], 128, [0])
        at(a + 3.6)
        if SMALL[1] == "V":
            vts(b0[0:S, 0:128], T.best[0:S, :], 4.0, -1000.0, A.is_lt, A.mult, ["best", "sc"], ["nd"], 128, [0])
        else:
            act(b0[0:S, 0:128], T.best[0:S, :], ["best", "sc", "c4"], ["nd"], 128, [0], f=AF.Relu, scale=-1.0e6, bias=T.BC[0:S, 6:7])
        picks = [(2, 4, 3.7, 3.8, 4.2), (3, 5, 3.9, 5.3, 5.4)]
        if t:
            picks += [(0, 6, 4.0, 5.5, 15.2), (1, 7, 4.1, 5.6, 15.2), (4, 8, 5.4, 5.8, 15.2), (5, 9, 5.7, 5.9, 15.2)]
        for q, r, k1, k2, k3 in picks:
            c = 128 * (q % 4); at(a + k1)
            vtt(T.tq[0:S, 128 * q:128 * q + 128], b2[0:S, c:c + 128] if q < 4 else b3[0:S, 256 + c:384 + c], T.sel[0:S, :], A.mult,
                ["F2" if q < 4 else "G2", "sel"], ["tq%d" % q], 128, [2 if q < 4 else 3])
        for q, r, k1, k2, k3 in picks:
            c = 128 * (q % 4); at(a + k2)
            vtt(prow(r), (b1 if q < 4 else b3)[0:S, c:c + 128], T.tq[0:S, 128 * q:128 * q + 128], A.add, ["F1" if q < 4 else "G1", "tq%d" % q],
                ["pc%d" % r], 128, [1 if q < 4 else 3])
            at(a + (min(k3, 6.0) if t in (1, RO - 1) else k3))
            act(T.DYN[0:S, 128 * q:128 * q + 128], prow(r), ["pc%d" % r], ["DYN%d" % q], 128)
        at(a + 4.05)
        if SMALL[2] == "V":
            vts(T.nhd[0:S, :], prow(4), 1.0 / 15.0, 130.0 - (7.0 + OFF) / 15.0, A.mult, A.add, ["pc4"], ["nhd"], 64)
        else:
            act(T.nhd[0:S, :], prow(4), ["pc4", "c130"], ["nhd"], 128, scale=1.0 / 15.0, bias=T.BC[0:S, 7:8])
        at(a + 4.3)
        vtt(T.key[0:S, :], b0[0:S, 0:128], T.nhd[0:S, :], A.add, ["nhd", "nd"], ["key"], 128, [0])
        for h in range(4):
            vts(T.mk[0:S, 128 * h:128 * h + 128], T.key[0:S, :], 130.0 + h, None, A.is_equal, None, ["key"], ["mk%d" % h], 64)
        MK = ["mk0", "mk1", "mk2", "mk3"]
        op("V", lambda: V.tensor_tensor_scan(T.scn[0:S, :], T.sgm[0:S, :], T.mk[0:S, :], 0.0, A.mult, A.add), MK + ["sgm"], ["scn"], FIX + CY * 256)
        lst = grp(b2[0:S, :], [(T.NU[0:S, 0:S], T.mk[0:S, :]), (T.one[0:S, 0:S], T.scn[0:S, :])])
        mm(lst[:1], MK + ["NU"], ["F2"], 512, [2])
        mm(lst[1:], ["scn", "one", "F2"], ["cnt"], 512, [2])
        at(a + 6.0)
        act(T.u[0:S, :], b2[0:S, :], ["cnt", "c128"], ["u"], 512, [2], f=AF.Sign, scale=-1.0, bias=T.BC[0:S, 5:6])
        nm = [(T.DYN[0:S, 256:384], T.I64[0:S, 0:S]), (T.DYN[0:S, 384:512], T.IB[0:S, 0:S])]
        if not last:
            at(a + 7.0)
            lst = grp(b4[:, 0:S], nm + [(T.u[0:S, 128 * h:128 * h + 128], T.IW[0:S, 0:S]) for h in range(4)])
            mm(lst, ["DYN2", "DYN3", "I64", "IB", "IW", "u"], ["m1"], 6 * S, [4])
            vts(T.moff[:], b4[:, 0:S], float(2 * W - BOTH), None, A.add, None, ["m1"], ["moff"], S, [4])
        if t > 0:
            at(a + (6.5 if last else 8.0))
            vts(T.t1[0:S, :], b2[0:S, :], 128.0, 0.0, A.add, A.min, ["cnt"], ["t1"], 512, [2])
            at(a + (7.0 if last else 8.5))
            mm(grp(b2[:, 0:S], [(T.u[0:S, 128 * h:128 * h + 128], T.RR[0:S, S * h:S * h + S]) for h in range(4)]
                   + [(T.t1[0:S, 128 * h:128 * h + 128], T.IB[0:S, 0:S]) for h in range(4)]), ["u", "t1", "IB"] + RRS, ["F2", "cnt", "y"], 8 * S, [2])
            if last:
                at(a + 6.8)
                mm(grp(b3[:, 0:S], nm), ["DYN2", "DYN3", "I64", "IB"], ["G1", "Tn"], 2 * S, [3])
                act(T.cix[:], b3[:, 0:S], ["Tn"], ["cix"], S, [3], f=AF.Copy, bias=float(YB + 1 - HALF - W - 512 - BOTH))
            at(a + (7.5 if last else 10.0))
            vtt(T.co[:], b2[:, 0:S], T.cix[:], A.max, ["y", "cix"], ["co"], S, [2])
            vts(T.coff[:], T.co[:], -float(YB + 1 - HALF - (W + 512 if last else K)), None, A.add, None, ["co"], ["coff"], S)
        for c in range(4):
            bk = (b0, b1)[c % 2]; res = F0 + ["sc1", "nd"] if c % 2 == 0 else ["F1"]
            at(a + (6.1, 7.7, 8.2, 8.7)[c])
            mm([(bk[:, k:448:16], PAYC[0:S, :, k], T.IB[0:S, 28 * c:28 * c + 28], True, True) for k in range(16)], PCS + ["IB"], res, 1024, [c % 2])
            out = T.PAY[:, 448 * c:448 * c + 448]
            if PAYE[t][c] == "S":
                if c:
                    at(a + (C2K if last else C1K)[t][c] - 0.1)
                act(out, bk[:, 0:448], res + ["BC"], ["pay%d" % c], 448, [c % 2], bias=T.BC[:, t:t + 1], scale=UNIT)
            else:
                vts(out, bk[:, 0:448], UNIT, T.BC[:, t:t + 1], A.mult, A.add, res + ["BC"], ["pay%d" % c], 448, [c % 2])

        def places(k):
            at(a + k)
            shift = YB + 1 - HALF - L0 - SEG * t if t else 0
            if t == 0:
                vts(T.xo[:, 0:S], b4[:, 0:S], float(2 * W - BOTH), None, A.add, None, ["m1", "xop"], ["xo"], S, [4])
            else:
                if not last:
                    mm(grp(b3[:, 0:S], nm), ["DYN2", "DYN3", "I64", "IB"], ["G1", "Tn"], 2 * S, [3])
                shifted(SMALL[4], T.nB[:], b3[:, 0:S], shift - BOTH, ["Tn"], ["nB"], S, [3])
                lst = []
                for j, q in enumerate((0, 4)):
                    lst += grp(b3[:, S + S * j:2 * S + S * j], [(T.one[0:1, :], T.DR[0:1, S * t:S * t + S]), (T.one[0:1, :], T.DR[0:1, RO * S:RO * S + S]), (T.DYN[0:S, 128 * q:128 * q + 128], T.I128[0:S, 0:S]),
                                                                 (T.DYN[0:S, 128 * q + 128:128 * q + 256], T.IB[0:S, 0:S])])
                mm(lst, ["DYN0", "DYN1", "DYN4", "DYN5", "I128", "IB", "one", "DR", "DR2"], ["G1", "G2", "Tp"], 8 * S, [3])
                vtt(T.o1[:], b3[:, S:2 * S], T.nB[:], A.max, ["Tp", "nB"], ["o1"], S, [3])
                vtt(T.o2[:], b3[:, 2 * S:3 * S], T.o1[:], A.max, ["Tp", "o1"], ["o2"], S, [3])
                vtt(T.xo[:, 0:S], b2[:, 0:S], T.o2[:], A.max, ["y", "o2", "xop"], ["xo"], S, [2])
            op("V", lambda: V.transpose(T.xv[:], T.xo[:]), ["xo", "xop"], ["xv"], FIX + CY * 128)
            lst = []
            for mh in range(7):
                b, d = divmod(mh, 2)
                lst += grp(b4[:, 304 + mh:416:7], [(T.MF[:, 128 * (2 * d + e):128 * (2 * d + e) + 128], T.xv[:, 32 * b + 16 * e:32 * b + 16 * e + 16]) for e in range(2)])
            mm(lst[:6], ["xv", "MF"], ["XW0", "XW"], 1536, [4])
            mm(lst[6:], ["xv", "MF"], ["XW"], 2048, [4])
            at(a + k + 2.0)
            vts(T.xoff[:, S * t:S * t + S], b4[:, 304:416], -float(shift), None, A.add, None, ["XW0", "XW"], ["xoff%d" % t], S, [4])

        def scatter(engs, turns, win, off, rd, wr):
            cw = S // len(engs)
            for c, en in enumerate(engs):
                out = win.indirect(off[:, cw * c:cw * c + cw]); src = T.PAY[:, 16 * cw * c:16 * cw * (c + 1)]
                pay = ["pay%d" % c]
                at(a + turns[c])
                if en == "S":
                    act(out, src, rd + pay, wr, CS * 16 * cw, f=AF.Tanh)
                else:
                    vcp(out, src, rd + pay, wr, CS * 16 * cw)

        def by_name():
            scatter(C1E[t], C1K[t], TB[:, 0:2 * W], T.moff, ["moff"], TB1 + TB2 + (["TCp2", "TCg2"] + ["TBz%d" % c for c in range(8)] if t == 0 else []) + ["C1"])

        def by_list():
            if last:
                scatter(C2E[t], C2K[t], TB[:, 0:W + 1024], T.coff, ["coff"], TB1 + ["LS", "C2"])
            else:
                scatter(C2E[t], C2K[t], LS[:, :], T.coff, ["coff"], ["LS", "C2"])
            at(a + LISTK[t])
            lists = TB[:, W + 512:W + 1024] if last else LS[:, K:K + 512]
            op("V", lambda: V.transpose(T.VT[:], lists), ["LS"], ["VT"], FIX + CY * 512)
            vcp(T.VB[:], T.VT[:, :, 4:10], ["VT"], ["VB"], 192)
            for q, big in ((0, 0), (2, 1), (1, 1)):
                lst = []
                for xh in range(2):
                    prs = []
                    for e in range(2):
                        c = 128 * (2 * xh + e)
                        prs += [(mm_big(big, c), T.VB[:, 6 * e + 2 * q::12]), (T.MM[:, c:c + 128], T.VB[:, 6 * e + 2 * q + 1::12])]
                    lst += grp(b4[:, 128 + 32 * q + xh:160 + 32 * q:2], prs)
                mm(lst, ["VB", "MM4", "MM5"] + MM1, ["LL%d" % q], 512, [4])
            at(a + LISTK[t] + 1.0)
            shifted(SMALL[5], T.n0[:], b4[:, 128:160], PRAW - BOTH, ["LL0"], ["n0"], 32, [4])
            shifted(SMALL[5], T.bz[:], b4[:, 192:224], -K, ["LL2"], ["bz"], 32, [4])
            vtt(T.c1[:], b4[:, 192:224], T.n0[:], A.max, ["LL2", "n0"], ["c1"], 32, [4])
            vtt(T.lb[:, 32:64], T.bz[:], T.n0[:], A.max, ["bz", "n0"], ["lbb"], 64)
            vtt(T.lb[:, 0:32], b4[:, 160:192], T.c1[:], A.max, ["LL1", "c1"], ["lba"], 32, [4])
            vtt(T.hv1[:], b4[:, 128:160], T.hoff[:], A.subtract, ["LL0", "hoff"], ["hv1"], 32, [4])
            vts(T.lb16[:, 64 * t:64 * t + 64], T.lb[:], -float(PRAW), None, A.add, None, ["lba", "lbb"], ["ll%d" % t], 64)
            vtt(T.PO[:, 4 * t - 4:4 * t, 128:136], T.hv1[:], T.hcap[:], A.min, ["hv1", "hcap"], ["hv%d" % t], 64)

        def closing(_):
            at(a + 20.0)
            vts(T.nl16[:], T.n0[:], -float(PRAW), None, A.add, None, ["n0", "PO%d_%d" % (t, peers[2])], ["nl"], 32)
            act(TB[:, 0:W + 512].indirect(T.nl16[:]), TB[:, W + 512:W + 1024], ["nl", "LS"], TB1 + ["C1"], CS * 512, f=AF.Tanh)
            at(a + 22.0)
            c32, cb, fm, fd = W + 1024, 2160, W + 1984, 3120
            for j, r in enumerate((2, 3, 8, 9)):
                dma("Y", TB[:, c32 + 240 * j:c32 + 240 * j + 240], TB[r::16, 0:W], ["TBo", "TBp", "TBq"], ["cl%d" % j], 130)
            at(a + 25.2)
            for j in range(2):
                o = cb + 480 * j
                act(T0[:, o:o + 480], TB[:, c32 + 480 * j:c32 + 480 * j + 480], ["cl%d" % (2 * j), "cl%d" % (2 * j + 1)], ["cb%d" % j], 480)
                mm(grp(b0[:, 240 * j:240 * j + 240], [(T.I128[:], T0[:, o:o + 240]), (T.IB[:], T0[:, o + 240:o + 480])]),
                   ["cb%d" % j, "I128", "IB"], F0 + ["fv%d" % j], 480, [0])
            vtt(TB[:, fm:fm + 240], b0[:, 0:240], T.nmc[:], A.max, ["fv0", "nmc"] + F0, ["fm0"], 240, [0])
            vtt(TB[:, fm + 240:fm + 480], b0[:, 240:480], TB[:, fm:fm + 240], A.max, ["fv1", "fm0"] + F0, ["fm1"], 240, [0])
            act(T0[:, fd:fd + 240], TB[:, fm + 240:fm + 480], ["fm1"], ["fd0"], 240)
            vtt(T0[:, fd + 256:fd + 496], TB[:, fm + 240:fm + 480], T0[:, fd:fd + 240], A.subtract, ["fm1", "fd0"], ["fd1"], 480)
            op("V", lambda: V.transpose(T.EB[:, peers[2], 0:512], T0[:, fd:fd + 512]), ["fd0", "fd1"], ["EBr", "VF"], FIX + CY * 256)
            for part in range(3):
                lst = []
                for y1 in range(5 * part, 5 * part + 5):
                    b, d = divmod(y1, 2); prs = []
                    for e in range(2):
                        c = 128 * (2 * d + e); o = 32 * b + 16 * e
                        prs += [(T.MM[:, c:c + 128], T.EB[:, peers[2], o:o + 16]), (T.MM[:, c:c + 128], T.EB[:, peers[2], 256 + o:256 + o + 16])]
                    lst += grp(b4[:, 64 + y1:304:15], prs)
                mm(lst, ["VF"] + MM1, ["LL0", "LL1", "LL2", "m1", "AS%d" % part], 1280, [4])
            at(a + 30.7)
            vts(T.fo[:], b4[:, 64:304], -float(PRAW), None, A.add, None, ["AS0", "AS1", "AS2", "LL0"], ["fo"], 240, [4])

        if last:
            by_list()
            places(20.5)
            later.append(closing)
            return
        if t != 1:
            places((9.7, 0, 16.4)[t])
        by_name()
        at(a + 14.6)
        d = dma("Y", T.gr[:], TB[10 + t::16, W:2 * W], ["TCg"], ["gr"], 130)
        d = dma("Y", T.tk[:], TB[10 + t::16, 0:W], ["TBo"], ["tk"], 130, [d])
        dma("Y", TB[8::16, 0:W], TB[2::16, W:2 * W], ["TCp"], ["TBp"], 120, [d])
        dma("Y", TB[9::16, 0:W], TB[3::16, W:2 * W], ["TCp"], ["TBq"], 120, [d])
        dma("Y", TB[0::16, 0:W], T.dW[:], ["dW"], ["TBw"], 120, [d])
        if t == 0:
            dma("Y", TB[4::16, 0:W], LS[0:120, 0:256], ["LS", "C1"], ["TBn"], 130, [d])
            dma("Y", TB[5::16, 0:W], LS[0:120, 256:512], ["LS", "C1"], ["TBm"], 130, [d])
        at(a + 16.3)
        gb = T0[:, 1440 + 240 * t:1680 + 240 * t]

        def land(j):
            return T0[:, 720 * t - 720 + 240 * j:720 * t - 480 + 240 * j] if t else T.FL[:, 240 * j:240 * j + 240]
        cp(GBE[t], gb, T.gr[:], ["gr"], (T0N if t == 0 else []) + ["gb%d" % t], 240)
        s, n = send_all([land(slot(rank, r)) for r in peers], gb, "rG%d_%d" % (t, rank), ["gb%d" % t], 70)
        for r in peers:
            recv("rG%d_%d" % (t, r), n, [s], ["FL%d_%d" % (t, r)])
        at(a + 17.0)
        if SMALL[3] == "V":
            vts(T.cap[:], gb, -100.0, 102.0, A.mult, A.add, ["gb%d" % t], ["cap"], 120)
        else:
            act(T.cap[:], gb, ["gb%d" % t], ["cap"], 240, f=AF.Copy, scale=-100.0, bias=102.0)
        lst = grp(b0[:, 0:240], [(T.IF[:], T.ac[:]), (T.I2[:], T.tk[:]), (T.IB[:], gb), (T.IB[:], gb)] + [(T.IB[:], land(j)) for j in range(3)])
        at(a + 13.9)
        mm(lst[:1], ["IF", "ac"], F0 + ["sc1", "nd", "AS"], 960, [0])
        at(a + 16.4)
        mm(lst[1:4], ["I2", "IB", "tk", "gb%d" % t], ["AS"], 1440, [0])
        at(a + 19.4)
        mm(lst[4:], ["IB", "AS"] + ["FL%d_%d" % (t, r) for r in peers], ["AS1"], 720, [0])
        vtt(T.ac[:], b0[:, 0:240], T.cap[:], A.min, ["AS", "AS1", "cap"] + F0, ["ac"], 240, [0])
        dma("Y", TB[1::16, 0:W], T.ac[:], ["ac"], ["TBa"], 130)
        if t > 0:
            by_list()
        if t == 1:
            places(20.0)

    def exchange(t):
        last = t == RO - 1; a = 24.0 * t
        kp, ko, kr, ka = DATAK[t][:4]
        a0 = L0 + SEG * t
        HW = T.H[:, :]
        lists = {r: T.HL[:, 32 * t + 8 * r:32 * t + 8 * r + 8] for r in range(N)}
        lres = {r: "HL%d_%d" % (t, r) for r in range(N)}
        sent = {}
        at(a + kp)
        for r in peers + [rank]:
            o = 64 * t + 8 * r
            i = (r - rank) % N; bg = T.ht[:, 128 * i:128 * i + 128]
            cp(BGE, bg, LOG[:, 0:a0 - K].indirect(T.lb16[:, o + 32:o + 40]), logres(t, False, False) + ["ll%d" % t], ["ht%d" % i], CG * 128)
            vtt(T.PO[:, 4 * t - 4 + r, 0:128], LOG[:, 0:a0].indirect(T.lb16[:, o:o + 8]), bg, A.subtract,
                logres(t, False) + ["ll%d" % t, "ht%d" % i], ["PO%d_%d" % (t, r)], CG * 128)
            if r != rank:
                j = slot(rank, r)
                sent[j], n = send1(r, T.PL[:, 3 * t - 3 + j, :], T.PO[:, 4 * t - 4 + r, :], "rP%d_%d" % (t, j), ["PO%d_%d" % (t, r), "hv%d" % t])
        for j in range(3):
            recv("rP%d_%d" % (t, j), n, [sent[j]], ["PL%d_%d" % (t, j)])
        for i, r in enumerate([rank] + peers[::-1]):
            if r == rank:
                rs = ["PO%d_%d" % (t, r), "hv%d" % t]; buf, bi = T.PO, 4 * t - 4 + r; at(a + ko)
            else:
                j = slot(r, rank); rs = ["PL%d_%d" % (t, j)]; buf, bi = T.PL, 3 * t - 3 + j; at(a + kr[i - 1])
            k = now[1]; at(k - (0.75 if last and i > 1 else 0.0))
            vcp(lists[r], buf[:, bi, 128:136], rs, [lres[r]], 8)
            at(k)
            act(T.ht[:, 128 * i:128 * i + 128], HW.indirect(lists[r]), ["H", "Hd", lres[r]], ["ht%d" % i], CG * 128)
            at(now[1] + 0.15)
            vtt(HW.indirect(lists[r]), T.ht[:, 128 * i:128 * i + 128], buf[:, bi, 0:128], A.add, ["ht%d" % i, lres[r]] + rs, ["H", "Hd"], CS * 128)
        sent = []
        at(a + ka)
        for i, r in enumerate(peers):
            c = 128 * (3 * t - 3 + i)
            cp("VSV"[i] if last else AOE[i], T.AO[:, c:c + 128], HW.indirect(lists[r]), ["H", "Hd", lres[r]], ["AO%d_%d" % (t, i)], CG * 128)
            s, n = send1(r, LOG[:, a0 + 128 * rank:a0 + 128 * rank + 128], T.AO[:, c:c + 128], "rA%d" % t, ["AO%d_%d" % (t, i)])
            sent.append(s)
        cp("S", LOG[:, a0 + 128 * rank:a0 + 128 * rank + 128], HW.indirect(lists[rank]), ["H", "Hd", lres[rank]], ["A%d_o" % t], CG * 128)
        recv("rA%d" % t, 3 * n, sent, ["A%d_r" % t])
        if last:
            dma("Y", T.yh[:], T.H[:, 0:M], ["H", "A%d_r" % t], ["yh"], 480)

    def data(t):
        last = t == RO - 1; a = 24.0 * t
        k1, kq, k0, ke, ks = DATAK[t][4:]
        x0 = L0 + SEG * t + 512; X0 = x0 + K

        def x(o, n):
            return LOG[:, x0 + o:x0 + o + n]
        X1 = ["x%d_%d" % (t, c) for c in range(1, 5)]; XA = "x%d_0" % t; XX = [XA] + X1
        rd = logres(t, True) + ["xoff%d" % t]; e1, e0 = XG[t]; np1 = 4 if last else 2; cw = 56 // np1
        at(a + k1)
        for c in range(np1):
            o = S * t + 56 + cw * c
            cp(e1, x(896 + 16 * cw * c, 16 * cw), LOG[:, 0:x0].indirect(T.xoff[:, o:o + cw]), rd, X1[4 // np1 * c:4 // np1 * (c + 1)], CG * 16 * cw)
        lst = grp(b5[:, 0:S], [(T.BO[0:16, :], T.tgf[0:16, S * t:S * t + S])] + [(T.BO[:], T.PR[:, S * k:S * k + S]) for k in range(8)])
        mm(lst[:1], ["BO", "tgf"], ["p0", "st1"], 448, [5])
        at(a + kq)
        for c in range(4):
            o = S * t + 14 * c
            vtt(T.PR[:, 224 * c:224 * c + 224], LOG[:, 0:x0].indirect(T.xoff[:, o:o + 14]), x(896 + 224 * c, 224), A.mult, rd + [X1[c]], ["PR%d" % c], CG * 224)
            mm(lst[1 + 2 * c:3 + 2 * c], ["BO", "PR%d" % c, "p%d" % c], ["p%d" % (c + 1)], 896, [5])
        at(a + k0)
        cp(e0, x(0, 896), LOG[:, 0:x0].indirect(T.xoff[:, S * t:S * t + 56]), rd, [XA], CG * 896)
        at(a + ke)
        act(T.e[:], b5[:, 0:S], ["p0", "p1", "p2", "p3", "p4"], ["e"], S, [5], f=AF.Tanh, scale=-1.0 / 128.0)
        EE = ["E0", "E1", "E2", "E3"]
        if last:
            for j in range(4):
                vts(b6[:, S * j:S * j + S], T.e[:], 1.0 / 32.0, None, A.mult, None, ["e"], ["E%d" % j], S, [6])
        else:
            mm([(b6[:, S * j:S * j + S], T.IE[:], T.e[:], True, True) for j in range(4)], ["IE", "e"], EE, 1792, [6])
        for i, c in enumerate((2, 3, 0, 1) if PEADD[t] else (0, 1, 2, 3)):
            bk, bn = ((b7, 7), (b5, 5))[1 if PEADD[t] and not last else c % 2]
            own = [XA] if c < 2 else X1; other = X1 if c < 2 else [XA]; pk = (448 * c + 896) % K
            if PEADD[t] and c >= 2:
                bk, bn, res = ((b2, 2, ["F2", "cnt", "y"]) if last else (b7, 7, ["st0"])) if c == 2 else (b1, 1, ["F1"])
                pr = ["PR%d" % (2 * c - 4), "PR%d" % (2 * c - 3)]; dd = T.PR[:, 448 * c - 896:448 * c - 448]
                lst = grp(bk[:, 0:448], [(T.IF[:], x(448 * c, 448)), (T.IF[:], dd)])
                at(a + ke + (-0.1 if last else 0.1))
                mm(lst[:1], ["IF", "p4"] + own, res, 1792, [bn])
                at(a + ks[i])
                vtt(dd, b6[:, 0:448], x(pk, 448), A.mult, EE + other, pr, 448, [6])
                mm(lst[1:], ["IF"] + pr + res, ["ad%d" % c], 1792, [bn])
                act(LOG[:, X0 + 448 * c:X0 + 448 * c + 448], bk[:, 0:448], res + ["ad%d" % c], ["X%d_%d" % (t, c)], 448, [bn])
                continue
            at(a + ks[i])
            st = "st%d" % (bn == 5)
            vtt(bk[:, 0:448], b6[:, 0:448], x(pk, 448), A.mult, EE + other, [st] + (["p0", "p1", "p2", "p3", "p4"] if bn == 5 else []), 448, [6, bn])
            at(a + ks[i] + (0.6 if i % 2 == 0 else 0.0))
            vtt(LOG[:, X0 + 448 * c:X0 + 448 * c + 448], bk[:, 0:448], x(448 * c, 448), A.add, [st] + own, ["X%d_%d" % (t, c)], 448, [bn])

    for f, t in ((control, 0), (data, 0), (control, 1), (exchange, 1), (control, 2), (data, 1), (exchange, 2), (control, 3), (data, 2), (exchange, 3), (None, 3), (data, 3)):
        now[0] = "%s%d" % ("c" if f is control else "d", t)
        (f or later[0])(t)
    now[0] = "f"; at(200.0)
    for c in range(8):
        yo = TB[:, W + 480 * c:W + 480 * c + 480]
        cp("VS"[c % 2], yo, LOG[:, :].indirect(T.fo[:, 30 * c:30 * c + 30]), logres(RO, False) + ["fo"], ["YO%d" % c], CG * 480)
        dma("Y", T.yr[:, 480 * c:480 * c + 480], yo, ["YO%d" % c], ["yr%d" % c], 240)
    return ops


def order(sets):
    ops = sets[0]
    n = len(ops); lastw = {}; readers = {}; bank = {}
    for i, o in enumerate(ops):
        d = set()
        for r in o["r"]:
            if r in lastw:
                d.add(lastw[r])
        for w in o["w"]:
            if w in lastw:
                d.add(lastw[w])
            d.update(readers.get(w, ()))
        for b in o["banks"]:
            st = bank.setdefault(b, {"eng": None, "cur": [], "prev": []})
            if st["eng"] != o["eng"]:
                st["prev"] = st["cur"]; st["cur"] = []; st["eng"] = o["eng"]
            d.update(st["prev"]); st["cur"].append(i)
        for r in o["r"]:
            readers.setdefault(r, []).append(i)
        for w in o["w"]:
            lastw[w] = i; readers[w] = []
        d.discard(i)
        o["deps"] = d
    if "seq" in PLAN:
        return PLAN["seq"]
    pre = [set(o["deps"]) | set(o.get("after", ())) | set(o.get("behind", ())) for o in ops]
    succ = [[] for _ in range(n)]
    for i in range(n):
        for j in pre[i]:
            succ[j].append(i)

    def gap(i, j):
        return 0.0 if ops[j]["kind"] == "recv" or (ops[j]["eng"] == "P" and ops[i]["eng"] == "P") else WAKE
    above = [0] * n; ins = []
    for j in range(n):
        hard = [i for i in pre[j] if i not in ops[j].get("behind", ())]; far = 0
        for i in hard:
            far |= above[i]
        ins.append([(i, gap(i, j)) for i in hard if not far >> i & 1])
        above[j] = far | sum(1 << i for i in hard)
    fls = [[(" VSPGY".index(o["eng"] or " "), o["cost"], o["lat"], o.get("move", 0.0)) for o in st] for st in sets]
    began = [0.0] * n; why = [-1] * n; tail = [0, 0.0]

    def replay(seq, fl):
        free = [0.0] * 6; who = [-1] * 7; fin = [0.0] * n; dm = 0.0
        for i in seq:
            q, c, lat, mv = fl[i]; t = free[q]; w = who[q]
            for j, wk in ins[i]:
                if fin[j] + wk > t:
                    t = fin[j] + wk; w = j
            began[i] = t
            t += c
            if q:
                free[q] = t; who[q] = i
            if mv:
                t += lat - 600.0
                if dm > t:
                    t = dm; w = who[6]
                dm = t + mv; t = dm + 600.0; who[6] = i
            fin[i] = t; why[i] = w
        end = max(fin); tail[0] = fin.index(end); tail[1] = end
        return end + EARLY * sum(fin) / n

    def judge(seq):
        return sum(replay(seq, fl) * wt for fl, wt in zip(fls[::-1], WEIGHT[::-1]))
    turn = [o["turn"] for o in ops]
    for i in range(n - 1, -1, -1):
        if turn[i] is None:
            turn[i] = min([turn[j] for j in succ[i]] + [1e3]) - 0.01
    busy = {}; last = {}; rdy = [0.0] * n; start = [0.0] * n; left = [len(p) for p in pre]; ready = [i for i in range(n) if not left[i]]
    while ready:
        i = min(ready, key=lambda j: (turn[j], j)); ready.remove(i)
        q, c, lat, mv = fls[0][i]; t = rdy[i]
        if q:
            if ops[i]["turn"] is not None:
                t = max(t, last.get(q, 0.0))
            iv = busy.setdefault(q, [])
            for s0, s1 in iv:
                if s0 < t + c and s1 > t:
                    t = s1
            iv.append((t, t + c)); iv.sort()
            if ops[i]["turn"] is not None:
                last[q] = t + c
        start[i] = t
        for j in succ[i]:
            rdy[j] = max(rdy[j], t + c + (0.0 if i in ops[j].get("behind", ()) else lat + mv + gap(i, j)))
            left[j] -= 1
            if not left[j]:
                ready.append(j)
    seq = sorted(range(n), key=lambda i: start[i]); at = judge(seq); best = (at, seq); held = None
    x = [SEED]

    def rnd(k):
        x[0] = (x[0] * 1103515245 + 12345) % 2147483648
        return (x[0] >> 8) % k
    outs = [[] for _ in range(n)]
    for j in range(n):
        for i, wk in ins[j]:
            outs[i].append((j, wk))
    mean = [(fls[0][i][0], sum(fl[i][1] * w for fl, w in zip(fls, WEIGHT)), sum((fl[i][2] + fl[i][3]) * w for fl, w in zip(fls, WEIGHT))) for i in range(n)]
    bh = [list(o.get("behind", ())) for o in ops]; hb = [[j for j in succ[i] if i in bh[j]] for i in range(n)]

    def pack(lst, back):
        lo = [[] for _ in range(6)]; hi = [[] for _ in range(6)]; end = [0.0] * n; edges = outs if back else ins
        for i in lst:
            q, c, lat = mean[i]; t = 0.0
            for j, wk in edges[i]:
                f = end[j] + wk + (lat if back else mean[j][2])
                if f > t:
                    t = f
            for j in (hb if back else bh)[i]:
                if end[j] > t:
                    t = end[j]
            if q:
                a0 = lo[q]; a1 = hi[q]; k = len(a0)
                while k and a1[k - 1] > t:
                    k -= 1
                while k < len(a0) and a0[k] < t + c:
                    t = a1[k]; k += 1
                a0.insert(k, t); a1.insert(k, t + c)
            end[i] = t + c
        return end

    def lawful(key):
        key = list(key)
        for j in range(n):
            for i in pre[j]:
                if key[i] > key[j]:
                    key[j] = key[i]
        return sorted(range(n), key=lambda j: key[j])
    replay(seq, fls[0]); cur = list(began)
    for late in LATE:
        end = pack(lawful([turn[j] + (late if ops[j]["tag"][0] == "d" else 0.0) for j in range(n)]), False)
        for again in range(3):
            st = [end[j] - mean[j][1] for j in range(n)]
            cand = lawful(st); val = judge(cand)
            if val < at:
                cur = st; at = val; best = (at, cand)
            end = pack(sorted(range(n), key=lambda j: (-end[j] - mean[j][2], -j)), True)
            end = pack(lawful([-e for e in end]), False)
    for it in range(PASSES):
        key = list(cur); i = rnd(n); d = (rnd(41) - 20) * (50, 200, 800)[rnd(3)]
        for j in range(i, min(n, i + 1 + rnd((1, 4, 12, 40)[rnd(4)]))):
            key[j] += d
        end = pack(lawful(key), False)
        if rnd(3) == 0:
            end = pack(sorted(range(n), key=lambda j: (-end[j] - mean[j][2], -j)), True)
            end = pack(lawful([-e for e in end]), False)
        st = [end[j] - mean[j][1] for j in range(n)]
        cand = lawful(st); val = judge(cand)
        if val <= at + 3.0 * HEAT * (1.0 - it / PASSES) * rnd(100) / 100.0:
            cur = st; at = val
            if at < best[0]:
                best = (at, cand)
    at, seq = best
    for it in range(MOVES):
        if held is None:
            held = []; pos = {j: k for k, j in enumerate(seq)}
            for fl in fls[::-1]:
                replay(seq, fl); j = tail[0]
                while why[j] >= 0:
                    if why[j] not in pre[j]:
                        held.append((pos[why[j]], pos[j]))
                    j = why[j]
            every = [(pos[why[j]], pos[j]) for j in range(n) if why[j] >= 0 and why[j] not in pre[j]]
        pick = held if rnd(2) else every
        lo, hi = pick[rnd(len(pick))]; ln = hi - lo + (0, 0, rnd(10), rnd(60))[rnd(4)]
        if rnd(2):
            win = seq[lo:lo + ln + 1]; moved = {win[0]}
            for j in win[1:]:
                if not moved.isdisjoint(pre[j]):
                    moved.add(j)
            new = [j for j in win if j not in moved] + [j for j in win if j in moved]
        else:
            lo = max(0, hi - ln); win = seq[lo:hi + 1]; need = set(pre[win[-1]]); moved = {win[-1]}
            for j in win[-2::-1]:
                if j in need:
                    moved.add(j); need.update(pre[j])
            new = [j for j in win if j in moved] + [j for j in win if j not in moved]
        cand = seq[:lo] + new + seq[lo + len(win):]
        val = judge(cand)
        if val <= at + HEAT * (1.0 - it / MOVES) * rnd(100) / 100.0:
            seq = sorted(cand, key=lambda j: began[j]); held = None
            at = val if seq == cand else judge(seq)
            if at < best[0]:
                best = (at, seq)
    PLAN["seq"] = best[1]; PLAN["t"] = [replay(best[1], fl) * 0 + tail[1] for fl in fls]
    PLAN["path"] = []
    for fl in fls:
        replay(best[1], fl); j = tail[0]; p = []
        while j >= 0:
            p.append((round(began[j]), ops[j]["tag"], why[j] in pre[j])); j = why[j]
        PLAN["path"].append(p[::-1])
    return PLAN["seq"]


def rank_program(g, core, T, topo):
    rank = T.rank_of(core)
    if rank is None:
        return
    sets = [build(g, T, topo, rank, pace) for pace in PACES]
    seq = order(sets); ops = sets[0]
    Q = {"V": g.vector, "S": g.scalar, "P": g.tensor, "G": g, "Y": g.sync}
    need = set()
    for o in ops:
        o["waits"] = [j for j in o["deps"] if not (o["eng"] == "P" and ops[j]["eng"] == "P") and ops[j]["kind"] != "rem"]
        need.update(o["waits"])
    cnt = {"cV": 0, "cS": 0, "cP": 0, "cG": 0}; nd = 0; ev = {}; ls = 0
    for i in seq:
        o = ops[i]
        if o["kind"] == "c" and i in need:
            s = "c" + o["eng"]; cnt[s] += 1; ev[i] = (s, cnt[s])
        elif o["kind"] == "dma":
            ev[i] = ("d%d" % nd, 16); nd += 1
        elif o["kind"] == "recv":
            ev[i] = (o["sem"], o["cnt"])
    waited = {q: {} for q in Q}; top = {}
    for i in seq:
        o = ops[i]
        if o["kind"] == "recv":
            continue
        want = {}
        for j in sorted(o["waits"]):
            s, c = ev[j]; want[s] = max(want.get(s, 0), c)
        for s, c in want.items():
            if waited[o["eng"]].get(s, 0) < c:
                Q[o["eng"]].wait_ge(T.sem[s], c); waited[o["eng"]][s] = c; top[s] = max(top.get(s, 0), c)
        ins = o["fn"]()
        if o["kind"] == "dma":
            ins.then_inc(T.sem[ev[i][0]], 16)
        elif o["kind"] == "rem":
            ls += o["ls"]
        elif i in ev:
            ins.then_inc(T.sem[ev[i][0]], 1)
    for s, c in sorted(set(ev.values())):
        if top.get(s, 0) < c:
            g.wait_ge(T.sem[s], c); top[s] = c
    g.wait_ge(T.sem.ls, ls)
